import numpy as np, ml_dtypes
CORES = [5,29,101,125,133,157,229,253]
N = 8
import mx_ref
BF = ml_dtypes.bfloat16
def gentries(a):
    return np.ascontiguousarray(a.reshape(8, 16, -1).transpose(0, 2, 1)).reshape(8, -1)
def gtable(e):
    e = np.asarray(e); return np.ascontiguousarray(e.reshape(8, -1, 16).transpose(0, 2, 1)).reshape(128, -1).astype(np.int32)
def gcols(t, e):
    v = np.concatenate([t.reshape(8, 16, -1, 4), np.zeros((8, 16, 1, 4), BF)], axis=2)
    return np.ascontiguousarray(np.stack([v[g][:, e[g]] for g in range(8)])).reshape(128, -1)
def gpick(z, e):
    return np.concatenate([z[16 * g:16 * g + 16][:, e[g]] for g in range(8)])
def tile(rs):
    return np.stack(rs, axis=2).reshape(128, -1).astype(BF)
def pick(q, e):
    c = np.concatenate([q[0].reshape(128, -1, 4), np.zeros((128, 1, 4), np.uint8)], axis=1); s = np.concatenate([q[1], np.ones((16, 1), np.uint8)], axis=1)
    return (np.ascontiguousarray(c[:, e].reshape(128, -1)), np.ascontiguousarray(s[:, e]))
def join(*qs):
    return (np.concatenate([q[0] for q in qs], axis=1), np.concatenate([q[1] for q in qs], axis=1))
def put(q, e, v):
    c, s = q[0].reshape(128, -1, 4).copy(), q[1].copy(); c[:, e] = v[0].reshape(128, -1, 4); s[:, e] = v[1]
    return (c.reshape(128, -1), s)
def pk(c, s):
    return (np.ascontiguousarray(c), mx_ref.live(s))
def emit(q):
    return q[0], q[1]
def packed(v, rng):
    q = [mx_ref.quantize(np.ascontiguousarray(v[r])) for r in range(N)]
    return np.stack([a for a, b in q]), np.stack([mx_ref.plane(b, rng) for a, b in q])
def values_of_codes():
    e, c = np.zeros((128, 128, 4), np.float32), np.zeros((128, 2, 4), np.uint8)
    e[np.arange(128), np.arange(128), 0] = 1
    c[:127, :, 0] = np.arange(256).reshape(2, 128).T[:127]
    return mx_ref.matmul(mx_ref.quantize(e.reshape(128, 512).astype(BF)), (c.reshape(128, 8), np.full((16, 2), 127, np.uint8))).T.reshape(-1).astype(np.float64)
CODE_VALUE, SCALE_VALUE = values_of_codes(), 2.0 ** (np.arange(256) - 127.0)
def decode(q):
    return (CODE_VALUE[q[0]].reshape(16, 8, -1, 4) * SCALE_VALUE[q[1]][:, None, :, None] + 0.0).reshape(128, -1).astype(np.float32)
def f(rng, *shape):
    return mx_ref.flush((rng.standard_normal(shape, dtype=np.float32) * np.exp2(rng.integers(-2, 3, shape[:-1] + (1,)))).astype(BF))
def wide(rng, *shape, cols=0):
    v = rng.standard_normal(shape, dtype=np.float32) * np.exp2(rng.integers(-12, 13, shape)).astype(np.float32)
    if cols: v *= np.repeat(np.exp2(rng.integers(-cols, cols + 1, shape[:-2] + (1, shape[-1] // 4))) * (rng.random(shape[:-2] + (1, shape[-1] // 4)) > 0.0625), 4, axis=-1).astype(np.float32)
    return mx_ref.flush(v.astype(BF))
C, H = 288, 144
STEP = [4, 1, 2]
G, OWN = np.arange(8)[:, None], np.tile(np.arange(C), (8, 1))
def numbers_of(rng):
    return {"x": np.array(f(rng, N, 128, 4 * C)), "u": np.array(f(rng, N, 128, 512)), "v": np.array(f(rng, N, 128, 512))}
def stored(a, m):
    return {"fl": np.stack([gtable(a[r]) for r in range(N)]), "ml": np.stack([gtable(m[r]) for r in range(N)])}
def pairs(o):
    m = np.zeros(o.shape, np.int64)
    np.put_along_axis(m, o[..., ::2], o[..., 1::2], axis=-1)
    np.put_along_axis(m, o[..., 1::2], o[..., ::2], axis=-1)
    return m
def ring(o):
    a = np.zeros(C, np.int64)
    a[o] = np.roll(o, -1)
    return a
def lists(rng):
    e = np.tile(np.arange(C), (N, 8, 1))
    return rng.permuted(e, axis=2), pairs(rng.permuted(e, axis=2))
def layers(rng, still=[]):
    w = np.array(f(rng, N, 128, 2048)).reshape(N, 8, 16, 4, 8, 16, 4)
    for i in still:
        w[:, :, i] = 0
        w[:, :, :, :, :, i] = 0
    return w
def weights(rng, w):
    c, s = packed(np.ascontiguousarray(w).reshape(N, 128, 2048), rng)
    return {"wc": c, "ws": s}
def parity():
    i = np.arange(N)
    return (i ^ (i >> 1) ^ (i >> 2)) % 2
def setup_inputs(rng):
    return {**numbers_of(rng), **stored(*lists(rng)), **weights(rng, layers(rng))}
def setup_inputs_ties(rng):
    d = numbers_of(rng)
    o = rng.permutation(N)
    k = rng.integers(0, 4, (N, 8, C))
    k[o[1]] += 1
    k[o[2], rng.permutation(8)[:4]] = 1
    a, m = lists(rng)
    g = int(rng.integers(8))
    a[:, g] = np.arange(C)
    m[:, g] = (np.arange(C) + H) % C
    k[o[3], g] = np.arange(C) >= H
    x = d["x"].reshape(N, 8, 16, C, 4)
    x[:, :, 0] = 0
    x[:, :, 0, :, 0] = k.astype(np.float32).astype(BF)
    u = d["u"].reshape(N, 128, 128, 4)
    u[:, :, ::16] = 0
    for r in range(N):
        for h in range(0, 128, 16): u[r, h, h, 0] = 0.0 if r == o[0] else -1.0 if r == o[1] else 1.0
    return {"x": x.reshape(N, 128, 4 * C), "u": u.reshape(N, 128, 512), "v": d["v"], **stored(a, m), **weights(rng, layers(rng, [0]))}
def setup_inputs_near(rng):
    d = numbers_of(rng)
    x = d["x"].astype(np.float32).reshape(N, 8, 16, C, 4)
    x[:, :, 0] = 0
    x[:, :, 8:] = 0
    x[:, :, 15, :, 0] = 2.0 ** -26
    u = d["u"].reshape(N, 128, 128, 4)
    u[:, :, ::16] = 0
    o = rng.permutation(N) % 4
    for r in range(N):
        c = rng.choice([-1.0, 1.0], (8, 1))
        s = rng.integers(0, 16, (8, C))
        digits = ((s[:, :, None] >> np.arange(4)) & 1) * np.exp2(np.arange(4) - 23.0)
        if o[r] < 2:
            x[r, :, 0, :, 0] = c
            x[r, :, 8] = digits
            x[r, :, 11, :, 0] = 2.0 ** -10
        elif o[r] == 2: x[r, :, 8] = digits * rng.choice([-1.0, 1.0], (8, C, 1))
        else:
            x[r, :, 8, :, 0] = np.where(s < 8, 1.25, 0.0) * 2.0 ** -30 * c
            x[r, :, 9, :, 0] = np.where(s < 8, 0.0, 1.125) * 2.0 ** -30 * c
            for g in rng.permutation(8)[:4]:
                e = rng.choice([-1.0, 1.0], C) * 2.0 ** -30
                x[r, g, 8, :, 0] = 1.25 * e
                x[r, g, 9, :, 0] = -1.125 * e
            x[r, :, 13, :, 0] = rng.choice([-1.0, 1.0], (8, C)) * 2.0 ** -30
        at = [0, C - 1, int(rng.integers(C)), int(rng.integers(C))]
        for g, j in zip(rng.permutation(8)[:4], at): x[r, g, 0, j, 0] = 2.0 ** 29 * rng.choice([-1.0, 1.0])
        k = 1.0 if o[r] == 0 else 2.0 ** -30
        for h in range(0, 128, 16):
            u[r, h, h, 0] = k if o[r] < 2 else 1.0
            if o[r] < 2: u[r, h + 11, h, 0] = k
            if o[r] < 3: u[r, h + 8, h] = k
            else:
                u[r, h + 8, h, 0] = k
                u[r, h + 9, h, 0] = 1.125 * k
                u[r, h + 14, h, 0] = k
    w = layers(rng, [0, 8, 9, 10, 11, 12, 13, 14, 15])
    for g in range(8): w[:, g, 13, 0, g, 14, 0] = 2.0 ** -5
    return {"x": x.reshape(N, 128, 4 * C).astype(BF), "u": u.reshape(N, 128, 512), "v": d["v"], **stored(*lists(rng)), **weights(rng, w)}
def setup_inputs_odd(rng):
    d = numbers_of(rng)
    x = (1.0 + (2 * rng.integers(0, 64, (N, 16, 8, C, 4)) + 1) * 2.0 ** -7) * np.exp2(-rng.integers(0, 7, (N, 16, 8, C, 4)).astype(np.float64)) * rng.choice([-1.0, 1.0], (N, 16, 8, C, 4))
    x[:, :, 0, :, 0] = (np.where((parity()[:, None] + np.arange(16)) % 2 == 0, 1.96875, 1.875) * 2.0 ** 8)[:, :, None]
    x[:, :, 1, :, 0] = rng.integers(8, 16, (N, 16, C)) * 2.0 ** -8
    u = d["u"].reshape(N, 16, 8, 128, 4)
    u[:, :, 0, ::16] = 0
    for r in range(N):
        for g in rng.permutation(8)[:2]:
            u[r, :, :, 16 * g] = 0
            u[r, 2 * g + parity()[r], 1, 16 * g, 0] = 1.0
    w = layers(rng, [0, 1, 8, 9])
    for g in range(8):
        for i in (0, 8): w[:, g, i, 0, g, i, 0] = -0.5
    return {"x": x.astype(np.float32).reshape(N, 128, 4 * C).astype(BF), "u": u.reshape(N, 128, 512), "v": d["v"], **stored(*lists(rng)), **weights(rng, w)}
def setup_inputs_ends(rng):
    d = numbers_of(rng)
    r0 = int(rng.integers(N))
    a = rng.permutation(np.array([r0, r0 ^ STEP[0], r0 ^ STEP[1], r0 ^ STEP[0] ^ STEP[1]]))
    z = rng.permutation(np.setdiff1d(np.arange(N), a))
    x = np.where(rng.random((N, 128, C, 4)) < 0.5, -1.0, -0.9375) * 2.0 ** 30
    x[:, 5] *= 2.0 ** -10
    c = rng.choice([-1.0, 1.0], (128, 1, 4))
    for r in z[:2]: x[r] = c * (1.0 + 0.125 * rng.integers(0, 8, (128, C, 4))) * 2.0 ** -30
    for r in z[2:]: x[r] = x[r] * rng.choice([-1.0, 1.0], (1, C, 1))
    size = np.full(N, 2.0 ** 30)
    size[a[2:]] = 2.0 ** -30
    size[z[1::2]] = 2.0 ** -30
    u = d["u"].astype(np.float32).reshape(N, 128, 128, 4)
    w = np.zeros((N, 128, 4, 128, 4), np.float32)
    i = np.arange(128)
    for b in range(4): w[:, i, b, i, b] = 32.0
    w[a[2], 5, 0, 5, 0] = 2.0 ** 8
    w[a[2], 6, 0, 6, 0] = 2.0 ** -8
    k = np.array([[0, 0, 2, 2, 1, 1, 3, 3], [2, 1, 0, 3, 0, 3, 2, 1]])[parity()][:, rng.permutation(8)]
    e, m = lists(rng)
    j = np.arange(C)
    for r in range(N):
        h = rng.permutation(8)
        u[r, :, ::16] = (np.where(h < 2, 0.0, h % 2 * 2.0 - 1.0) * size[r])[None, :, None]
        for g in range(8):
            t = int(rng.integers(4))
            if t: m[r, g] = [C - 1 - j, j ^ 1, (j + H) % C][t - 1]
            e[r, g] = [ring(rng.permutation(C)), j, ring(j), m[r, g]][k[r, g]]
    u[:, 5, ::16] = 0
    v = rng.choice([-1.0, 1.0], (N, 128, 512)) * size[:, None, None]
    return {"x": x.astype(np.float32).reshape(N, 128, 4 * C).astype(BF), "u": u.reshape(N, 128, 512).astype(BF), "v": v.astype(np.float32).astype(BF), **stored(e, m), **weights(rng, w.astype(BF))}
def setup_inputs_spread(rng):
    d = setup_inputs(rng)
    d["x"] = wide(rng, N, 128, 4 * C, cols=6)
    return d
def check_inputs(d):
    b = []
    for k in ("x", "u", "v"):
        a = np.abs(d[k].astype(np.float32))
        if not (np.isfinite(a).all() and ((a == 0) | (a >= 2.0 ** -30) & (a <= 2.0 ** 30)).all()): b.append("a value of " + k)
    none, least, most = [emit(mx_ref.quantize(np.full((128, 16), k, np.float32).astype(BF)))[1][0, 0] for k in (0.0, 2.0 ** -8, 2.0 ** 8)]
    for r in range(N):
        if (np.sort(gentries(d["fl"][r]), axis=1) != OWN).any(): b.append("fl: a group that doesn't name every column once")
        m = gentries(d["ml"][r])
        if ((m < 0) | (m >= C)).any() or (m == OWN).any() or (m[G, m] != OWN).any(): b.append("ml: columns that aren't each other's mates")
        if ((d["wc"][r] == 0x7F) | (d["wc"][r] == 0xFF)).any(): b.append("wc: a code that is no number")
        s = mx_ref.live(d["ws"][r])
        if ((s != none) & ((s < least) | (s > most))).any(): b.append("ws: a scale out of range")
    return b
def leaders(a, s):
    best, w = OWN, a
    for _ in range(C - 1):
        p, o = s[G, w], s[G, best]
        best = np.where((p > o) | (p == o) & (w < best), w, best)
        w = a[G, w]
    return best
def hops(a, best):
    n, w = np.zeros((8, C), np.int64), best
    for _ in range(C - 1):
        go = w != OWN
        n, w = n + go, np.where(go, a[G, w], w)
    return n
def walk(a, at, n):
    for i in range(C - 1): at = np.where(i < n, a[G, at], at)
    return at
def reference(x, u, v, fl, ml, wc, ws):
    qu = [mx_ref.quantize(u[r]) for r in range(N)]
    lay = [pk(wc[r], ws[r]) for r in range(N)]
    cyc, mate = [gentries(fl[r]) for r in range(N)], [gentries(ml[r]) for r in range(N)]
    now = [x[r] for r in range(N)]
    for step in STEP:
        q = [mx_ref.quantize(now[r]) for r in range(N)]
        t = [decode(q[r]).astype(BF) for r in range(N)]
        made, after = [], []
        for r in range(N):
            p = r ^ step
            s = mx_ref.matmul(qu[r], q[r])[::16] + np.float32(0.0)
            lead = leaders(cyc[r], s)
            far = walk(cyc[p], lead, hops(cyc[r], lead))
            mine = s[G, far]
            other = mine[G, mate[r]]
            swap = np.where(OWN < mate[r], mine < other, other < mine)
            new = cyc[r][G, np.where(swap, mate[r], OWN)]
            back = np.argsort(new, axis=1)
            z = mx_ref.quantize(((gcols(t[r], new).astype(np.float32) + gcols(t[p], far).astype(np.float32)) * np.float32(0.5)).astype(BF))
            res = [mx_ref.matmul(pick(lay[r], np.arange(128 * b, 128 * b + 128)), z) * np.float32(0.03125) for b in range(4)]
            made.append(tile([(t[r][:, b::4].astype(np.float32) + gpick(res[b], back)) * np.float32(0.5) for b in range(4)]))
            after.append(new)
        now, cyc = made, after
    y, nl = np.zeros((N, 128, C), np.float32), np.zeros((N, 8, C), np.float32)
    oc, osc = np.zeros((N, 128, 4 * C), np.uint8), np.zeros((N, 16, C), np.uint8)
    for r in range(N):
        q = mx_ref.quantize(now[r])
        y[r] = mx_ref.matmul(mx_ref.quantize(v[r]), q)
        nl[r] = cyc[r]
        oc[r], osc[r] = emit(q)
    return {"y": y, "nl": nl, "oc": oc, "osc": osc}

@@ -1,0 +1,548 @@
+from concourse.mybir import dt, AluOpType, ActivationFunctionType
+
+A = AluOpType
+COPY = ActivationFunctionType.Copy
+IDENT = ActivationFunctionType.Identity
+SIGN = ActivationFunctionType.Sign
+C = 288
+TC = C // 16
+MASKS = [4, 1, 2]
+LEVELS = [(3, 1), (3, 3), (2, 9), (2, 18), (2, 36), (2, 72), (2, 144)]
+PARTS = {"a": (0, 160), "b": (160, C)}
+Z_HOME = (2,)
+TWIN_HOME = ()
+R_HOME = (1,)
+WAKE, GATHER, EL = 0.06, 1.5e-3, 1.04e-3
+LOOK, EDGE = 1.0, 1.0
+HASTE = {"hr": -1.0, "er": -0.6, "sc": 0.6, "et": 0.3, "rb": 3.0, "fh": -0.6, "k": 0.3, "ho": -3.0, "gp": -3.0}
+AFTER = ["zq"]
+S_HOME = False
+P_FAR = (2, 3)
+NE, NL = 8, 2
+NMK = 6
+
+SCRATCH = {}
+
+
+def _b(names, n, dtype, where="sbuf"):
+    for name in names.split():
+        SCRATCH[name] = (where, [128, n], dtype)
+
+
+CODE = "float8_e4m3fn_x4"
+_b("x0 xt z fh fs gt", 4 * C, "bfloat16")
+_b("rb gp", 4 * C, "float32")
+_b("xq0 xq1 xq2 xq3 lc0 lc1 lc2 zq", C, CODE)
+_b("xs0 xs1 xs2 xs3 ls0 ls1 ls2 zs", C, "uint8")
+_b("fo0 fo1 fo2 fo3 lo0 lo1 lo2 w1 w2 w3 to mo loo hio eo8 eo64 so", TC, "uint16")
+_b("wq eq", 512, CODE)
+_b("wsp eqs", 512, "uint8")
+_b("uq uk vq", 128, CODE)
+_b("uqs uks vqs", 128, "uint8")
+_b("et", 2048, "bfloat16")
+_b("ub vb", 512, "bfloat16")
+_b("fli mli ki ka k0 k1 k2 x1", TC, "int32")
+_b("jf j16 key s s2 mc0 mc1 m0 m1 m2 y0 y1 y2 y3 za0 za1 zb0 zb1 mine mhi km ks yb nlr mbig", C, "float32")
+_b("jc mask keep frow srow cand", C, "bfloat16")
+_b("mk sc", NMK * C, "bfloat16")
+_b("hr", 8 * C, "bfloat16")
+_b("er", 21 * C, "bfloat16")
+_b("ho", 7 * TC, "uint16")
+_b("uo", 8, "uint16")
+_b("c16 jt mtf ffc ff dfm dmt ta tb tc x2 x3", TC, "float32")
+_b("pi p16i", 2, "int32")
+_b("pn p16", 2, "float32")
+_b("diag", 256, "float32")
+_b("p0 p1 p2 p3 p4 p5 p6 p7", 512, "float32", "psum")
+
+SEMAPHORES = ["cv", "cs", "ct", "cp", "lx", "lu", "lv", "lf", "lm", "lw", "lq", "lout", "sent"]
+SEMAPHORES += ["ac%d" % r for r in range(3)] + ["al%d" % r for r in range(3)]
+
+
+def relay_of(src, dst, topo):
+    if topo.may_write(src, dst):
+        return None
+    cs = [c for c in topo.cores_of(src) if topo.may_write(c, dst)]
+    near = [c for c in cs if topo.die(c) == topo.die(src)]
+    return (near or cs)[0]
+
+
+def send(g, T, topo, src, dst, out_ap, in_ap, sem, count):
+    rid, pid = topo.addr(dst, src)
+    e = topo.engines(src, dst)[:count]
+    m = 0
+    for k in e:
+        m |= 1 << k
+    g.remote_dma(out_ap=out_ap, in_ap=in_ap, remote_sem=T.sem[sem], local_sem=T.sem.sent, pid=pid, routing_id=rid,
+                 dma_engine_mask=m)
+    return len(e)
+
+
+def order(ops):
+    n = len(ops)
+    users = [[] for _ in range(n)]
+    for i, o in enumerate(ops):
+        for d in o["deps"]:
+            users[d].append(i)
+    far = [0.0] * n
+    for i in range(n - 1, -1, -1):
+        o = ops[i]
+        far[i] = o["c"] + o["tail"] + max([far[u] + WAKE for u in users[i]] or [0.0])
+    far = [far[i] + HASTE.get(ops[i]["kind"], 0.0) for i in range(n)]
+    left = [len(o["deps"]) for o in ops]
+    ready = [0.0] * n
+    end = [0.0] * n
+    open_ = {}
+    free = {}
+    out = []
+
+    def finish(i, t):
+        end[i] = t
+        for u in users[i]:
+            left[u] -= 1
+            ready[u] = max(ready[u], t if ops[i]["q"] == ops[u]["q"] and not ops[i]["tail"] and ops[i]["free"] else t + WAKE)
+            if left[u] == 0:
+                release(u)
+
+    def release(u):
+        if ops[u]["q"] is None:
+            out.append(u)
+            finish(u, ready[u] + ops[u]["tail"])
+        else:
+            open_.setdefault(ops[u]["q"], []).append(u)
+
+    for i in range(n):
+        if not ops[i]["deps"]:
+            release(i)
+    while any(open_.values()):
+        pick = None
+        for q, cand in open_.items():
+            if not cand:
+                continue
+            t = max(free.get(q, 0.0), min(ready[i] for i in cand))
+            now = [i for i in cand if ready[i] <= t + 1e-9]
+            b = max(now, key=lambda i: (far[i], -i))
+            stop = t + ops[b]["c"]
+            for i in cand:
+                if far[i] > far[b] + EDGE and ready[i] < stop and ready[i] - t < LOOK * (stop - ready[i]):
+                    b = i
+            s = max(t, ready[b])
+            if pick is None or s < pick[0]:
+                pick = (s, q, b)
+        s, q, b = pick
+        open_[q].remove(b)
+        free[q] = s + ops[b]["c"]
+        out.append(b)
+        finish(b, free[q] + ops[b]["tail"])
+    return out
+
+
+def rank_program(g, core, T, topo):
+    rank = T.rank_of(core)
+    if rank is None:
+        relay_program(g, core, T, topo)
+        return
+    queues = {"v": g.vector, "s": g.scalar, "t": g.tensor, "p": g, "y": g.sync}
+    own = {"v": "cv", "s": "cs", "t": "ct", "p": "cp"}
+    V, S, P = g.vector, g.scalar, g.tensor
+    ops = []
+    acc = {}
+
+    def op(qn, rd, wr, fn, cost, sem=None, inc=1, tail=0.0, ev=None):
+        deps = set()
+        me = len(ops)
+        for r in rd:
+            a = acc.setdefault(r, [None, []])
+            if a[0] is not None:
+                deps.add(a[0])
+        for r in wr:
+            a = acc.setdefault(r, [None, []])
+            deps.update(a[1])
+            if a[0] is not None:
+                deps.add(a[0])
+        for r in rd:
+            acc[r][1].append(me)
+        for r in wr:
+            acc[r] = [me, []]
+        deps.discard(me)
+        ops.append(dict(q=qn, c=cost, tail=tail, kind=(wr or [""])[0].rstrip("0123456789"), deps=deps, fn=fn, sem=sem or own.get(qn), inc=inc, ev=ev, free=False))
+        return me
+
+    def emit():
+        total, know = {}, {k: {} for k in queues}
+        for i in order(ops):
+            o = ops[i]
+            if o["q"] is None:
+                o["knows"] = {}
+                continue
+            k = know[o["q"]]
+            waits = sorted((ops[d]["ev"] + (d,) for d in o["deps"] if ops[d]["ev"]), key=lambda e: -len(ops[e[2]]["knows"]))
+            top = {}
+            for s, n, d in waits:
+                if n > top.get(s, (0,))[0]:
+                    top[s] = (n, d)
+            for s, n, d in waits:
+                if top[s] != (n, d) or k.get(s, 0) >= n:
+                    continue
+                queues[o["q"]].wait_ge(T.sem[s], n)
+                for a, b in ops[d]["knows"].items():
+                    if k.get(a, 0) < b:
+                        k[a] = b
+                k[s] = n
+            if o["sem"] is None:
+                o["fn"]()
+                o["knows"] = {}
+                continue
+            total[o["sem"]] = total.get(o["sem"], 0) + o["inc"]
+            o["fn"]().then_inc(T.sem[o["sem"]], o["inc"])
+            o["ev"] = (o["sem"], total[o["sem"]])
+            o["knows"] = dict(k)
+            o["knows"][o["sem"]] = total[o["sem"]]
+        for s in sorted(total):
+            if know["p"].get(s, 0) < total[s]:
+                g.wait_ge(T.sem[s], total[s])
+        g.wait_ge(T.sem.sent, sends[0])
+
+    def el(n, k=1.0):
+        return max(n * k, 64) * EL
+
+    def ga(n):
+        return 0.055 + n * GATHER
+
+    def ts(out, ow, in0, ir, s1, o1, s2=None, o2=None, n=TC):
+        if o2 is None:
+            op("v", ir, ow, lambda: V.tensor_scalar(out, in0, s1, None, o1), el(n))
+        else:
+            op("v", ir, ow, lambda: V.tensor_scalar(out, in0, s1, s2, o1, o2), el(n))
+
+    def tt(out, ow, a, b, ir, o, c=None):
+        op("v", ir, ow, lambda: V.tensor_tensor(out, a, b, o), el(TC) if c is None else c)
+
+    def cp(out, ow, a, ir, c=None):
+        op("v", ir, ow, lambda: V.tensor_copy(out, a), el(TC) if c is None else c)
+
+    def sg(out, ow, a, ir, c=None, scale=None):
+        c = ga(C) if c is None else c
+        if scale is None:
+            op("s", ir, ow, lambda: S.activation(out, a, COPY), c)
+        else:
+            op("s", ir, ow, lambda: S.activation(out, a, COPY, scale=scale), c)
+
+    def lin(out, ow, a, ir, scale, bias, n=C):
+        op("s", ir, ow, lambda: S.activation(out, a, IDENT, bias=float(bias), scale=float(scale)), el(n))
+
+    def hslot(k):
+        return T.hr[:, k * C:(k + 1) * C], "hr%d" % k
+
+    def eslot(k):
+        return T.er[:, k * C:(k + 1) * C], "er%d" % k
+
+    def htab(k):
+        return T.ho[:, k * TC:(k + 1) * TC], "ho%d" % k
+
+    rot = [0]
+
+    def turn_mk():
+        k = rot[0] % NMK
+        rot[0] += 1
+        return T.mk[:, k * C:(k + 1) * C], "mk%d" % k, k, "sc%d" % k
+
+    def scan(mk, mr, k, sr):
+        op("v", [mr, "keep"], [sr],
+           lambda: V.tensor_tensor_scan(T.sc[:, k * C:(k + 1) * C], T.keep[:, :], mk, 0.0, A.mult, A.add), el(C, 0.5))
+        return T.sc[:, k * C + 15:(k + 1) * C:16], sr
+
+    def conv(win, wr, off, orr):
+        mk, mr, sc, sr = turn_mk()
+        tt(mk, [mr], win.indirect(off), T.mask[:, :], wr + [orr, "mask"], A.mult, ga(C))
+        return scan(mk, mr, sc, sr)
+
+    def to_off(out, ow, view, vr):
+        ts(out, [ow], view, [vr], float(C // 2), A.add)
+
+    def mm(bank, st, sts, sr, mv, mvs, mr):
+        op("t", sr + mr, [bank], lambda: P.matmul_mx(T[bank][:, 0:C], st, sts, mv, mvs, True, True), 0.3)
+
+    def quant(q, s, rd, wr, src, n):
+        op("v", rd, wr, lambda: V.quantize_mx(q, s, src), 0.012 + 0.28e-3 * n)
+
+    def load(qn, out, in_, res, sem, tail=2.0):
+        op(qn, [], [res], lambda: queues[qn].dma_start(out=out, in_=in_), 0.1, sem, 16, tail)
+
+    sends = [0]
+
+    def to_partner(r, bufs, sem, count, n, land, tail):
+        dst = T.cores[rank ^ MASKS[r]]
+        via = relay_of(core, dst, topo)
+        hop = dst if via is None else via
+        ids = []
+
+        def go(o, i):
+            sends[0] += send(g, T, topo, core, hop, o, i, sem, count)
+
+        for o, i, res in bufs:
+            op("p", [res], ["out" + sem], lambda o=o, i=i: go(o, i), 0.5)
+            ops[-1]["sem"] = None
+        op(None, ["out" + sem], [land], None, 0.0, None, 0, tail if via is None else 2 * tail, (sem, n))
+
+    def send_list(r):
+        to_partner(r, [(T["lo%d" % r][:, :], T["fo%d" % r][:, :], "fo%d" % r)], "al%d" % r, NL, NL, "lo%d" % r, 4.0)
+
+    def send_codes(r):
+        to_partner(r, [(T["lc%d" % r][:, :].bitcast(dt.uint8), T["xq%d" % r][:, :].bitcast(dt.uint8), "xq%d" % r),
+                       (T["ls%d" % r][:, :], T["xs%d" % r][:, :], "xq%d" % r)], "ac%d" % r, NE, 2 * NE, "lc%d" % r, 7.0)
+
+    load("y", T.fli[:, :], T.fl[:, :], "fli", "lf")
+    load("s", T.x0[:, :], T.x[:, :], "x0", "lx", 3.0)
+    load("y", T.ub[:, :], T.u[:, :], "ub", "lu")
+    load("y", T.mli[:, :], T.ml[:, :], "mli", "lm")
+    load("y", T.wq[:, :].bitcast(dt.uint8), T.wc[:, :], "wq", "lw")
+    load("y", T.wsp[:, :], T.ws[:, :], "wsp", "lq")
+    load("y", T.vb[:, :], T.v[:, :], "vb", "lv")
+
+    def iota(name, pattern, mult, n, flag=True):
+        if flag:
+            op("p", [], [name], lambda: g.iota(T[name][:, :], pattern, 0, mult, allow_small_or_imprecise_dtypes=True),
+               0.13 + 2 * n * EL)
+        else:
+            op("p", [], [name], lambda: g.iota(T[name][:, :], pattern, 0, mult), 0.13 + 2 * n * EL)
+
+    iota("pi", [[0, 2]], 1, 2, False)
+    iota("j16", [[0, TC], [1, 16]], 0, C)
+    iota("jf", [[1, C]], 0, C)
+    iota("c16", [[16, TC]], 0, TC)
+    op("v", [], ["et"], lambda: V.memset(T.et[:, :], 0.0), 0.9)
+    ts(T.p16i[:, :], ["p16i"], T.pi[:, :], ["pi"], 15, A.bitwise_and)
+    cp(T.p16[:, :], ["p16"], T.p16i[:, :], ["p16i"])
+    ts(T.mask[:, :], ["mask"], T.j16[:, :], ["j16", "p16"], T.p16[:, 0:1], A.is_equal, n=C)
+    ts(T.pn[:, :], ["pn"], T.pi[:, :], ["pi"], -1.0, A.mult)
+    lin(T.jc[:, :], ["jc"], T.jf[:, :], ["jf"], 1.0, -(C // 2))
+    op("s", ["j16"], ["keep"], lambda: S.activation(T.keep[:, :], T.j16[:, :], SIGN), el(C))
+    for k in (7, 15, 20):
+        sg(eslot(k)[0], [eslot(k)[1]], T.jc[:, :], ["jc"], el(C))
+    lin(T.mbig[:, :], ["mbig"], T.mask[:, :], ["mask"], 2e29, -1e29)
+    lin(T.key[:, :], ["key"], T.jf[:, :], ["jf"], -512.0, 512 * C + 224)
+
+    cp(T.fo0[:, :], ["fo0"], T.fli[:, :], ["fli"])
+    send_list(0)
+    op("v", ["jc", "fo0"], ["hr0"], lambda: V.tensor_copy(T.hr[:, 0:C].indirect(T.fo0[:, :]), T.jc[:, :]), 1.0)
+    mk, mr, sc, sr = turn_mk()
+    tt(mk, [mr], T.hr[:, 0:C], T.mask[:, :], ["hr0", "mask"], A.mult, el(C, 2))
+    to_off(htab(0)[0], "ho0", *scan(mk, mr, sc, sr))
+    ts(T.ffc[:, :], ["ffc"], T.fli[:, :], ["fli"], float(-(C // 2)), A.add)
+
+    quant(T.xq0[:, :], T.xs0[:, :], ["x0"], ["xq0"], T.x0[:, :], 4 * C)
+    send_codes(0)
+    quant(T.uq[:, :], T.uqs[:, :], ["ub"], ["uq"], T.ub[:, :], 512)
+    cp(T.uo[:, :], ["uo"], T.c16[:, 0:8], ["c16"])
+    cp(T.uk[:, :].bitcast(dt.uint32), ["uk"], T.uq[:, :].bitcast(dt.uint32).indirect(T.uo[:, :]), ["uq", "uo"], ga(128))
+    cp(T.uks[:, :], ["uks"], T.uqs[:, :].indirect(T.uo[:, :]), ["uq", "uo"], ga(128))
+    op("s", ["jf", "pn"], ["d0"], lambda: S.activation(T.diag[:, 0:128], T.jf[:, 0:128], SIGN, bias=T.pn[:, 0:1]), el(128))
+    op("s", ["d0"], ["d1"], lambda: S.activation(T.diag[:, 128:256], T.diag[:, 0:128], ActivationFunctionType.Square), el(128))
+    for b in range(4):
+        lo = 512 * b
+        op("s", ["d1", "et"], ["et%d" % b], lambda lo=lo, b=b: S.activation(
+            T.et[:, lo + b:lo + 512:4], T.diag[:, 128:256], IDENT, bias=0.5, scale=-0.5), el(128))
+    quant(T.eq[:, :], T.eqs[:, :], ["et", "et0", "et1", "et2", "et3"], ["eq"], T.et[:, :], 2048)
+    cp(T.mo[:, :], ["mo"], T.mli[:, :], ["mli"])
+    cp(T.mtf[:, :], ["mtf"], T.mli[:, :], ["mli"])
+    ts(T.jt[:, :], ["jt"], T.c16[:, :], ["c16", "p16"], T.p16[:, 0:1], A.add)
+    tt(T.loo[:, :], ["loo"], T.mtf[:, :], T.jt[:, :], ["mtf", "jt"], A.min)
+    tt(T.hio[:, :], ["hio"], T.mtf[:, :], T.jt[:, :], ["mtf", "jt"], A.max)
+    tt(T.dmt[:, :], ["dmt"], T.mtf[:, :], T.jt[:, :], ["mtf", "jt"], A.subtract)
+
+    def hrow(k, frm, tab):
+        w, wr = (T.jc[:, :], "jc") if frm is None else hslot(frm)
+        o, orr = htab(tab)
+        sg(hslot(k)[0], [hslot(k)[1]], w.indirect(o), [wr, orr])
+
+    def hconv(frm, tab, new):
+        w, wr = hslot(frm)
+        o, orr = htab(tab)
+        to_off(*htab(new), *conv(w, [wr], o, orr))
+
+    def erow(k, off, orr):
+        w, wr = eslot(k + 1)
+        sg(eslot(k)[0], [eslot(k)[1]], w.indirect(off), [wr, orr])
+
+    for r in range(3):
+        last = r == 2
+        xq, xs, xr = T["xq%d" % r], T["xs%d" % r], ["xq%d" % r]
+        eo, eor = T["lo%d" % r][:, :], "lo%d" % r
+        mm("p4", T.uk[:, :], T.uks[:, :], ["uk", "uks"], xq[:, :], xs[:, :], xr)
+        mm("p5", T.uk[:, :], T.uks[:, :], ["uk", "uks"], xq[:, :], xs[:, :], xr)
+        sg(T.s[:, :], ["s", "p4"], T.p4[:, 0:C], [], el(C))
+        if S_HOME:
+            cp(T.s2[:, :], ["s2", "p5"], T.p5[:, 0:C], [], el(C))
+        else:
+            sg(T.s2[:, :], ["s2", "p5"], T.p5[:, 0:C], [], el(C))
+        for b in range(4):
+            mm("p%d" % b, T.eq[:, 128 * b:128 * b + 128], T.eqs[:, 128 * b:128 * b + 128], ["eq"], xq[:, :], xs[:, :], xr)
+        if r:
+            hrow(0, None, 0)
+        hrow(1, 0, 0)
+        hrow(2, 1, 0)
+        hconv(1, 0, 1)
+        hrow(3, 2, 1)
+        for k in range(5):
+            hconv(3 + k, 1 + k, 2 + k)
+            if k < 4:
+                hrow(4 + k, 3 + k, 1 + k)
+        if r == 0:
+            sg(T.frow[:, :], ["frow"], T.jc[:, :].indirect(T.fo0[:, :]), ["jc", "fo0"])
+            v, vr = conv(T.frow[:, :], ["frow"], T.mo[:, :], "mo")
+            tt(T.dfm[:, :], ["dfm"], v, T.ffc[:, :], [vr, "ffc"], A.subtract)
+            cp(T.ff[:, :], ["ff"], T.fli[:, :], ["fli"])
+        for k in range(6, -1, -1):
+            erow(k, eo, eor)
+        to_off(T.eo8[:, :], "eo8", *conv(eslot(0)[0], [eslot(0)[1]], eo, eor))
+        for k in range(14, 7, -1):
+            erow(k, T.eo8[:, :], "eo8")
+        to_off(T.eo64[:, :], "eo64", *conv(eslot(8)[0], [eslot(8)[1]], T.eo8[:, :], "eo8"))
+        for k in range(19, 15, -1):
+            erow(k, T.eo64[:, :], "eo64")
+
+        cur = "s"
+        turn = 0
+        for level, (rad, n) in enumerate(LEVELS):
+            o, orr = htab(level)
+            base, side = cur, "s2"
+            if level:
+                side = "mc%d" % (level % 2)
+                if level in TWIN_HOME:
+                    cp(T[side][:, :], [side], T[cur][:, :], [cur], el(C))
+                else:
+                    sg(T[side][:, :], [side], T[cur][:, :], [cur], el(C))
+            for i in range(rad - 1):
+                d = "m%d" % (turn % 3)
+                turn += 1
+                z = base if i else side
+                tt(T[d][:, :], [d], T[cur][:, :].indirect(o), T[z][:, :], [cur, z, orr], A.max, ga(C))
+                cur = d
+        tt(T.cand[:, :], ["cand", "p5"], T[cur][:, :], T.p5[:, 0:C], [cur], A.is_equal, el(C))
+        for p, (lo, hi) in PARTS.items():
+            tt(T.y0[:, lo:hi], ["y0" + p], T.cand[:, lo:hi], T.key[:, lo:hi], ["cand", "key"], A.mult, el(hi - lo, 2))
+        cur = "y0"
+        turn = 1
+        for level, (rad, n) in enumerate(LEVELS):
+            orr = htab(level)[1]
+            base = cur
+            for i in range(rad - 1):
+                zz = "z%s%d" % ("ab"[i], level % 2)
+                for p, (lo, hi) in PARTS.items():
+                    if level in Z_HOME:
+                        ts(T[zz][:, lo:hi], [zz + p], T[base][:, lo:hi], [base + p], float(n * (i + 1)), A.add, n=hi - lo)
+                    else:
+                        lin(T[zz][:, lo:hi], [zz + p], T[base][:, lo:hi], [base + p], 1.0, n * (i + 1), hi - lo)
+            for i in range(rad - 1):
+                zz = "z%s%d" % ("ab"[i], level % 2)
+                d = "y%d" % (turn % 4)
+                turn += 1
+                for p, (lo, hi) in PARTS.items():
+                    off = T.ho[:, level * TC + lo // 16:level * TC + hi // 16]
+                    tt(T[d][:, lo:hi], [d + p], T[cur][:, :].indirect(off), T[zz][:, lo:hi],
+                       [cur + q for q in PARTS] + [zz + p, orr], A.max, ga(hi - lo))
+                cur = d
+        for b in range(4):
+            sg(T.fh[:, b * C:(b + 1) * C], ["fh%d" % b, "p%d" % b], T["p%d" % b][:, 0:C], [], el(C))
+        for b in range(4):
+            mm("p%d" % (4 + b), T.eq[:, 128 * b:128 * b + 128], T.eqs[:, 128 * b:128 * b + 128], ["eq"],
+               T["lc%d" % r][:, :], T["ls%d" % r][:, :], ["lc%d" % r])
+            sg(T.fs[:, b * C:(b + 1) * C], ["fs%d" % b, "p%d" % (4 + b)], T["p%d" % (4 + b)][:, 0:C], [], el(C))
+
+        tt(T.km[:, :], ["km"], T[cur][:, :], T.mask[:, :], [cur + p for p in PARTS] + ["mask"], A.mult, el(C, 2))
+        op("v", ["km", "keep"], ["ks"],
+           lambda: V.tensor_tensor_scan(T.ks[:, :], T.keep[:, :], T.km[:, :], 0.0, A.mult, A.add), el(C))
+        cp(T.ki[:, :], ["ki"], T.ks[:, 15:C:16], ["ks"])
+        ts(T.k0[:, :], ["k0"], T.ki[:, :], ["ki"], 7, A.bitwise_and)
+        ts(T.ka[:, :], ["ka"], T.ki[:, :], ["ki"], 9, A.logical_shift_right)
+        ts(T.k1[:, :], ["k1"], T.ki[:, :], ["ki"], 3, A.logical_shift_right, 7, A.bitwise_and)
+        ts(T.x1[:, :], ["x1"], T.k0[:, :], ["k0"], float(C), A.mult, float(C), A.add)
+        ts(T.k2[:, :], ["k2"], T.ki[:, :], ["ki"], 6, A.logical_shift_right, 7, A.bitwise_and)
+        tt(T.w1[:, :], ["w1"], T.x1[:, :], T.ka[:, :], ["x1", "ka"], A.subtract)
+        ts(T.x2[:, :], ["x2"], T.k1[:, :], ["k1"], float(C), A.mult, float(C // 2), A.add)
+        ts(T.x3[:, :], ["x3"], T.k2[:, :], ["k2"], float(C), A.mult, float(C // 2 - 3 * C), A.add)
+        v, vr = conv(T.er[:, 0:8 * C], ["er%d" % k for k in range(8)], T.w1[:, :], "w1")
+        tt(T.w2[:, :], ["w2"], T.x2[:, :], v, ["x2", vr], A.add)
+        v, vr = conv(T.er[:, 8 * C:16 * C], ["er%d" % k for k in range(8, 16)], T.w2[:, :], "w2")
+        tt(T.w3[:, :], ["w3"], T.x3[:, :], v, ["x3", vr], A.add)
+        to_off(T.to[:, :], "to", *conv(T.er[:, 16 * C:21 * C], ["er%d" % k for k in range(16, 21)], T.w3[:, :], "w3"))
+
+        for b in range(4):
+            sg(T.gt[:, b * C:(b + 1) * C], ["gt%d" % b], T.fs[:, b * C:(b + 1) * C].indirect(T.to[:, :]),
+               ["fs%d" % b, "to"])
+        nfo, nfr = T["fo%d" % (r + 1)], "fo%d" % (r + 1)
+        cp(T.mine[:, :], ["mine"], T.s[:, :].indirect(T.to[:, :]), ["s", "to"], ga(C))
+        tt(T.mhi[:, :], ["mhi"], T.mine[:, :].indirect(T.hio[:, :]), T.mbig[:, :], ["mine", "hio", "mbig"], A.min, ga(C))
+        mk, mr, sc, sr = turn_mk()
+        tt(mk, [mr], T.mine[:, :].indirect(T.loo[:, :]), T.mhi[:, :], ["mine", "mhi", "loo"], A.is_lt, ga(C))
+        v, vr = scan(mk, mr, sc, sr)
+        tt(T.ta[:, :], ["ta"], v, T.dfm[:, :], [vr, "dfm"], A.mult)
+        tt(T.tb[:, :], ["tb"], v, T.dmt[:, :], [vr, "dmt"], A.mult)
+        tt(nfo[:, :], [nfr], T.ta[:, :], T.ff[:, :], ["ta", "ff"], A.add)
+        if not last:
+            tt(T.ff[:, :], ["ff"], T.ta[:, :], T.ff[:, :], ["ta"], A.add)
+            send_list(r + 1)
+            ts(T.tc[:, :], ["tc"], T.ta[:, :], ["ta"], -2.0, A.mult)
+            tt(T.dfm[:, :], ["dfm"], T.tc[:, :], T.dfm[:, :], ["tc"], A.add)
+        tt(T.so[:, :], ["so"], T.tb[:, :], T.jt[:, :], ["tb", "jt"], A.add)
+        sg(T.srow[:, :], ["srow"], T.jc[:, :].indirect(T.so[:, :]), ["jc", "so"])
+        o, orr = htab(0)
+        for b in range(4):
+            tt(T.z[:, b:4 * C:4], ["z%d" % b], T.fh[:, b * C:(b + 1) * C].indirect(nfo[:, :]),
+               T.gt[:, b * C:(b + 1) * C], ["fh%d" % b, "gt%d" % b, nfr], A.add, ga(C))
+        quant(T.zq[:, :], T.zs[:, :], ["z0", "z1", "z2", "z3"], ["zq"], T.z[:, :], 4 * C)
+        to_off(o, orr, *conv(T.srow[:, :], ["srow"] + AFTER, o, orr))
+        for b in (2, 3, 0, 1):
+            bank = "p%d" % (4 + b)
+            mm(bank, T.wq[:, 128 * b:128 * b + 128], T.wsp[:, 128 * b:128 * b + 128], ["wq", "wsp"],
+               T.zq[:, :], T.zs[:, :], ["zq"])
+            if b in R_HOME:
+                ts(T.rb[:, b * C:(b + 1) * C], ["rb%d" % b, bank], T[bank][:, 0:C], [], 2.0 ** -6, A.mult, n=C)
+            else:
+                sg(T.rb[:, b * C:(b + 1) * C], ["rb%d" % b, bank], T[bank][:, 0:C], [], el(C), 2.0 ** -6)
+        for b in P_FAR:
+            sg(T.gp[:, b * C:(b + 1) * C], ["gp%d" % b], T.rb[:, b * C:(b + 1) * C].indirect(o), ["rb%d" % b, orr])
+        for b in [b for b in range(4) if b not in P_FAR]:
+            tt(T.xt[:, b:4 * C:4], ["xt%d" % b], T.rb[:, b * C:(b + 1) * C].indirect(o), T.fh[:, b * C:(b + 1) * C],
+               ["rb%d" % b, "fh%d" % b, orr], A.add, ga(C))
+        for b in P_FAR:
+            tt(T.xt[:, b:4 * C:4], ["xt%d" % b, "p%d" % b], T.gp[:, b * C:(b + 1) * C], T["p%d" % b][:, 0:C],
+               ["gp%d" % b], A.add, el(C))
+        quant(T["xq%d" % (r + 1)][:, :], T["xs%d" % (r + 1)][:, :], ["xt0", "xt1", "xt2", "xt3"], ["xq%d" % (r + 1)],
+              T.xt[:, :], 4 * C)
+        if not last:
+            send_codes(r + 1)
+        else:
+            sg(T.nlr[:, :], ["nlr"], T.jf[:, :].indirect(nfo[:, :]), ["jf", nfr])
+
+    quant(T.vq[:, :], T.vqs[:, :], ["vb"], ["vq"], T.vb[:, :], 512)
+    mm("p4", T.vq[:, :], T.vqs[:, :], ["vq"], T.xq3[:, :], T.xs3[:, :], ["xq3"])
+    sg(T.yb[:, :], ["yb", "p4"], T.p4[:, 0:C], [], el(C))
+
+    def store(out, in_, res, tail=2.0):
+        op("y", [res], [], lambda: g.sync.dma_start(out=out, in_=in_), 0.1, "lout", 16, tail)
+
+    store(T.nl[:, :], T.nlr[0:128:16, :], "nlr")
+    store(T.y[:, :], T.yb[:, :], "yb", 3.0)
+    store(T.oc[:, :], T.xq3[:, :].bitcast(dt.uint8), "xq3")
+    for k in range(4):
+        store(T.osc[4 * k:4 * k + 4, :], T.xs3[32 * k:32 * k + 4, :], "xq3")
+    emit()
+
+
+def relay_program(g, core, T, topo):
+    n = 0
+    for r in range(3):
+        for i, src in enumerate(T.cores):
+            dst = T.cores[i ^ MASKS[r]]
+            if relay_of(src, dst, topo) != core:
+                continue
+            g.wait_ge(T.sem["al%d" % r], NL)
+            n += send(g, T, topo, core, dst, T["lo%d" % r][:, :], T["lo%d" % r][:, :], "al%d" % r, NL)
+            g.wait_ge(T.sem["ac%d" % r], 2 * NE)
+            n += send(g, T, topo, core, dst, T["lc%d" % r][:, :].bitcast(dt.uint8),
+                      T["lc%d" % r][:, :].bitcast(dt.uint8), "ac%d" % r, NE)
+            n += send(g, T, topo, core, dst, T["ls%d" % r][:, :], T["ls%d" % r][:, :], "ac%d" % r, NE)
+    if n:
+        g.wait_ge(T.sem.sent, n)

@@ -6,20 +6,27 @@ IDENT = ActivationFunctionType.Identity
 SIGN = ActivationFunctionType.Sign
 C = 288
 TC = C // 16
+H = C // 2
+M = 1024.0
+UP = 2.0 ** 40
+BIG = 2.0 ** 72
 MASKS = [4, 1, 2]
-LEVELS = [(3, 1), (3, 3), (2, 9), (2, 18), (2, 36), (2, 72), (2, 144)]
-PARTS = {"a": (0, 160), "b": (160, C)}
-Z_HOME = (2,)
-TWIN_HOME = ()
-R_HOME = (1,)
-WAKE, GATHER, EL = 0.06, 1.5e-3, 1.04e-3
-LOOK, EDGE = 1.0, 1.0
-HASTE = {"hr": -1.0, "er": -0.6, "sc": 0.6, "et": 0.3, "rb": 3.0, "fh": -0.6, "k": 0.3, "ho": -3.0, "gp": -3.0}
-AFTER = ["zq"]
-S_HOME = False
+LEVELS = [(2, 1), (2, 2), (2, 4), (2, 8), (2, 16), (3, 32), (3, 96)]
+SPLIT = {"a": (0, 160), "b": (160, C)}
+WHOLE = {"ab": (0, C)}
+SPLIT_IN = (0,)
+R_HOME = ()
 P_FAR = (2, 3)
-NE, NL = 8, 2
-NMK = 6
+TWIN = True
+ON_S = ()
+SMALL_S = ("enf", "pef", "tc", "td")
+WAKE, GATHER, EL = 0.1, 1.62e-3, 1.04e-3
+LOOK, EDGE = 1.0, 1.0
+HASTE = {'x0v': 11.5, '+zv': -0.6, 'zs': 6.0, '+score0': 3.6, 'xs2': 1.0, 'fss0': -6.5, '+x0v': 3.7, 'xv': -7.5, '+matess': 1.7, 'leadv0': -12, 'zv': -7.5, '+xs2': -3.8, '+keys': 1.1, 'linev': -7.5, 'fss': -12, 'powv': 6.0, '+matesv': 0.6, '+backs': 2.4, 'backv': 11.5, '+walks0': -1.6, '+fars': 1.8, 'walks': 10.5, 'tees2': -4.5, '+rbs2': -2.0, 'zs2': 12, '+xv2': -4.9, '+backv': 3.6, 'pows': 4.0, '+score': 0.9, '+walks': 2.2, '+linev0': 1.4, '+fss0': -2.1, '+': -2.9, 'scores0': -7.5, '+splicev0': -0.5, 'matesv': -2.0, '+xs': -0.7, 'keys': -5.5, '+splicev': -4.4, 'keyv': -5.5, '+line': 1.8, '+xqv': -2.8, '+keys0': 5.0, '+fars0': -0.3, '+powv': -3.2, '+line0': 3.4, '+scores0': 2.6, '+walkv0': 1.5, '+zv2': -4.8, '+leadv0': -5.0, '+keyv': 0.6}
+SPAN = [0.0]
+LIST_US, CODE_US = 3.0, 5.0
+NE, NL = 8, 8
+NB, NF = 16, 3
 
 SCRATCH = {}
 
@@ -34,37 +41,53 @@ _b("x0 xt z fh fs gt", 4 * C, "bfloat16")
 _b("rb gp", 4 * C, "float32")
 _b("xq0 xq1 xq2 xq3 lc0 lc1 lc2 zq", C, CODE)
 _b("xs0 xs1 xs2 xs3 ls0 ls1 ls2 zs", C, "uint8")
-_b("fo0 fo1 fo2 fo3 lo0 lo1 lo2 w1 w2 w3 to mo loo hio eo8 eo64 so", TC, "uint16")
+_b("fo0 fo1 fo2 fo3 sb0 sb1 sb2 lb0 lb1 lb2 ho0 ho1 mo", TC, "uint16")
+_b("sa0 sa1 sa2 la0 la1 la2", 3 * TC, "uint16")
+_b("ft", 6 * TC, "uint16")
+_b("tu", 4 * TC, "uint16")
+_b("rep", TC, "uint16")
 _b("wq eq", 512, CODE)
 _b("wsp eqs", 512, "uint8")
 _b("uq uk vq", 128, CODE)
 _b("uqs uks vqs", 128, "uint8")
 _b("et", 2048, "bfloat16")
 _b("ub vb", 512, "bfloat16")
-_b("fli mli ki ka k0 k1 k2 x1", TC, "int32")
-_b("jf j16 key s s2 mc0 mc1 m0 m1 m2 y0 y1 y2 y3 za0 za1 zb0 zb1 mine mhi km ks yb nlr mbig", C, "float32")
-_b("jc mask keep frow srow cand", C, "bfloat16")
-_b("mk sc", NMK * C, "bfloat16")
-_b("hr", 8 * C, "bfloat16")
-_b("er", 21 * C, "bfloat16")
-_b("ho", 7 * TC, "uint16")
+_b("fli mli", TC, "int32")
+_b("ti", 8 * TC, "int32")
+_b("tf", 22 * TC, "float32")
+_b("key0 key1 keyb step s y0 y1 y2 y3 za0 za1 zb0 twin dn st ord so top ck run lead ms nms yb nlr", C, "float32")
+_b("jf fla flb", C + 16, "float32")
+_b("jc", C + 16, "bfloat16")
+_b("cand sw", C, "bfloat16")
+_b("cv pl oer sc2", 2 * C, "bfloat16")
+_b("both", 2 * C, "float32")
+_b("fr", 8 * C, "bfloat16")
+_b("pr", 3 * C, "bfloat16")
+_b("row sc", NB * C, "bfloat16")
+_b("scf", NF * C, "float32")
 _b("uo", 8, "uint16")
-_b("c16 jt mtf ffc ff dfm dmt ta tb tc x2 x3", TC, "float32")
+_b("c16", TC, "float32")
+_b("cva cvb", 16, "float32")
+_b("cv16", 16, "bfloat16")
 _b("pi p16i", 2, "int32")
-_b("pn p16", 2, "float32")
+_b("pn p16 p17", 2, "float32")
+_b("col", 8, "float32")
 _b("diag", 256, "float32")
 _b("p0 p1 p2 p3 p4 p5 p6 p7", 512, "float32", "psum")
+TU = "ro lo wa to".split()
+TI = "ki dj kl q x0i x1i a0i a1i".split()
+TF = "jt ca dfm dh i lnf rl enf pef zz t m w0 w0a ta tc th td u0 u1".split()
 
 SEMAPHORES = ["cv", "cs", "ct", "cp", "lx", "lu", "lv", "lf", "lm", "lw", "lq", "lout", "sent"]
-SEMAPHORES += ["ac%d" % r for r in range(3)] + ["al%d" % r for r in range(3)]
+SEMAPHORES += [k + str(r) for k in ("ac", "aa", "ab") for r in range(3)]
 
 
-def relay_of(src, dst, topo):
+def relay_of(src, dst, topo, k):
     if topo.may_write(src, dst):
         return None
     cs = [c for c in topo.cores_of(src) if topo.may_write(c, dst)]
-    near = [c for c in cs if topo.die(c) == topo.die(src)]
-    return (near or cs)[0]
+    cs = [c for c in cs if topo.die(c) == topo.die(src)] or cs
+    return cs[k % len(cs)]
 
 
 def send(g, T, topo, src, dst, out_ap, in_ap, sem, count):
@@ -87,20 +110,20 @@ def order(ops):
     far = [0.0] * n
     for i in range(n - 1, -1, -1):
         o = ops[i]
-        far[i] = o["c"] + o["tail"] + max([far[u] + WAKE for u in users[i]] or [0.0])
+        far[i] = o["c"] + o["tail"] + HASTE.get("+" + o["kind"], 0.0) + max([far[u] + WAKE for u in users[i]] or [0.0])
     far = [far[i] + HASTE.get(ops[i]["kind"], 0.0) for i in range(n)]
     left = [len(o["deps"]) for o in ops]
     ready = [0.0] * n
-    end = [0.0] * n
     open_ = {}
     free = {}
     out = []
+    span = [0.0]
 
     def finish(i, t):
-        end[i] = t
+        span[0] = max(span[0], t)
         for u in users[i]:
             left[u] -= 1
-            ready[u] = max(ready[u], t if ops[i]["q"] == ops[u]["q"] and not ops[i]["tail"] and ops[i]["free"] else t + WAKE)
+            ready[u] = max(ready[u], t + WAKE)
             if left[u] == 0:
                 release(u)
 
@@ -120,8 +143,7 @@ def order(ops):
             if not cand:
                 continue
             t = max(free.get(q, 0.0), min(ready[i] for i in cand))
-            now = [i for i in cand if ready[i] <= t + 1e-9]
-            b = max(now, key=lambda i: (far[i], -i))
+            b = max((i for i in cand if ready[i] <= t + 1e-9), key=lambda i: far[i])
             stop = t + ops[b]["c"]
             for i in cand:
                 if far[i] > far[b] + EDGE and ready[i] < stop and ready[i] - t < LOOK * (stop - ready[i]):
@@ -134,6 +156,7 @@ def order(ops):
         free[q] = s + ops[b]["c"]
         out.append(b)
         finish(b, free[q] + ops[b]["tail"])
+    SPAN[0] = span[0]
     return out
 
 
@@ -146,7 +169,13 @@ def rank_program(g, core, T, topo):
     own = {"v": "cv", "s": "cs", "t": "ct", "p": "cp"}
     V, S, P = g.vector, g.scalar, g.tensor
     ops = []
+    stage = ["const", ""]
     acc = {}
+
+    def phase(name, mark=None):
+        stage[0] = name
+        if mark is not None:
+            stage[1] = mark
 
     def op(qn, rd, wr, fn, cost, sem=None, inc=1, tail=0.0, ev=None):
         deps = set()
@@ -165,7 +194,8 @@ def rank_program(g, core, T, topo):
         for r in wr:
             acc[r] = [me, []]
         deps.discard(me)
-        ops.append(dict(q=qn, c=cost, tail=tail, kind=(wr or [""])[0].rstrip("0123456789"), deps=deps, fn=fn, sem=sem or own.get(qn), inc=inc, ev=ev, free=False))
+        kind = stage[0] + (qn if qn in ("s", "v") else "") + stage[1] if qn else ""
+        ops.append(dict(q=qn, c=cost, tail=tail, kind=kind, deps=deps, fn=fn, sem=sem or own.get(qn), inc=inc, ev=ev))
         return me
 
     def emit():
@@ -209,93 +239,130 @@ def rank_program(g, core, T, topo):
     def ga(n):
         return 0.055 + n * GATHER
 
-    def ts(out, ow, in0, ir, s1, o1, s2=None, o2=None, n=TC):
+    def R(name, lo=None, hi=None, tag=None):
+        if lo is None:
+            return T[name][:, :], [name]
+        return T[name][:, lo:hi], [tag or name]
+
+    def slot(name, k, n=C):
+        return T[name][:, k * n:(k + 1) * n], ["%s%d" % (name, k)]
+
+    def tab(name, n=1):
+        for buf, names in (("tu", TU), ("ti", TI), ("tf", TF)):
+            if name in names:
+                k = names.index(name)
+                return T[buf][:, k * TC:(k + n) * TC], names[k:k + n]
+
+    def by(win, off):
+        return win[0].indirect(off[0]), win[1] + off[1]
+
+    def num(x):
+        return (x, []) if isinstance(x, (int, float)) else x
+
+    def ts(out, a, s1, o1, s2=None, o2=None, c=None):
+        s1 = num(s1)
+        c = el(TC) if c is None else c
         if o2 is None:
-            op("v", ir, ow, lambda: V.tensor_scalar(out, in0, s1, None, o1), el(n))
+            op("v", a[1] + s1[1], out[1], lambda: V.tensor_scalar(out[0], a[0], s1[0], None, o1), c)
         else:
-            op("v", ir, ow, lambda: V.tensor_scalar(out, in0, s1, s2, o1, o2), el(n))
+            s2 = num(s2)
+            op("v", a[1] + s1[1] + s2[1], out[1], lambda: V.tensor_scalar(out[0], a[0], s1[0], s2[0], o1, o2), c)
 
-    def tt(out, ow, a, b, ir, o, c=None):
-        op("v", ir, ow, lambda: V.tensor_tensor(out, a, b, o), el(TC) if c is None else c)
+    def tt(out, a, b, o, c=None):
+        op("v", a[1] + b[1], out[1], lambda: V.tensor_tensor(out[0], a[0], b[0], o), el(TC) if c is None else c)
 
-    def cp(out, ow, a, ir, c=None):
-        op("v", ir, ow, lambda: V.tensor_copy(out, a), el(TC) if c is None else c)
+    def cp(out, a, c=None):
+        op("v", a[1], out[1], lambda: V.tensor_copy(out[0], a[0]), el(TC) if c is None else c)
 
-    def sg(out, ow, a, ir, c=None, scale=None):
-        c = ga(C) if c is None else c
-        if scale is None:
-            op("s", ir, ow, lambda: S.activation(out, a, COPY), c)
+    def act(out, a, c, scale=1.0, bias=0.0, func=IDENT):
+        scale, bias = num(scale), num(bias)
+        if func is IDENT and not scale[1] and not bias[1] and scale[0] == 1.0 and bias[0] == 0.0:
+            op("s", a[1], out[1], lambda: S.activation(out[0], a[0], COPY), c)
         else:
-            op("s", ir, ow, lambda: S.activation(out, a, COPY, scale=scale), c)
+            op("s", a[1] + scale[1] + bias[1], out[1],
+               lambda: S.activation(out[0], a[0], func, bias=bias[0], scale=scale[0]), c)
 
-    def lin(out, ow, a, ir, scale, bias, n=C):
-        op("s", ir, ow, lambda: S.activation(out, a, IDENT, bias=float(bias), scale=float(scale)), el(n))
+    def lin(out, a, scale, bias):
+        if out[1][0] in SMALL_S:
+            act(out, a, el(TC), scale, bias)
+        else:
+            ts(out, a, scale, A.mult, bias, A.add)
 
-    def hslot(k):
-        return T.hr[:, k * C:(k + 1) * C], "hr%d" % k
+    def pick(out, win, off):
+        if out[1][0] in ON_S:
+            act(out, by(win, off), ga(C))
+        else:
+            cp(out, by(win, off), ga(C))
 
-    def eslot(k):
-        return T.er[:, k * C:(k + 1) * C], "er%d" % k
+    def col(k):
+        return T.col[:, k:k + 1], ["col%d" % k]
 
-    def htab(k):
-        return T.ho[:, k * TC:(k + 1) * TC], "ho%d" % k
+    DOWN, DOWN_M, LESS_M, LESS, LESS_2 = range(5)
+    turn = {"row": 0, "sc": 0, "scf": 0}
 
-    rot = [0]
+    def fresh(name, n):
+        turn[name] += 1
+        return turn[name] % n
 
-    def turn_mk():
-        k = rot[0] % NMK
-        rot[0] += 1
-        return T.mk[:, k * C:(k + 1) * C], "mk%d" % k, k, "sc%d" % k
+    def scan(out, d0, d1, first, o0, o1, c):
+        op("v", d0[1] + d1[1], out[1], lambda: V.tensor_tensor_scan(out[0], d0[0], d1[0], first, o0, o1), c)
 
-    def scan(mk, mr, k, sr):
-        op("v", [mr, "keep"], [sr],
-           lambda: V.tensor_tensor_scan(T.sc[:, k * C:(k + 1) * C], T.keep[:, :], mk, 0.0, A.mult, A.add), el(C, 0.5))
-        return T.sc[:, k * C + 15:(k + 1) * C:16], sr
+    def table_of(row, wide=False):
+        name = "scf" if wide else "sc"
+        k = fresh(name, NF if wide else NB)
+        out = slot(name, k)
+        scan(out, slot("cv", 0), row, 0.0, A.mult, A.add, el(C, 1.0 if wide else 0.5))
+        return T[name][:, k * C + 15:(k + 1) * C:16], out[1]
 
-    def conv(win, wr, off, orr):
-        mk, mr, sc, sr = turn_mk()
-        tt(mk, [mr], win.indirect(off), T.mask[:, :], wr + [orr, "mask"], A.mult, ga(C))
-        return scan(mk, mr, sc, sr)
+    def offsets(out, view):
+        ts(out, view, col(DOWN), A.mult, float(H), A.add)
 
-    def to_off(out, ow, view, vr):
-        ts(out, [ow], view, [vr], float(C // 2), A.add)
+    def spare():
+        return slot("row", fresh("row", NB))
 
     def mm(bank, st, sts, sr, mv, mvs, mr):
-        op("t", sr + mr, [bank], lambda: P.matmul_mx(T[bank][:, 0:C], st, sts, mv, mvs, True, True), 0.3)
+        op("t", sr + mr, [bank], lambda: P.matmul_mx(T[bank][:, 0:C], st, sts, mv, mvs, True, True), 0.38)
 
     def quant(q, s, rd, wr, src, n):
-        op("v", rd, wr, lambda: V.quantize_mx(q, s, src), 0.012 + 0.28e-3 * n)
+        op("v", rd, wr, lambda: V.quantize_mx(q, s, src), 0.015 + 0.28e-3 * n)
 
     def load(qn, out, in_, res, sem, tail=2.0):
         op(qn, [], [res], lambda: queues[qn].dma_start(out=out, in_=in_), 0.1, sem, 16, tail)
 
+    def out_of(out, bank, scale=1.0, home=False):
+        o, a = (out[0], out[1] + [bank]), (T[bank][:, 0:C], [])
+        if home:
+            ts(o, a, scale, A.mult, c=el(C))
+        else:
+            act(o, a, el(C), scale)
+
     sends = [0]
 
-    def to_partner(r, bufs, sem, count, n, land, tail):
+    def to_partner(r, bufs, sem, count, land, tail, lane):
         dst = T.cores[rank ^ MASKS[r]]
-        via = relay_of(core, dst, topo)
+        via = relay_of(core, dst, topo, lane)
         hop = dst if via is None else via
-        ids = []
 
         def go(o, i):
             sends[0] += send(g, T, topo, core, hop, o, i, sem, count)
 
         for o, i, res in bufs:
-            op("p", [res], ["out" + sem], lambda o=o, i=i: go(o, i), 0.5)
+            op("p", res, ["out" + sem], lambda o=o, i=i: go(o, i), 0.3)
             ops[-1]["sem"] = None
-        op(None, ["out" + sem], [land], None, 0.0, None, 0, tail if via is None else 2 * tail, (sem, n))
+        op(None, ["out" + sem], [land], None, 0.0, None, 0, tail if via is None else 2 * tail, (sem, count * len(bufs)))
 
-    def send_list(r):
-        to_partner(r, [(T["lo%d" % r][:, :], T["fo%d" % r][:, :], "fo%d" % r)], "al%d" % r, NL, NL, "lo%d" % r, 4.0)
+    def send_list(r, k, res):
+        a, b = "l%s%d" % (k, r), "s%s%d" % (k, r)
+        to_partner(r, [(T[a][:, :], T[b][:, :], res)], "a%s%d" % (k, r), NL, a, LIST_US, 1)
 
     def send_codes(r):
-        to_partner(r, [(T["lc%d" % r][:, :].bitcast(dt.uint8), T["xq%d" % r][:, :].bitcast(dt.uint8), "xq%d" % r),
-                       (T["ls%d" % r][:, :], T["xs%d" % r][:, :], "xq%d" % r)], "ac%d" % r, NE, 2 * NE, "lc%d" % r, 7.0)
+        to_partner(r, [(T["lc%d" % r][:, :].bitcast(dt.uint8), T["xq%d" % r][:, :].bitcast(dt.uint8), ["xq%d" % r]),
+                       (T["ls%d" % r][:, :], T["xs%d" % r][:, :], ["xq%d" % r])], "ac%d" % r, NE, "lc%d" % r, CODE_US, 0)
 
     load("y", T.fli[:, :], T.fl[:, :], "fli", "lf")
     load("s", T.x0[:, :], T.x[:, :], "x0", "lx", 3.0)
-    load("y", T.ub[:, :], T.u[:, :], "ub", "lu")
     load("y", T.mli[:, :], T.ml[:, :], "mli", "lm")
+    load("y", T.ub[:, :], T.u[:, :], "ub", "lu")
     load("y", T.wq[:, :].bitcast(dt.uint8), T.wc[:, :], "wq", "lw")
     load("y", T.wsp[:, :], T.ws[:, :], "wsp", "lq")
     load("y", T.vb[:, :], T.v[:, :], "vb", "lv")
@@ -303,222 +370,249 @@ def rank_program(g, core, T, topo):
     def iota(name, pattern, mult, n, flag=True):
         if flag:
             op("p", [], [name], lambda: g.iota(T[name][:, :], pattern, 0, mult, allow_small_or_imprecise_dtypes=True),
-               0.13 + 2 * n * EL)
+               0.16 + 2 * n * EL)
         else:
-            op("p", [], [name], lambda: g.iota(T[name][:, :], pattern, 0, mult), 0.13 + 2 * n * EL)
+            op("p", [], [name], lambda: g.iota(T[name][:, :], pattern, 0, mult), 0.16 + 2 * n * EL)
 
     iota("pi", [[0, 2]], 1, 2, False)
-    iota("j16", [[0, TC], [1, 16]], 0, C)
-    iota("jf", [[1, C]], 0, C)
+    iota("jf", [[1, C + 16]], 0, C + 16)
     iota("c16", [[16, TC]], 0, TC)
-    op("v", [], ["et"], lambda: V.memset(T.et[:, :], 0.0), 0.9)
-    ts(T.p16i[:, :], ["p16i"], T.pi[:, :], ["pi"], 15, A.bitwise_and)
-    cp(T.p16[:, :], ["p16"], T.p16i[:, :], ["p16i"])
-    ts(T.mask[:, :], ["mask"], T.j16[:, :], ["j16", "p16"], T.p16[:, 0:1], A.is_equal, n=C)
-    ts(T.pn[:, :], ["pn"], T.pi[:, :], ["pi"], -1.0, A.mult)
-    lin(T.jc[:, :], ["jc"], T.jf[:, :], ["jf"], 1.0, -(C // 2))
-    op("s", ["j16"], ["keep"], lambda: S.activation(T.keep[:, :], T.j16[:, :], SIGN), el(C))
-    for k in (7, 15, 20):
-        sg(eslot(k)[0], [eslot(k)[1]], T.jc[:, :], ["jc"], el(C))
-    lin(T.mbig[:, :], ["mbig"], T.mask[:, :], ["mask"], 2e29, -1e29)
-    lin(T.key[:, :], ["key"], T.jf[:, :], ["jf"], -512.0, 512 * C + 224)
+    jf, jc = R("jf", 0, C), R("jc")
+    p16 = (T.p16[:, 0:1], ["p16"])
+    ts(R("p16i"), R("pi"), 15, A.bitwise_and)
+    cp(R("p16"), R("p16i"))
+    ts(R("p17"), R("p16i"), 1.0, A.add)
+    act(jc, R("jf"), el(C), 1.0, float(-H))
+    act(R("key0"), jf, el(C), M, C - 1.0)
+    act(R("key1"), jf, el(C), M, C - 2.0)
+    act(R("keyb"), jf, el(C), -M, M * C)
+    ts(R("cva"), R("jf", 0, 16), p16, A.not_equal)
+    ts(R("cvb"), R("jf", 0, 16), (T.p17[:, 0:1], ["p17"]), A.is_equal, UP, A.mult)
+    tt(R("cv16"), R("cva"), R("cvb"), A.max)
+    ts(R("rep"), R("jf", 0, TC), 0.0, A.mult, p16, A.add)
+    act(slot("cv", 0), by(R("cv16"), R("rep")), ga(C))
+    act(slot("cv", 1), slot("cv", 0), el(C))
+    ts(col(DOWN), p16, 15.0, A.is_equal, 1.0 / UP, A.max)
+    for k, f in ((DOWN_M, 1.0 / M), (LESS_M, -1.0 / M), (LESS, -1.0), (LESS_2, -2.0)):
+        act(col(k), col(DOWN), el(1), f)
+    act(R("step"), jf, el(C), 0.0, M + 1.0)
+    act(R("fla", 0, 1, "fla0"), R("jf", 0, 1), el(1))
 
-    cp(T.fo0[:, :], ["fo0"], T.fli[:, :], ["fli"])
-    send_list(0)
-    op("v", ["jc", "fo0"], ["hr0"], lambda: V.tensor_copy(T.hr[:, 0:C].indirect(T.fo0[:, :]), T.jc[:, :]), 1.0)
-    mk, mr, sc, sr = turn_mk()
-    tt(mk, [mr], T.hr[:, 0:C], T.mask[:, :], ["hr0", "mask"], A.mult, el(C, 2))
-    to_off(htab(0)[0], "ho0", *scan(mk, mr, sc, sr))
-    ts(T.ffc[:, :], ["ffc"], T.fli[:, :], ["fli"], float(-(C // 2)), A.add)
-
+    phase("first")
+    cp(R("fo0"), R("fli"))
+    phase("x0")
     quant(T.xq0[:, :], T.xs0[:, :], ["x0"], ["xq0"], T.x0[:, :], 4 * C)
     send_codes(0)
     quant(T.uq[:, :], T.uqs[:, :], ["ub"], ["uq"], T.ub[:, :], 512)
-    cp(T.uo[:, :], ["uo"], T.c16[:, 0:8], ["c16"])
-    cp(T.uk[:, :].bitcast(dt.uint32), ["uk"], T.uq[:, :].bitcast(dt.uint32).indirect(T.uo[:, :]), ["uq", "uo"], ga(128))
-    cp(T.uks[:, :], ["uks"], T.uqs[:, :].indirect(T.uo[:, :]), ["uq", "uo"], ga(128))
-    op("s", ["jf", "pn"], ["d0"], lambda: S.activation(T.diag[:, 0:128], T.jf[:, 0:128], SIGN, bias=T.pn[:, 0:1]), el(128))
-    op("s", ["d0"], ["d1"], lambda: S.activation(T.diag[:, 128:256], T.diag[:, 0:128], ActivationFunctionType.Square), el(128))
+    cp(R("uo"), R("c16", 0, 8))
+    cp((T.uk[:, :].bitcast(dt.uint32), ["uk"]), (T.uq[:, :].bitcast(dt.uint32).indirect(T.uo[:, :]), ["uq", "uo"]), ga(128))
+    cp(R("uks"), (T.uqs[:, :].indirect(T.uo[:, :]), ["uq", "uo"]), ga(128))
+    phase("unit")
+    op("v", [], ["et"], lambda: V.memset(T.et[:, :], 0.0), 1.06)
+    ts(R("pn"), R("pi"), -1.0, A.mult)
+    act(R("diag", 0, 128, "d0"), R("jf", 0, 128), el(128), 1.0, (T.pn[:, 0:1], ["pn"]), SIGN)
+    act(R("diag", 128, 256, "d1"), R("diag", 0, 128, "d0"), el(128), 1.0, 0.0, ActivationFunctionType.Square)
     for b in range(4):
         lo = 512 * b
-        op("s", ["d1", "et"], ["et%d" % b], lambda lo=lo, b=b: S.activation(
-            T.et[:, lo + b:lo + 512:4], T.diag[:, 128:256], IDENT, bias=0.5, scale=-0.5), el(128))
+        act((T.et[:, lo + b:lo + 512:4], ["et%d" % b]), (T.diag[:, 128:256], ["d1", "et"]), el(128), -0.5, 0.5)
     quant(T.eq[:, :], T.eqs[:, :], ["et", "et0", "et1", "et2", "et3"], ["eq"], T.et[:, :], 2048)
-    cp(T.mo[:, :], ["mo"], T.mli[:, :], ["mli"])
-    cp(T.mtf[:, :], ["mtf"], T.mli[:, :], ["mli"])
-    ts(T.jt[:, :], ["jt"], T.c16[:, :], ["c16", "p16"], T.p16[:, 0:1], A.add)
-    tt(T.loo[:, :], ["loo"], T.mtf[:, :], T.jt[:, :], ["mtf", "jt"], A.min)
-    tt(T.hio[:, :], ["hio"], T.mtf[:, :], T.jt[:, :], ["mtf", "jt"], A.max)
-    tt(T.dmt[:, :], ["dmt"], T.mtf[:, :], T.jt[:, :], ["mtf", "jt"], A.subtract)
+    phase("mates")
+    cp(R("mo"), R("mli"))
+    ts(tab("jt"), R("c16"), p16, A.add)
+    tt(tab("u0"), R("mli"), tab("jt"), A.is_lt)
+    ts(tab("ca"), tab("u0"), float(C), A.mult)
 
-    def hrow(k, frm, tab):
-        w, wr = (T.jc[:, :], "jc") if frm is None else hslot(frm)
-        o, orr = htab(tab)
-        sg(hslot(k)[0], [hslot(k)[1]], w.indirect(o), [wr, orr])
+    def difference(out, view, minus):
+        offsets(tab("u0"), view)
+        tt(tab("u1"), tab("u0"), minus, A.subtract)
+        ts(out, tab("u1"), col(DOWN), A.mult)
 
-    def hconv(frm, tab, new):
-        w, wr = hslot(frm)
-        o, orr = htab(tab)
-        to_off(*htab(new), *conv(w, [wr], o, orr))
+    first = spare()
+    op("v", ["jc", "fo0"], first[1], lambda: V.tensor_copy(first[0].indirect(T.fo0[:, :]), T.jc[:, 0:C]), 1.2)
+    offsets(R("ho0"), table_of(first))
+    a, b = spare(), spare()
+    act(a, by(jc, R("mo")), ga(C))
+    act(b, by(a, R("ho0")), ga(C))
+    difference(tab("dh"), table_of(b), R("ho0"))
 
-    def erow(k, off, orr):
-        w, wr = eslot(k + 1)
-        sg(eslot(k)[0], [eslot(k)[1]], w.indirect(off), [wr, orr])
+    def parts(name):
+        return T[name][:, :], [name + "a", name + "b"]
+
+    def part(name, p, lo, hi):
+        return T[name][:, lo:hi], [name + k for k in p]
 
     for r in range(3):
         last = r == 2
+        PARTS = SPLIT if r in SPLIT_IN else WHOLE
         xq, xs, xr = T["xq%d" % r], T["xs%d" % r], ["xq%d" % r]
-        eo, eor = T["lo%d" % r][:, :], "lo%d" % r
-        mm("p4", T.uk[:, :], T.uks[:, :], ["uk", "uks"], xq[:, :], xs[:, :], xr)
-        mm("p5", T.uk[:, :], T.uks[:, :], ["uk", "uks"], xq[:, :], xs[:, :], xr)
-        sg(T.s[:, :], ["s", "p4"], T.p4[:, 0:C], [], el(C))
-        if S_HOME:
-            cp(T.s2[:, :], ["s2", "p5"], T.p5[:, 0:C], [], el(C))
-        else:
-            sg(T.s2[:, :], ["s2", "p5"], T.p5[:, 0:C], [], el(C))
-        for b in range(4):
-            mm("p%d" % b, T.eq[:, 128 * b:128 * b + 128], T.eqs[:, 128 * b:128 * b + 128], ["eq"], xq[:, :], xs[:, :], xr)
-        if r:
-            hrow(0, None, 0)
-        hrow(1, 0, 0)
-        hrow(2, 1, 0)
-        hconv(1, 0, 1)
-        hrow(3, 2, 1)
-        for k in range(5):
-            hconv(3 + k, 1 + k, 2 + k)
-            if k < 4:
-                hrow(4 + k, 3 + k, 1 + k)
+        fo, nfo = R("fo%d" % r), R("fo%d" % (r + 1))
+        ho, nho = R("ho%d" % (r % 2)), R("ho%d" % ((r + 1) % 2))
+        phase("pow", "0" if r == 0 else "")
+        tabs = [fo] + [slot("ft", k, TC) for k in range(6)]
+        act(slot("fr", 0), by(jc, fo), ga(C))
+        for k in range(1, 8):
+            act(slot("fr", k), by(slot("fr", k - 1), tabs[min(k - 1, 5)]), ga(C))
+            if k != 6:
+                offsets(tabs[min(k, 6)], table_of(slot("fr", k)))
         if r == 0:
-            sg(T.frow[:, :], ["frow"], T.jc[:, :].indirect(T.fo0[:, :]), ["jc", "fo0"])
-            v, vr = conv(T.frow[:, :], ["frow"], T.mo[:, :], "mo")
-            tt(T.dfm[:, :], ["dfm"], v, T.ffc[:, :], [vr, "ffc"], A.subtract)
-            cp(T.ff[:, :], ["ff"], T.fli[:, :], ["fli"])
-        for k in range(6, -1, -1):
-            erow(k, eo, eor)
-        to_off(T.eo8[:, :], "eo8", *conv(eslot(0)[0], [eslot(0)[1]], eo, eor))
-        for k in range(14, 7, -1):
-            erow(k, T.eo8[:, :], "eo8")
-        to_off(T.eo64[:, :], "eo64", *conv(eslot(8)[0], [eslot(8)[1]], T.eo8[:, :], "eo8"))
-        for k in range(19, 15, -1):
-            erow(k, T.eo64[:, :], "eo64")
-
-        cur = "s"
-        turn = 0
+            phase("mates")
+            a = spare()
+            act(a, by(slot("fr", 0), R("mo")), ga(C))
+            difference(tab("dfm"), table_of(a), R("fli"))
+        phase("key")
+        cur, k = "key0", 0
         for level, (rad, n) in enumerate(LEVELS):
-            o, orr = htab(level)
-            base, side = cur, "s2"
-            if level:
-                side = "mc%d" % (level % 2)
-                if level in TWIN_HOME:
-                    cp(T[side][:, :], [side], T[cur][:, :], [cur], el(C))
-                else:
-                    sg(T[side][:, :], [side], T[cur][:, :], [cur], el(C))
-            for i in range(rad - 1):
-                d = "m%d" % (turn % 3)
-                turn += 1
-                z = base if i else side
-                tt(T[d][:, :], [d], T[cur][:, :].indirect(o), T[z][:, :], [cur, z, orr], A.max, ga(C))
-                cur = d
-        tt(T.cand[:, :], ["cand", "p5"], T[cur][:, :], T.p5[:, 0:C], [cur], A.is_equal, el(C))
-        for p, (lo, hi) in PARTS.items():
-            tt(T.y0[:, lo:hi], ["y0" + p], T.cand[:, lo:hi], T.key[:, lo:hi], ["cand", "key"], A.mult, el(hi - lo, 2))
-        cur = "y0"
-        turn = 1
-        for level, (rad, n) in enumerate(LEVELS):
-            orr = htab(level)[1]
             base = cur
             for i in range(rad - 1):
-                zz = "z%s%d" % ("ab"[i], level % 2)
+                zz = "key1" if level == 0 else "za%d" % (level % 2) if i == 0 else "zb0"
                 for p, (lo, hi) in PARTS.items():
-                    if level in Z_HOME:
-                        ts(T[zz][:, lo:hi], [zz + p], T[base][:, lo:hi], [base + p], float(n * (i + 1)), A.add, n=hi - lo)
-                    else:
-                        lin(T[zz][:, lo:hi], [zz + p], T[base][:, lo:hi], [base + p], 1.0, n * (i + 1), hi - lo)
-            for i in range(rad - 1):
-                zz = "z%s%d" % ("ab"[i], level % 2)
-                d = "y%d" % (turn % 4)
-                turn += 1
+                    if level:
+                        act(part(zz, p, lo, hi), part(base, p, lo, hi), el(hi - lo), 1.0, float(-n * (i + 1)))
+                d = "y%d" % (k % 4)
+                k += 1
                 for p, (lo, hi) in PARTS.items():
-                    off = T.ho[:, level * TC + lo // 16:level * TC + hi // 16]
-                    tt(T[d][:, lo:hi], [d + p], T[cur][:, :].indirect(off), T[zz][:, lo:hi],
-                       [cur + q for q in PARTS] + [zz + p, orr], A.max, ga(hi - lo))
+                    off = (tabs[level][0][:, lo // 16:hi // 16], tabs[level][1])
+                    win = parts(cur) if level else R(cur)
+                    tt(part(d, p, lo, hi), by(win, off), part(zz, p, lo, hi) if level else R(zz, lo, hi), A.min, ga(hi - lo))
                 cur = d
+        key = parts(cur)
+        phase("line")
+        v = table_of(key, True)
+        ts(tab("ro"), v, col(DOWN_M), A.mult)
+        ts(tab("ki"), v, col(DOWN), A.mult)
+        ts(tab("dj"), tab("ki"), int(M) - 1, A.bitwise_and)
+        sa = "sa%d" % r
+        po, ln, eo = [R(sa, k * TC, (k + 1) * TC, sa + "e" * (k == 2)) for k in range(3)]
+        if TWIN:
+            for p, (lo, hi) in PARTS.items():
+                act(part("twin", p, lo, hi), part(cur, p, lo, hi), el(hi - lo))
+        tt(R("dn"), by(key, fo), parts("twin") if TWIN else key, A.subtract, ga(C))
+        scan(R("st"), R("step"), R("dn"), -1.0 - M - H, A.add, A.add, el(C))
+        tt(slot("pl", 0), by(R("st"), tab("ro")), key, A.subtract, ga(C))
+        act(slot("pl", 1), by(R("dn"), tab("ro")), ga(C), 1.0, 1.0 - H)
+        scan(R("sc2"), (T.cv[:, :], ["cv0", "cv1"]), (T.pl[:, :], ["pl0", "pl1"]), 0.0, A.mult, A.add, el(C))
+        offsets(R(sa, 0, 2 * TC), (T.sc2[:, 15:2 * C:16], ["sc2"]))
+        tt(eo, po, tab("dj"), A.add)
+        send_list(r, "a", [sa, sa + "e"])
+        op("v", ["keyb", sa], ["ord"], lambda po=po: V.tensor_copy(T.ord[:, :].indirect(po[0]), T.keyb[:, :]), 1.2)
+        oo = R("sb%d" % r)
+        ts(oo, table_of(R("ord"), True), col(LESS_M), A.mult, float(C), A.add)
+        send_list(r, "b", oo[1])
+
+        phase("score")
+        mm("p4", T.uk[:, :], T.uks[:, :], ["uk", "uks"], xq[:, :], xs[:, :], xr)
+        out_of(R("s"), "p4")
+        phase("fh")
         for b in range(4):
-            sg(T.fh[:, b * C:(b + 1) * C], ["fh%d" % b, "p%d" % b], T["p%d" % b][:, 0:C], [], el(C))
+            mm("p%d" % b, T.eq[:, 128 * b:128 * b + 128], T.eqs[:, 128 * b:128 * b + 128], ["eq"], xq[:, :], xs[:, :], xr)
+            out_of(slot("fh", b), "p%d" % b)
+        phase("fs")
         for b in range(4):
             mm("p%d" % (4 + b), T.eq[:, 128 * b:128 * b + 128], T.eqs[:, 128 * b:128 * b + 128], ["eq"],
                T["lc%d" % r][:, :], T["ls%d" % r][:, :], ["lc%d" % r])
-            sg(T.fs[:, b * C:(b + 1) * C], ["fs%d" % b, "p%d" % (4 + b)], T["p%d" % (4 + b)][:, 0:C], [], el(C))
+            out_of(slot("fs", b), "p%d" % (4 + b))
 
-        tt(T.km[:, :], ["km"], T[cur][:, :], T.mask[:, :], [cur + p for p in PARTS] + ["mask"], A.mult, el(C, 2))
-        op("v", ["km", "keep"], ["ks"],
-           lambda: V.tensor_tensor_scan(T.ks[:, :], T.keep[:, :], T.km[:, :], 0.0, A.mult, A.add), el(C))
-        cp(T.ki[:, :], ["ki"], T.ks[:, 15:C:16], ["ks"])
-        ts(T.k0[:, :], ["k0"], T.ki[:, :], ["ki"], 7, A.bitwise_and)
-        ts(T.ka[:, :], ["ka"], T.ki[:, :], ["ki"], 9, A.logical_shift_right)
-        ts(T.k1[:, :], ["k1"], T.ki[:, :], ["ki"], 3, A.logical_shift_right, 7, A.bitwise_and)
-        ts(T.x1[:, :], ["x1"], T.k0[:, :], ["k0"], float(C), A.mult, float(C), A.add)
-        ts(T.k2[:, :], ["k2"], T.ki[:, :], ["ki"], 6, A.logical_shift_right, 7, A.bitwise_and)
-        tt(T.w1[:, :], ["w1"], T.x1[:, :], T.ka[:, :], ["x1", "ka"], A.subtract)
-        ts(T.x2[:, :], ["x2"], T.k1[:, :], ["k1"], float(C), A.mult, float(C // 2), A.add)
-        ts(T.x3[:, :], ["x3"], T.k2[:, :], ["k2"], float(C), A.mult, float(C // 2 - 3 * C), A.add)
-        v, vr = conv(T.er[:, 0:8 * C], ["er%d" % k for k in range(8)], T.w1[:, :], "w1")
-        tt(T.w2[:, :], ["w2"], T.x2[:, :], v, ["x2", vr], A.add)
-        v, vr = conv(T.er[:, 8 * C:16 * C], ["er%d" % k for k in range(8, 16)], T.w2[:, :], "w2")
-        tt(T.w3[:, :], ["w3"], T.x3[:, :], v, ["x3", vr], A.add)
-        to_off(T.to[:, :], "to", *conv(T.er[:, 16 * C:21 * C], ["er%d" % k for k in range(16, 21)], T.w3[:, :], "w3"))
+        phase("lead")
+        pick(R("so"), R("s"), oo)
+        act(R("fla", 1, C + 1), by(R("dn"), oo), ga(C), -BIG, -BIG)
+        fla = (T.fla[:, 0:C], ["fla", "fla0"])
+        act(R("flb", 0, C), fla, el(C), 1.0, -1.0)
+        scan(R("top"), fla, R("so"), -BIG, A.add, A.max, el(C))
+        tt(R("cand"), by(R("top"), eo), R("s"), A.is_equal, ga(C))
+        tt(R("ck"), by(R("cand"), oo), R("ord"), A.mult, ga(C))
+        scan(R("run"), R("flb", 0, C), R("ck"), 0.0, A.add, A.max, el(C))
+        pick(R("lead"), R("run"), eo)
+        v = table_of(R("lead"), True)
+        ts(tab("lo"), v, col(LESS_M), A.mult, float(C), A.add)
+        ts(tab("kl"), v, col(LESS), A.mult, M * C, A.add)
+        tt(tab("x0i"), tab("kl"), tab("dj"), A.subtract)
+        tt(tab("x1i"), tab("x0i"), ln, A.add)
+        ts(tab("a0i", 2), tab("x0i", 2), int(M) - 1, A.bitwise_and)
+        tt(tab("i"), tab("a0i"), tab("a1i"), A.min)
 
-        for b in range(4):
-            sg(T.gt[:, b * C:(b + 1) * C], ["gt%d" % b], T.fs[:, b * C:(b + 1) * C].indirect(T.to[:, :]),
-               ["fs%d" % b, "to"])
-        nfo, nfr = T["fo%d" % (r + 1)], "fo%d" % (r + 1)
-        cp(T.mine[:, :], ["mine"], T.s[:, :].indirect(T.to[:, :]), ["s", "to"], ga(C))
-        tt(T.mhi[:, :], ["mhi"], T.mine[:, :].indirect(T.hio[:, :]), T.mbig[:, :], ["mine", "hio", "mbig"], A.min, ga(C))
-        mk, mr, sc, sr = turn_mk()
-        tt(mk, [mr], T.mine[:, :].indirect(T.loo[:, :]), T.mhi[:, :], ["mine", "mhi", "loo"], A.is_lt, ga(C))
-        v, vr = scan(mk, mr, sc, sr)
-        tt(T.ta[:, :], ["ta"], v, T.dfm[:, :], [vr, "dfm"], A.mult)
-        tt(T.tb[:, :], ["tb"], v, T.dmt[:, :], [vr, "dmt"], A.mult)
-        tt(nfo[:, :], [nfr], T.ta[:, :], T.ff[:, :], ["ta", "ff"], A.add)
+        phase("far")
+        la, oe = "la%d" % r, R("lb%d" % r)
+        for k in (1, 0, 2):
+            act(slot("pr", k), by(jc, R(la, k * TC, (k + 1) * TC)), ga(C))
+        act(slot("oer", 0), by(jc, oe), ga(C))
+        act(slot("oer", 1), slot("oer", 0), el(C))
+        act(slot("both", 0), by(R("s"), oe), ga(C))
+        act(slot("both", 1), slot("both", 0), el(C), -1.0)
+        phase("walk")
+        for k, name, home in ((1, "lnf", False), (0, "pef", True), (2, "enf", False)):
+            a = spare()
+            if home:
+                cp(a, by(slot("pr", k), tab("lo")), ga(C))
+            else:
+                act(a, by(slot("pr", k), tab("lo")), ga(C))
+            lin(tab(name), table_of(a), col(DOWN), float(H))
+        op("v", ["lnf"], ["rl"], lambda: V.reciprocal(tab("rl")[0], tab("lnf")[0]), 0.35)
+        tt(tab("w0"), tab("pef"), tab("i"), A.add)
+        tt(tab("zz"), tab("enf"), tab("w0"), A.subtract)
+        tt(tab("t"), tab("zz"), tab("rl"), A.mult)
+        ts(tab("q"), tab("t"), -0.499, A.add)
+        tt(tab("m"), tab("q"), tab("lnf"), A.mult)
+        tt(tab("w0a"), tab("w0"), tab("ca"), A.add)
+        tt(tab("wa"), tab("w0a"), tab("m"), A.add)
+
+        phase("splice")
+        both = (T.both[:, :], ["both0", "both1"])
+        act(R("nms"), by(both, tab("wa")), ga(C), -1.0)
+        cp(R("ms"), by(both, tab("wa")), ga(C))
+        tt(R("sw"), by(R("nms"), R("mo")), R("ms"), A.is_gt, ga(C))
+        tt(tab("ta"), table_of(R("sw")), tab("dfm"), A.mult)
+        tt(nfo, tab("ta"), fo, A.add)
         if not last:
-            tt(T.ff[:, :], ["ff"], T.ta[:, :], T.ff[:, :], ["ta"], A.add)
-            send_list(r + 1)
-            ts(T.tc[:, :], ["tc"], T.ta[:, :], ["ta"], -2.0, A.mult)
-            tt(T.dfm[:, :], ["dfm"], T.tc[:, :], T.dfm[:, :], ["tc"], A.add)
-        tt(T.so[:, :], ["so"], T.tb[:, :], T.jt[:, :], ["tb", "jt"], A.add)
-        sg(T.srow[:, :], ["srow"], T.jc[:, :].indirect(T.so[:, :]), ["jc", "so"])
-        o, orr = htab(0)
+            phase("keep")
+            lin(tab("tc"), tab("ta"), col(LESS_2), 0.0)
+            tt(tab("dfm"), tab("tc"), tab("dfm"), A.add)
+        phase("tee", "2" if last else "")
+        a = spare()
+        act(a, by((T.oer[:, :], ["oer0", "oer1"]), tab("wa")), ga(C))
+        offsets(tab("to"), table_of(a))
+        phase("back")
+        a = spare()
+        act(a, by(R("sw"), ho), ga(C))
+        tt(tab("th"), table_of(a), tab("dh"), A.mult)
+        tt(nho, tab("th"), ho, A.add)
+        if not last:
+            phase("keep")
+            lin(tab("td"), tab("th"), col(LESS_2), 0.0)
+            tt(tab("dh"), tab("td"), tab("dh"), A.add)
+
+        phase("z")
         for b in range(4):
-            tt(T.z[:, b:4 * C:4], ["z%d" % b], T.fh[:, b * C:(b + 1) * C].indirect(nfo[:, :]),
-               T.gt[:, b * C:(b + 1) * C], ["fh%d" % b, "gt%d" % b, nfr], A.add, ga(C))
+            act(slot("gt", b), by(slot("fs", b), tab("to")), ga(C))
+            tt((T.z[:, b:4 * C:4], ["z%d" % b]), by(slot("fh", b), nfo), slot("gt", b), A.add, ga(C))
+        phase("zq")
         quant(T.zq[:, :], T.zs[:, :], ["z0", "z1", "z2", "z3"], ["zq"], T.z[:, :], 4 * C)
-        to_off(o, orr, *conv(T.srow[:, :], ["srow"] + AFTER, o, orr))
+        phase("rb")
         for b in (2, 3, 0, 1):
             bank = "p%d" % (4 + b)
             mm(bank, T.wq[:, 128 * b:128 * b + 128], T.wsp[:, 128 * b:128 * b + 128], ["wq", "wsp"],
                T.zq[:, :], T.zs[:, :], ["zq"])
-            if b in R_HOME:
-                ts(T.rb[:, b * C:(b + 1) * C], ["rb%d" % b, bank], T[bank][:, 0:C], [], 2.0 ** -6, A.mult, n=C)
+            out_of(slot("rb", b), bank, 2.0 ** -6, b in R_HOME)
+        phase("x")
+        for b in P_FAR:
+            act(slot("gp", b), by(slot("rb", b), nho), ga(C))
+        for b in range(4):
+            out = (T.xt[:, b:4 * C:4], ["xt%d" % b])
+            if b in P_FAR:
+                tt((out[0], out[1] + ["p%d" % b]), slot("gp", b), (T["p%d" % b][:, 0:C], []), A.add, el(C))
             else:
-                sg(T.rb[:, b * C:(b + 1) * C], ["rb%d" % b, bank], T[bank][:, 0:C], [], el(C), 2.0 ** -6)
-        for b in P_FAR:
-            sg(T.gp[:, b * C:(b + 1) * C], ["gp%d" % b], T.rb[:, b * C:(b + 1) * C].indirect(o), ["rb%d" % b, orr])
-        for b in [b for b in range(4) if b not in P_FAR]:
-            tt(T.xt[:, b:4 * C:4], ["xt%d" % b], T.rb[:, b * C:(b + 1) * C].indirect(o), T.fh[:, b * C:(b + 1) * C],
-               ["rb%d" % b, "fh%d" % b, orr], A.add, ga(C))
-        for b in P_FAR:
-            tt(T.xt[:, b:4 * C:4], ["xt%d" % b, "p%d" % b], T.gp[:, b * C:(b + 1) * C], T["p%d" % b][:, 0:C],
-               ["gp%d" % b], A.add, el(C))
+                tt(out, by(slot("rb", b), nho), slot("fh", b), A.add, ga(C))
+        phase("xq")
         quant(T["xq%d" % (r + 1)][:, :], T["xs%d" % (r + 1)][:, :], ["xt0", "xt1", "xt2", "xt3"], ["xq%d" % (r + 1)],
               T.xt[:, :], 4 * C)
         if not last:
             send_codes(r + 1)
         else:
-            sg(T.nlr[:, :], ["nlr"], T.jf[:, :].indirect(nfo[:, :]), ["jf", nfr])
+            act(R("nlr"), by(jf, nfo), ga(C))
 
+    phase("out")
     quant(T.vq[:, :], T.vqs[:, :], ["vb"], ["vq"], T.vb[:, :], 512)
     mm("p4", T.vq[:, :], T.vqs[:, :], ["vq"], T.xq3[:, :], T.xs3[:, :], ["xq3"])
-    sg(T.yb[:, :], ["yb", "p4"], T.p4[:, 0:C], [], el(C))
+    out_of(R("yb"), "p4")
 
     def store(out, in_, res, tail=2.0):
         op("y", [res], [], lambda: g.sync.dma_start(out=out, in_=in_), 0.1, "lout", 16, tail)
@@ -536,13 +630,14 @@ def relay_program(g, core, T, topo):
     for r in range(3):
         for i, src in enumerate(T.cores):
             dst = T.cores[i ^ MASKS[r]]
-            if relay_of(src, dst, topo) != core:
-                continue
-            g.wait_ge(T.sem["al%d" % r], NL)
-            n += send(g, T, topo, core, dst, T["lo%d" % r][:, :], T["lo%d" % r][:, :], "al%d" % r, NL)
-            g.wait_ge(T.sem["ac%d" % r], 2 * NE)
-            n += send(g, T, topo, core, dst, T["lc%d" % r][:, :].bitcast(dt.uint8),
-                      T["lc%d" % r][:, :].bitcast(dt.uint8), "ac%d" % r, NE)
-            n += send(g, T, topo, core, dst, T["ls%d" % r][:, :], T["ls%d" % r][:, :], "ac%d" % r, NE)
+            if relay_of(src, dst, topo, 0) == core:
+                g.wait_ge(T.sem["ac%d" % r], 2 * NE)
+                n += send(g, T, topo, core, dst, T["lc%d" % r][:, :].bitcast(dt.uint8),
+                          T["lc%d" % r][:, :].bitcast(dt.uint8), "ac%d" % r, NE)
+                n += send(g, T, topo, core, dst, T["ls%d" % r][:, :], T["ls%d" % r][:, :], "ac%d" % r, NE)
+            for k in "ab" if relay_of(src, dst, topo, 1) == core else "":
+                g.wait_ge(T.sem["a%s%d" % (k, r)], NL)
+                name = "l%s%d" % (k, r)
+                n += send(g, T, topo, core, dst, T[name][:, :], T[name][:, :], "a%s%d" % (k, r), NL)
     if n:
         g.wait_ge(T.sem.sent, n)

@@ -1,9 +1,9 @@
+import math
 from concourse.mybir import dt, AluOpType, ActivationFunctionType
 
 A = AluOpType
 COPY = ActivationFunctionType.Copy
 IDENT = ActivationFunctionType.Identity
-SIGN = ActivationFunctionType.Sign
 C = 288
 TC = C // 16
 H = C // 2
@@ -12,21 +12,20 @@ UP = 2.0 ** 40
 BIG = 2.0 ** 72
 MASKS = [4, 1, 2]
 LEVELS = [(2, 1), (2, 2), (2, 4), (2, 8), (2, 16), (3, 32), (3, 96)]
-SPLIT = {"a": (0, 160), "b": (160, C)}
+HALVES = {"a": (0, 160), "b": (160, C)}
 WHOLE = {"ab": (0, C)}
-SPLIT_IN = (0,)
-R_HOME = ()
-P_FAR = (2, 3)
-TWIN = True
-ON_S = ()
-SMALL_S = ("enf", "pef", "tc", "td")
-WAKE, GATHER, EL = 0.1, 1.62e-3, 1.04e-3
-LOOK, EDGE = 1.0, 1.0
-HASTE = {'x0v': 11.5, '+zv': -0.6, 'zs': 6.0, '+score0': 3.6, 'xs2': 1.0, 'fss0': -6.5, '+x0v': 3.7, 'xv': -7.5, '+matess': 1.7, 'leadv0': -12, 'zv': -7.5, '+xs2': -3.8, '+keys': 1.1, 'linev': -7.5, 'fss': -12, 'powv': 6.0, '+matesv': 0.6, '+backs': 2.4, 'backv': 11.5, '+walks0': -1.6, '+fars': 1.8, 'walks': 10.5, 'tees2': -4.5, '+rbs2': -2.0, 'zs2': 12, '+xv2': -4.9, '+backv': 3.6, 'pows': 4.0, '+score': 0.9, '+walks': 2.2, '+linev0': 1.4, '+fss0': -2.1, '+': -2.9, 'scores0': -7.5, '+splicev0': -0.5, 'matesv': -2.0, '+xs': -0.7, 'keys': -5.5, '+splicev': -4.4, 'keyv': -5.5, '+line': 1.8, '+xqv': -2.8, '+keys0': 5.0, '+fars0': -0.3, '+powv': -3.2, '+line0': 3.4, '+scores0': 2.6, '+walkv0': 1.5, '+zv2': -4.8, '+leadv0': -5.0, '+keyv': 0.6}
-SPAN = [0.0]
-LIST_US, CODE_US = 3.0, 5.0
+R_HOME = [(), (), ()]
+P_FAR = [(3,), (3,), ()]
+SMALL_S = ("pef", "tc", "td")
 NE, NL = 8, 8
-NB, NF = 16, 3
+NB, NF = 16, 4
+WAKE, GATHER, SCATTER, EL = 0.15, 1.43e-3, 3.6e-3, 0.955e-3
+LIST_US, CODE_US, HOP_US, FIRST_US = 0.55, 2.9, 2.0, 1.5
+AT = dict(x0=4.0, u=4.2, eq=2.7, mates=5.4, dfm=12.2, h0=16.6, level=1.1, gt=1.7, z=2.5, rb=5.2, x=5.5, fh=13.7, fs=18.7,
+          keep=15.6, far=16.4)
+TRIES = 20000
+SPAN = [0.0]
+FOUND = {}
 
 SCRATCH = {}
 
@@ -41,11 +40,9 @@ _b("x0 xt z fh fs gt", 4 * C, "bfloat16")
 _b("rb gp", 4 * C, "float32")
 _b("xq0 xq1 xq2 xq3 lc0 lc1 lc2 zq", C, CODE)
 _b("xs0 xs1 xs2 xs3 ls0 ls1 ls2 zs", C, "uint8")
-_b("fo0 fo1 fo2 fo3 sb0 sb1 sb2 lb0 lb1 lb2 ho0 ho1 mo", TC, "uint16")
-_b("sa0 sa1 sa2 la0 la1 la2", 3 * TC, "uint16")
-_b("ft", 6 * TC, "uint16")
-_b("tu", 4 * TC, "uint16")
-_b("rep", TC, "uint16")
+_b("fo0 fo1 fo2 fo3 sb0 sb1 sb2 lb0 lb1 lb2 sd0 sd1 sd2 ld0 ld1 ld2 ho0 ho1 mo rep", TC, "uint16")
+_b("sa0 sa1 sa2 la0 la1 la2", 2 * TC, "uint16")
+_b("ft tu", 6 * TC, "uint16")
 _b("wq eq", 512, CODE)
 _b("wsp eqs", 512, "uint8")
 _b("uq uk vq", 128, CODE)
@@ -53,10 +50,10 @@ _b("uqs uks vqs", 128, "uint8")
 _b("et", 2048, "bfloat16")
 _b("ub vb", 512, "bfloat16")
 _b("fli mli", TC, "int32")
-_b("ti", 8 * TC, "int32")
-_b("tf", 22 * TC, "float32")
+_b("ti", 9 * TC, "int32")
+_b("tf", 20 * TC, "float32")
 _b("key0 key1 keyb step s y0 y1 y2 y3 za0 za1 zb0 twin dn st ord so top ck run lead ms nms yb nlr", C, "float32")
-_b("jf fla flb", C + 16, "float32")
+_b("fla flb", C + 16, "float32")
 _b("jc", C + 16, "bfloat16")
 _b("cand sw", C, "bfloat16")
 _b("cv pl oer sc2", 2 * C, "bfloat16")
@@ -66,20 +63,20 @@ _b("pr", 3 * C, "bfloat16")
 _b("row sc", NB * C, "bfloat16")
 _b("scf", NF * C, "float32")
 _b("uo", 8, "uint16")
-_b("c16", TC, "float32")
+_b("j32", 32, "float32")
 _b("cva cvb", 16, "float32")
 _b("cv16", 16, "bfloat16")
 _b("pi p16i", 2, "int32")
-_b("pn p16 p17", 2, "float32")
+_b("p16 p17", 2, "float32")
 _b("col", 8, "float32")
-_b("diag", 256, "float32")
+_b("half", 128, "bfloat16")
 _b("p0 p1 p2 p3 p4 p5 p6 p7", 512, "float32", "psum")
-TU = "ro lo wa to".split()
-TI = "ki dj kl q x0i x1i a0i a1i".split()
-TF = "jt ca dfm dh i lnf rl enf pef zz t m w0 w0a ta tc th td u0 u1".split()
+TU = "ro lo wa to eo bo".split()
+TI = "ki dj dd kl q x0i x1i a0i a1i".split()
+TF = "jt ca dfm dh i lnf rl def pef zz t m w0 w0a ta tc th td u0 u1".split()
 
 SEMAPHORES = ["cv", "cs", "ct", "cp", "lx", "lu", "lv", "lf", "lm", "lw", "lq", "lout", "sent"]
-SEMAPHORES += [k + str(r) for k in ("ac", "aa", "ab") for r in range(3)]
+SEMAPHORES += [k + str(r) for k in ("ac", "ad", "aa", "ab") for r in range(3)]
 
 
 def relay_of(src, dst, topo, k):
@@ -101,63 +98,95 @@ def send(g, T, topo, src, dst, out_ap, in_ap, sem, count):
     return len(e)
 
 
+def place(cost, queue, before, after, rank):
+    n = len(cost)
+    left = [len(b) for b in before]
+    ready = [0.0] * n
+    start = [0.0] * n
+    busy = {}
+    free = [(rank[i], i) for i in range(n) if not left[i]]
+    while free:
+        top = min(free)
+        free.remove(top)
+        i = top[1]
+        t, d = ready[i], cost[i]
+        if queue[i] is not None:
+            line = busy.setdefault(queue[i], [])
+            k = len(line)
+            while k and line[k - 1][1] > t:
+                k -= 1
+            while k < len(line) and line[k][0] < t + d - 1e-9:
+                t = max(t, line[k][1])
+                k += 1
+            line.insert(k, (t, t + d))
+        start[i] = t
+        for u, lag in after[i]:
+            if t + d + lag > ready[u]:
+                ready[u] = t + d + lag
+            left[u] -= 1
+            if not left[u]:
+                free.append((rank[u], u))
+    return start
+
+
 def order(ops):
     n = len(ops)
-    users = [[] for _ in range(n)]
-    for i, o in enumerate(ops):
-        for d in o["deps"]:
-            users[d].append(i)
-    far = [0.0] * n
-    for i in range(n - 1, -1, -1):
-        o = ops[i]
-        far[i] = o["c"] + o["tail"] + HASTE.get("+" + o["kind"], 0.0) + max([far[u] + WAKE for u in users[i]] or [0.0])
-    far = [far[i] + HASTE.get(ops[i]["kind"], 0.0) for i in range(n)]
-    left = [len(o["deps"]) for o in ops]
-    ready = [0.0] * n
-    open_ = {}
-    free = {}
-    out = []
-    span = [0.0]
+    sign = tuple((o["q"], o["c"], o["tail"], tuple(sorted(o["deps"]))) for o in ops)
+    if sign not in FOUND:
+        fore = [[(d, ops[d]["tail"] + WAKE) for d in sorted(o["deps"])] for o in ops]
+        fore.append([(i, ops[i]["tail"]) for i in range(n)])
+        back = [[] for _ in fore]
+        for i, b in enumerate(fore):
+            for d, lag in b:
+                back[d].append((i, lag))
+        cost, queue = [o["c"] for o in ops] + [0.0], [o["q"] for o in ops] + [None]
+        seed = [4]
 
-    def finish(i, t):
-        span[0] = max(span[0], t)
-        for u in users[i]:
-            left[u] -= 1
-            ready[u] = max(ready[u], t + WAKE)
-            if left[u] == 0:
-                release(u)
+        def draw():
+            seed[0] = (seed[0] * 1103515245 + 12345) % 2147483648
+            return (seed[0] >> 8) / 8388608.0
 
-    def release(u):
-        if ops[u]["q"] is None:
-            out.append(u)
-            finish(u, ready[u] + ops[u]["tail"])
-        else:
-            open_.setdefault(ops[u]["q"], []).append(u)
+        def one(of):
+            return of[int(draw() * len(of))]
 
-    for i in range(n):
-        if not ops[i]["deps"]:
-            release(i)
-    while any(open_.values()):
-        pick = None
-        for q, cand in open_.items():
-            if not cand:
-                continue
-            t = max(free.get(q, 0.0), min(ready[i] for i in cand))
-            b = max((i for i in cand if ready[i] <= t + 1e-9), key=lambda i: far[i])
-            stop = t + ops[b]["c"]
-            for i in cand:
-                if far[i] > far[b] + EDGE and ready[i] < stop and ready[i] - t < LOOK * (stop - ready[i]):
-                    b = i
-            s = max(t, ready[b])
-            if pick is None or s < pick[0]:
-                pick = (s, q, b)
-        s, q, b = pick
-        open_[q].remove(b)
-        free[q] = s + ops[b]["c"]
-        out.append(b)
-        finish(b, free[q] + ops[b]["tail"])
-    SPAN[0] = span[0]
-    return out
+        def worth(start):
+            return start[n] + 2e-6 * sum(start)
+
+        now = best = place(cost, queue, fore, back, [o["at"] for o in ops] + [1e9])
+        for k in range(TRIES):
+            rank = list(now)
+            how = draw()
+            if how < 0.35:
+                i, s = int(draw() * n), one((-4, -2, -1, -0.5, 0.5, 1, 2, 4))
+                near, w = [i], one((1, 2, 4))
+                for u in near:
+                    for d, lag in (fore if s < 0 else back)[u]:
+                        if d not in near and abs(now[d] - now[i]) < w:
+                            near.append(d)
+                for u in near:
+                    rank[u] += s
+            elif how < 0.7:
+                for _ in range(one((1, 2, 5))):
+                    rank[int(draw() * n)] += one((-4, -2, -1, -0.5, -0.2, 0.2, 0.5, 1, 2, 4))
+            else:
+                a, w, s = draw() * now[n], one((1, 2, 4)), one((0.2, 0.6, 1.2))
+                for i in range(n):
+                    if a <= rank[i] < a + w:
+                        rank[i] += s * (draw() - 0.5)
+            new = place(cost, queue, fore, back, rank)
+            if draw() < 0.03:
+                late = place(cost, queue, back, fore, [-(new[i] + cost[i]) for i in range(n + 1)])
+                early = place(cost, queue, fore, back, [-(late[i] + cost[i]) for i in range(n + 1)])
+                if early[n] <= new[n]:
+                    new = early
+            heat = 0.15 * (1.0 - k / TRIES) + 0.003
+            if worth(new) <= worth(now) or draw() < math.exp((worth(now) - worth(new)) / heat):
+                now = new
+                if worth(now) < worth(best):
+                    best = now
+        SPAN[0] = best[n]
+        FOUND[sign] = sorted(range(n), key=lambda i: (best[i], i))
+    return FOUND[sign]
 
 
 def rank_program(g, core, T, topo):
@@ -169,13 +198,13 @@ def rank_program(g, core, T, topo):
     own = {"v": "cv", "s": "cs", "t": "ct", "p": "cp"}
     V, S, P = g.vector, g.scalar, g.tensor
     ops = []
-    stage = ["const", ""]
+    clock = [0.0, 0.0]
     acc = {}
 
-    def phase(name, mark=None):
-        stage[0] = name
-        if mark is not None:
-            stage[1] = mark
+    def at(t, base=None):
+        clock[1] = t
+        if base is not None:
+            clock[0] = base
 
     def op(qn, rd, wr, fn, cost, sem=None, inc=1, tail=0.0, ev=None):
         deps = set()
@@ -194,15 +223,14 @@ def rank_program(g, core, T, topo):
         for r in wr:
             acc[r] = [me, []]
         deps.discard(me)
-        kind = stage[0] + (qn if qn in ("s", "v") else "") + stage[1] if qn else ""
-        ops.append(dict(q=qn, c=cost, tail=tail, kind=kind, deps=deps, fn=fn, sem=sem or own.get(qn), inc=inc, ev=ev))
-        return me
+        plan = max([clock[0] + clock[1]] + [ops[d]["at"] + ops[d]["c"] + ops[d]["tail"] + WAKE for d in deps])
+        ops.append(dict(q=qn, c=cost, tail=tail, at=plan, deps=deps, fn=fn, sem=sem or own.get(qn), inc=inc, ev=ev))
 
     def emit():
         total, know = {}, {k: {} for k in queues}
         for i in order(ops):
             o = ops[i]
-            if o["q"] is None:
+            if o["fn"] is None:
                 o["knows"] = {}
                 continue
             k = know[o["q"]]
@@ -244,8 +272,8 @@ def rank_program(g, core, T, topo):
             return T[name][:, :], [name]
         return T[name][:, lo:hi], [tag or name]
 
-    def slot(name, k, n=C):
-        return T[name][:, k * n:(k + 1) * n], ["%s%d" % (name, k)]
+    def slot(name, k, n=C, lo=0, hi=None):
+        return T[name][:, k * n + lo:k * n + (hi or n)], ["%s%d" % (name, k)]
 
     def tab(name, n=1):
         for buf, names in (("tu", TU), ("ti", TI), ("tf", TF)):
@@ -274,25 +302,19 @@ def rank_program(g, core, T, topo):
     def cp(out, a, c=None):
         op("v", a[1], out[1], lambda: V.tensor_copy(out[0], a[0]), el(TC) if c is None else c)
 
-    def act(out, a, c, scale=1.0, bias=0.0, func=IDENT):
+    def act(out, a, c, scale=1.0, bias=0.0):
         scale, bias = num(scale), num(bias)
-        if func is IDENT and not scale[1] and not bias[1] and scale[0] == 1.0 and bias[0] == 0.0:
+        if not scale[1] and not bias[1] and scale[0] == 1.0 and bias[0] == 0.0:
             op("s", a[1], out[1], lambda: S.activation(out[0], a[0], COPY), c)
         else:
             op("s", a[1] + scale[1] + bias[1], out[1],
-               lambda: S.activation(out[0], a[0], func, bias=bias[0], scale=scale[0]), c)
+               lambda: S.activation(out[0], a[0], IDENT, bias=bias[0], scale=scale[0]), c)
 
     def lin(out, a, scale, bias):
         if out[1][0] in SMALL_S:
             act(out, a, el(TC), scale, bias)
         else:
             ts(out, a, scale, A.mult, bias, A.add)
-
-    def pick(out, win, off):
-        if out[1][0] in ON_S:
-            act(out, by(win, off), ga(C))
-        else:
-            cp(out, by(win, off), ga(C))
 
     def col(k):
         return T.col[:, k:k + 1], ["col%d" % k]
@@ -320,25 +342,30 @@ def rank_program(g, core, T, topo):
     def spare():
         return slot("row", fresh("row", NB))
 
-    def mm(bank, st, sts, sr, mv, mvs, mr):
-        op("t", sr + mr, [bank], lambda: P.matmul_mx(T[bank][:, 0:C], st, sts, mv, mvs, True, True), 0.38)
+    def mm(bank, st, sts, sr, mv, mvs, mr, n=C):
+        op("t", sr + mr, [bank], lambda: P.matmul_mx(T[bank][:, 0:n], st, sts, mv, mvs, True, True), (n + 16) * 1.25e-3)
 
     def quant(q, s, rd, wr, src, n):
-        op("v", rd, wr, lambda: V.quantize_mx(q, s, src), 0.015 + 0.28e-3 * n)
+        op("v", rd, wr, lambda: V.quantize_mx(q, s, src), 0.015 + 0.26e-3 * n)
 
-    def load(qn, out, in_, res, sem, tail=2.0):
+    def load(qn, out, in_, res, sem, tail=2.2):
         op(qn, [], [res], lambda: queues[qn].dma_start(out=out, in_=in_), 0.1, sem, 16, tail)
 
-    def out_of(out, bank, scale=1.0, home=False):
-        o, a = (out[0], out[1] + [bank]), (T[bank][:, 0:C], [])
+    def store(qn, out, in_, res, us=0.1):
+        tag = "store%d" % len(ops)
+        op(qn, res, [tag], lambda: queues[qn].dma_start(out=out, in_=in_), 0.1, "lout", 16)
+        op("d", [tag], [], None, us, None, 0, HOP_US)
+
+    def out_of(out, bank, scale=1.0, home=False, n=C):
+        o, a = (out[0], out[1] + [bank]), (T[bank][:, 0:n], [])
         if home:
-            ts(o, a, scale, A.mult, c=el(C))
+            ts(o, a, scale, A.mult, c=el(n))
         else:
-            act(o, a, el(C), scale)
+            act(o, a, el(n), scale)
 
     sends = [0]
 
-    def to_partner(r, bufs, sem, count, land, tail, lane):
+    def to_partner(r, bufs, sem, count, land, us, lane):
         dst = T.cores[rank ^ MASKS[r]]
         via = relay_of(core, dst, topo, lane)
         hop = dst if via is None else via
@@ -347,9 +374,13 @@ def rank_program(g, core, T, topo):
             sends[0] += send(g, T, topo, core, hop, o, i, sem, count)
 
         for o, i, res in bufs:
-            op("p", res, ["out" + sem], lambda o=o, i=i: go(o, i), 0.3)
+            op("p", res, ["out" + sem, "lane%d" % lane], lambda o=o, i=i: go(o, i), 0.3)
             ops[-1]["sem"] = None
-        op(None, ["out" + sem], [land], None, 0.0, None, 0, tail if via is None else 2 * tail, (sem, count * len(bufs)))
+        op("d", ["out" + sem], ["way" + sem], None, us, None, 0, HOP_US)
+        if via is not None:
+            us += 0.3 * len(bufs) + FIRST_US * (sem[1] in "cd")
+            op("r%d" % lane, ["way" + sem], ["way" + sem, "hop%d" % lane], None, us, None, 0, HOP_US)
+        op(None, ["way" + sem], [land], None, 0.0, None, 0, 0.0, (sem, count * len(bufs)))
 
     def send_list(r, k, res):
         a, b = "l%s%d" % (k, r), "s%s%d" % (k, r)
@@ -360,65 +391,63 @@ def rank_program(g, core, T, topo):
                        (T["ls%d" % r][:, :], T["xs%d" % r][:, :], ["xq%d" % r])], "ac%d" % r, NE, "lc%d" % r, CODE_US, 0)
 
     load("y", T.fli[:, :], T.fl[:, :], "fli", "lf")
-    load("s", T.x0[:, :], T.x[:, :], "x0", "lx", 3.0)
+    load("s", T.x0[:, :], T.x[:, :], "x0", "lx", 3.5)
     load("y", T.mli[:, :], T.ml[:, :], "mli", "lm")
-    load("y", T.ub[:, :], T.u[:, :], "ub", "lu")
-    load("y", T.wq[:, :].bitcast(dt.uint8), T.wc[:, :], "wq", "lw")
+    load("y", T.ub[:, :], T.u[:, :], "ub", "lu", 2.9)
+    load("y", T.wq[:, :].bitcast(dt.uint8), T.wc[:, :], "wq", "lw", 3.5)
     load("y", T.wsp[:, :], T.ws[:, :], "wsp", "lq")
-    load("y", T.vb[:, :], T.v[:, :], "vb", "lv")
+    load("y", T.vb[:, :], T.v[:, :], "vb", "lv", 2.9)
 
-    def iota(name, pattern, mult, n, flag=True):
+    def iota(name, pattern, base, mult, n, flag=True):
         if flag:
-            op("p", [], [name], lambda: g.iota(T[name][:, :], pattern, 0, mult, allow_small_or_imprecise_dtypes=True),
-               0.16 + 2 * n * EL)
+            op("p", [], [name], lambda: g.iota(T[name][:, :], pattern, base, mult, allow_small_or_imprecise_dtypes=True),
+               0.15 + 2 * n * EL)
         else:
-            op("p", [], [name], lambda: g.iota(T[name][:, :], pattern, 0, mult), 0.16 + 2 * n * EL)
+            op("p", [], [name], lambda: g.iota(T[name][:, :], pattern, base, mult), 0.15 + 2 * n * EL)
 
-    iota("pi", [[0, 2]], 1, 2, False)
-    iota("jf", [[1, C + 16]], 0, C + 16)
-    iota("c16", [[16, TC]], 0, TC)
-    jf, jc = R("jf", 0, C), R("jc")
+    iota("pi", [[0, 2]], 0, 1, 2, False)
+    iota("j32", [[1, 32]], 0, 0, 32)
+    iota("jc", [[1, C + 16]], -H, 0, C + 16)
+    jc = R("jc")
+    act(R("key0"), R("jc", 0, C), el(C), M, M * H + C - 1.0)
+    act(R("key1"), R("jc", 0, C), el(C), M, M * H + C - 2.0)
     p16 = (T.p16[:, 0:1], ["p16"])
     ts(R("p16i"), R("pi"), 15, A.bitwise_and)
     cp(R("p16"), R("p16i"))
     ts(R("p17"), R("p16i"), 1.0, A.add)
-    act(jc, R("jf"), el(C), 1.0, float(-H))
-    act(R("key0"), jf, el(C), M, C - 1.0)
-    act(R("key1"), jf, el(C), M, C - 2.0)
-    act(R("keyb"), jf, el(C), -M, M * C)
-    ts(R("cva"), R("jf", 0, 16), p16, A.not_equal)
-    ts(R("cvb"), R("jf", 0, 16), (T.p17[:, 0:1], ["p17"]), A.is_equal, UP, A.mult)
+    ts(R("cva"), R("j32", 0, 16), p16, A.not_equal)
+    ts(R("cvb"), R("j32", 0, 16), (T.p17[:, 0:1], ["p17"]), A.is_equal, UP, A.mult)
     tt(R("cv16"), R("cva"), R("cvb"), A.max)
-    ts(R("rep"), R("jf", 0, TC), 0.0, A.mult, p16, A.add)
+    ts(R("rep"), R("j32", 0, TC), 0.0, A.mult, p16, A.add)
     act(slot("cv", 0), by(R("cv16"), R("rep")), ga(C))
-    act(slot("cv", 1), slot("cv", 0), el(C))
     ts(col(DOWN), p16, 15.0, A.is_equal, 1.0 / UP, A.max)
     for k, f in ((DOWN_M, 1.0 / M), (LESS_M, -1.0 / M), (LESS, -1.0), (LESS_2, -2.0)):
         act(col(k), col(DOWN), el(1), f)
-    act(R("step"), jf, el(C), 0.0, M + 1.0)
-    act(R("fla", 0, 1, "fla0"), R("jf", 0, 1), el(1))
-
-    phase("first")
+    act(R("fla", 0, 1, "fla0"), R("j32", 0, 1), el(1))
     cp(R("fo0"), R("fli"))
-    phase("x0")
+    op("v", [], ["et"], lambda: V.memset(T.et[:, :], 0.0), el(2048, 0.5))
+    op("v", [], ["half"], lambda: V.memset(T.half[:, :], 0.5), el(64))
+    at(1.0)
+    for b in range(4):
+        op("p", ["half", "et"], ["et%d" % b], lambda b=b: g.affine_select(
+            T.et[:, 512 * b + b:512 * b + 512:4], T.half[:, :], [[-1, 128]], A.is_equal, 0.0, 0, 1), 0.2 + 256 * EL)
+    at(AT["eq"])
+    quant(T.eq[:, :], T.eqs[:, :], ["et", "et0", "et1", "et2", "et3"], ["eq"], T.et[:, :], 2048)
+    iota("step", [[0, C]], int(M) + 1, 0, C)
+    iota("keyb", [[-int(M), C]], int(M) * C, 0, C)
+    at(AT["x0"])
     quant(T.xq0[:, :], T.xs0[:, :], ["x0"], ["xq0"], T.x0[:, :], 4 * C)
     send_codes(0)
+    at(AT["u"])
+    act(slot("cv", 1), slot("cv", 0), el(C))
     quant(T.uq[:, :], T.uqs[:, :], ["ub"], ["uq"], T.ub[:, :], 512)
-    cp(R("uo"), R("c16", 0, 8))
+    quant(T.vq[:, :], T.vqs[:, :], ["vb"], ["vq"], T.vb[:, :], 512)
+    ts(R("uo"), R("j32", 0, 8), 16.0, A.mult)
     cp((T.uk[:, :].bitcast(dt.uint32), ["uk"]), (T.uq[:, :].bitcast(dt.uint32).indirect(T.uo[:, :]), ["uq", "uo"]), ga(128))
-    cp(R("uks"), (T.uqs[:, :].indirect(T.uo[:, :]), ["uq", "uo"]), ga(128))
-    phase("unit")
-    op("v", [], ["et"], lambda: V.memset(T.et[:, :], 0.0), 1.06)
-    ts(R("pn"), R("pi"), -1.0, A.mult)
-    act(R("diag", 0, 128, "d0"), R("jf", 0, 128), el(128), 1.0, (T.pn[:, 0:1], ["pn"]), SIGN)
-    act(R("diag", 128, 256, "d1"), R("diag", 0, 128, "d0"), el(128), 1.0, 0.0, ActivationFunctionType.Square)
-    for b in range(4):
-        lo = 512 * b
-        act((T.et[:, lo + b:lo + 512:4], ["et%d" % b]), (T.diag[:, 128:256], ["d1", "et"]), el(128), -0.5, 0.5)
-    quant(T.eq[:, :], T.eqs[:, :], ["et", "et0", "et1", "et2", "et3"], ["eq"], T.et[:, :], 2048)
-    phase("mates")
+    act(R("uks"), (T.uqs[:, :].indirect(T.uo[:, :]), ["uq", "uo"]), ga(128))
+    at(AT["mates"])
     cp(R("mo"), R("mli"))
-    ts(tab("jt"), R("c16"), p16, A.add)
+    ts(tab("jt"), R("j32", 0, TC), 16.0, A.mult, p16, A.add)
     tt(tab("u0"), R("mli"), tab("jt"), A.is_lt)
     ts(tab("ca"), tab("u0"), float(C), A.mult)
 
@@ -427,93 +456,88 @@ def rank_program(g, core, T, topo):
         tt(tab("u1"), tab("u0"), minus, A.subtract)
         ts(out, tab("u1"), col(DOWN), A.mult)
 
-    first = spare()
-    op("v", ["jc", "fo0"], first[1], lambda: V.tensor_copy(first[0].indirect(T.fo0[:, :]), T.jc[:, 0:C]), 1.2)
-    offsets(R("ho0"), table_of(first))
-    a, b = spare(), spare()
-    act(a, by(jc, R("mo")), ga(C))
-    act(b, by(a, R("ho0")), ga(C))
-    difference(tab("dh"), table_of(b), R("ho0"))
-
-    def parts(name):
-        return T[name][:, :], [name + "a", name + "b"]
-
-    def part(name, p, lo, hi):
-        return T[name][:, lo:hi], [name + k for k in p]
-
     for r in range(3):
         last = r == 2
-        PARTS = SPLIT if r in SPLIT_IN else WHOLE
         xq, xs, xr = T["xq%d" % r], T["xs%d" % r], ["xq%d" % r]
         fo, nfo = R("fo%d" % r), R("fo%d" % (r + 1))
         ho, nho = R("ho%d" % (r % 2)), R("ho%d" % ((r + 1) % 2))
-        phase("pow", "0" if r == 0 else "")
         tabs = [fo] + [slot("ft", k, TC) for k in range(6)]
+        at(2.1)
         act(slot("fr", 0), by(jc, fo), ga(C))
         for k in range(1, 8):
+            at(1.6 + AT["level"] * min(k, 6))
             act(slot("fr", k), by(slot("fr", k - 1), tabs[min(k - 1, 5)]), ga(C))
             if k != 6:
                 offsets(tabs[min(k, 6)], table_of(slot("fr", k)))
         if r == 0:
-            phase("mates")
+            at(AT["dfm"])
             a = spare()
             act(a, by(slot("fr", 0), R("mo")), ga(C))
             difference(tab("dfm"), table_of(a), R("fli"))
-        phase("key")
+        at(0.0)
         cur, k = "key0", 0
         for level, (rad, n) in enumerate(LEVELS):
             base = cur
             for i in range(rad - 1):
                 zz = "key1" if level == 0 else "za%d" % (level % 2) if i == 0 else "zb0"
-                for p, (lo, hi) in PARTS.items():
-                    if level:
-                        act(part(zz, p, lo, hi), part(base, p, lo, hi), el(hi - lo), 1.0, float(-n * (i + 1)))
+                if level:
+                    act(R(zz), R(base), el(C), 1.0, float(-n * (i + 1)))
                 d = "y%d" % (k % 4)
                 k += 1
-                for p, (lo, hi) in PARTS.items():
-                    off = (tabs[level][0][:, lo // 16:hi // 16], tabs[level][1])
-                    win = parts(cur) if level else R(cur)
-                    tt(part(d, p, lo, hi), by(win, off), part(zz, p, lo, hi) if level else R(zz, lo, hi), A.min, ga(hi - lo))
+                tt(R(d), by(R(cur), tabs[level]), R(zz), A.min, ga(C))
                 cur = d
-        key = parts(cur)
-        phase("line")
+        key = R(cur)
         v = table_of(key, True)
         ts(tab("ro"), v, col(DOWN_M), A.mult)
         ts(tab("ki"), v, col(DOWN), A.mult)
         ts(tab("dj"), tab("ki"), int(M) - 1, A.bitwise_and)
+        cp(R("sd%d" % r), tab("dj"))
+        send_list(r, "d", ["sd%d" % r])
         sa = "sa%d" % r
-        po, ln, eo = [R(sa, k * TC, (k + 1) * TC, sa + "e" * (k == 2)) for k in range(3)]
-        if TWIN:
-            for p, (lo, hi) in PARTS.items():
-                act(part("twin", p, lo, hi), part(cur, p, lo, hi), el(hi - lo))
-        tt(R("dn"), by(key, fo), parts("twin") if TWIN else key, A.subtract, ga(C))
+        po, ln, eo = R(sa, 0, TC), R(sa, TC, 2 * TC), tab("eo")
+        act(R("twin"), key, el(C))
+        tt(R("dn"), by(key, fo), R("twin"), A.subtract, ga(C))
         scan(R("st"), R("step"), R("dn"), -1.0 - M - H, A.add, A.add, el(C))
         tt(slot("pl", 0), by(R("st"), tab("ro")), key, A.subtract, ga(C))
         act(slot("pl", 1), by(R("dn"), tab("ro")), ga(C), 1.0, 1.0 - H)
         scan(R("sc2"), (T.cv[:, :], ["cv0", "cv1"]), (T.pl[:, :], ["pl0", "pl1"]), 0.0, A.mult, A.add, el(C))
-        offsets(R(sa, 0, 2 * TC), (T.sc2[:, 15:2 * C:16], ["sc2"]))
+        offsets(R(sa), (T.sc2[:, 15:2 * C:16], ["sc2"]))
+        send_list(r, "a", [sa])
         tt(eo, po, tab("dj"), A.add)
-        send_list(r, "a", [sa, sa + "e"])
-        op("v", ["keyb", sa], ["ord"], lambda po=po: V.tensor_copy(T.ord[:, :].indirect(po[0]), T.keyb[:, :]), 1.2)
+        tt(tab("dd"), tab("dj"), ln, A.subtract)
+        op("v", ["keyb", sa], ["ord"], lambda po=po: V.tensor_copy(T.ord[:, :].indirect(po[0]), T.keyb[:, :]),
+           0.05 + C * SCATTER)
         oo = R("sb%d" % r)
         ts(oo, table_of(R("ord"), True), col(LESS_M), A.mult, float(C), A.add)
         send_list(r, "b", oo[1])
+        if r == 0:
+            at(AT["h0"])
+            ts(tab("u0"), tab("dd"), -1.0, A.is_equal)
+            tt(tab("u1"), tab("u0"), ln, A.mult)
+            ts(tab("u0"), po, -1.0, A.add)
+            tt(tab("bo"), tab("u0"), tab("u1"), A.add)
+            act(R("nlr"), by(R("ord"), tab("bo")), ga(C))
+            ts(ho, table_of(R("nlr"), True), col(LESS_M), A.mult, float(C), A.add)
+            a, b = spare(), spare()
+            act(a, by(jc, R("mo")), ga(C))
+            act(b, by(a, ho), ga(C))
+            difference(tab("dh"), table_of(b), ho)
 
-        phase("score")
+        at(0.0)
         mm("p4", T.uk[:, :], T.uks[:, :], ["uk", "uks"], xq[:, :], xs[:, :], xr)
         out_of(R("s"), "p4")
-        phase("fh")
+        at(AT["fh"])
         for b in range(4):
             mm("p%d" % b, T.eq[:, 128 * b:128 * b + 128], T.eqs[:, 128 * b:128 * b + 128], ["eq"], xq[:, :], xs[:, :], xr)
             out_of(slot("fh", b), "p%d" % b)
-        phase("fs")
+        at(AT["fs"])
         for b in range(4):
             mm("p%d" % (4 + b), T.eq[:, 128 * b:128 * b + 128], T.eqs[:, 128 * b:128 * b + 128], ["eq"],
                T["lc%d" % r][:, :], T["ls%d" % r][:, :], ["lc%d" % r])
             out_of(slot("fs", b), "p%d" % (4 + b))
 
-        phase("lead")
-        pick(R("so"), R("s"), oo)
+        at(0.0)
+        cp(R("so"), by(R("s"), oo), ga(C))
         act(R("fla", 1, C + 1), by(R("dn"), oo), ga(C), -BIG, -BIG)
         fla = (T.fla[:, 0:C], ["fla", "fla0"])
         act(R("flb", 0, C), fla, el(C), 1.0, -1.0)
@@ -521,107 +545,99 @@ def rank_program(g, core, T, topo):
         tt(R("cand"), by(R("top"), eo), R("s"), A.is_equal, ga(C))
         tt(R("ck"), by(R("cand"), oo), R("ord"), A.mult, ga(C))
         scan(R("run"), R("flb", 0, C), R("ck"), 0.0, A.add, A.max, el(C))
-        pick(R("lead"), R("run"), eo)
+        cp(R("lead"), by(R("run"), eo), ga(C))
         v = table_of(R("lead"), True)
         ts(tab("lo"), v, col(LESS_M), A.mult, float(C), A.add)
         ts(tab("kl"), v, col(LESS), A.mult, M * C, A.add)
         tt(tab("x0i"), tab("kl"), tab("dj"), A.subtract)
-        tt(tab("x1i"), tab("x0i"), ln, A.add)
+        tt(tab("x1i"), tab("kl"), tab("dd"), A.subtract)
         ts(tab("a0i", 2), tab("x0i", 2), int(M) - 1, A.bitwise_and)
         tt(tab("i"), tab("a0i"), tab("a1i"), A.min)
 
-        phase("far")
+        at(AT["far"])
         la, oe = "la%d" % r, R("lb%d" % r)
-        for k in (1, 0, 2):
-            act(slot("pr", k), by(jc, R(la, k * TC, (k + 1) * TC)), ga(C))
-        act(slot("oer", 0), by(jc, oe), ga(C))
-        act(slot("oer", 1), slot("oer", 0), el(C))
+        for k, off in ((2, R("ld%d" % r)), (1, R(la, TC, 2 * TC)), (0, R(la, 0, TC))):
+            act(slot("pr", k), by(jc, off), ga(C))
         act(slot("both", 0), by(R("s"), oe), ga(C))
+        act(slot("oer", 0), by(jc, oe), ga(C))
         act(slot("both", 1), slot("both", 0), el(C), -1.0)
-        phase("walk")
-        for k, name, home in ((1, "lnf", False), (0, "pef", True), (2, "enf", False)):
+        act(slot("oer", 1), slot("oer", 0), el(C))
+        at(0.0)
+        for k, name, home in ((1, "lnf", False), (2, "def", True), (0, "pef", False)):
             a = spare()
             if home:
                 cp(a, by(slot("pr", k), tab("lo")), ga(C))
             else:
                 act(a, by(slot("pr", k), tab("lo")), ga(C))
             lin(tab(name), table_of(a), col(DOWN), float(H))
-        op("v", ["lnf"], ["rl"], lambda: V.reciprocal(tab("rl")[0], tab("lnf")[0]), 0.35)
-        tt(tab("w0"), tab("pef"), tab("i"), A.add)
-        tt(tab("zz"), tab("enf"), tab("w0"), A.subtract)
+        op("v", ["lnf"], ["rl"], lambda: V.reciprocal(tab("rl")[0], tab("lnf")[0]), 0.32)
+        tt(tab("zz"), tab("def"), tab("i"), A.subtract)
         tt(tab("t"), tab("zz"), tab("rl"), A.mult)
         ts(tab("q"), tab("t"), -0.499, A.add)
         tt(tab("m"), tab("q"), tab("lnf"), A.mult)
+        tt(tab("w0"), tab("pef"), tab("i"), A.add)
         tt(tab("w0a"), tab("w0"), tab("ca"), A.add)
         tt(tab("wa"), tab("w0a"), tab("m"), A.add)
 
-        phase("splice")
+        at(0.0, ops[-1]["at"])
         both = (T.both[:, :], ["both0", "both1"])
         act(R("nms"), by(both, tab("wa")), ga(C), -1.0)
         cp(R("ms"), by(both, tab("wa")), ga(C))
         tt(R("sw"), by(R("nms"), R("mo")), R("ms"), A.is_gt, ga(C))
         tt(tab("ta"), table_of(R("sw")), tab("dfm"), A.mult)
         tt(nfo, tab("ta"), fo, A.add)
-        if not last:
-            phase("keep")
-            lin(tab("tc"), tab("ta"), col(LESS_2), 0.0)
-            tt(tab("dfm"), tab("tc"), tab("dfm"), A.add)
-        phase("tee", "2" if last else "")
         a = spare()
         act(a, by((T.oer[:, :], ["oer0", "oer1"]), tab("wa")), ga(C))
         offsets(tab("to"), table_of(a))
-        phase("back")
         a = spare()
         act(a, by(R("sw"), ho), ga(C))
         tt(tab("th"), table_of(a), tab("dh"), A.mult)
         tt(nho, tab("th"), ho, A.add)
         if not last:
-            phase("keep")
+            at(AT["keep"])
+            lin(tab("tc"), tab("ta"), col(LESS_2), 0.0)
+            tt(tab("dfm"), tab("tc"), tab("dfm"), A.add)
             lin(tab("td"), tab("th"), col(LESS_2), 0.0)
             tt(tab("dh"), tab("td"), tab("dh"), A.add)
 
-        phase("z")
         for b in range(4):
+            at(AT["gt"] + 0.5 * b)
             act(slot("gt", b), by(slot("fs", b), tab("to")), ga(C))
+            at(AT["z"] + 0.5 * b)
             tt((T.z[:, b:4 * C:4], ["z%d" % b]), by(slot("fh", b), nfo), slot("gt", b), A.add, ga(C))
-        phase("zq")
         quant(T.zq[:, :], T.zs[:, :], ["z0", "z1", "z2", "z3"], ["zq"], T.z[:, :], 4 * C)
-        phase("rb")
-        for b in (2, 3, 0, 1):
+        for b in range(4):
+            at(AT["rb"] + 0.5 * b)
             bank = "p%d" % (4 + b)
             mm(bank, T.wq[:, 128 * b:128 * b + 128], T.wsp[:, 128 * b:128 * b + 128], ["wq", "wsp"],
                T.zq[:, :], T.zs[:, :], ["zq"])
-            out_of(slot("rb", b), bank, 2.0 ** -6, b in R_HOME)
-        phase("x")
-        for b in P_FAR:
-            act(slot("gp", b), by(slot("rb", b), nho), ga(C))
-        for b in range(4):
-            out = (T.xt[:, b:4 * C:4], ["xt%d" % b])
-            if b in P_FAR:
-                tt((out[0], out[1] + ["p%d" % b]), slot("gp", b), (T["p%d" % b][:, 0:C], []), A.add, el(C))
-            else:
-                tt(out, by(slot("rb", b), nho), slot("fh", b), A.add, ga(C))
-        phase("xq")
-        quant(T["xq%d" % (r + 1)][:, :], T["xs%d" % (r + 1)][:, :], ["xt0", "xt1", "xt2", "xt3"], ["xq%d" % (r + 1)],
-              T.xt[:, :], 4 * C)
+            out_of(slot("rb", b), bank, 2.0 ** -6, b in R_HOME[r])
+        nq, ns = "xq%d" % (r + 1), "xs%d" % (r + 1)
+        for p, (lo, hi) in (HALVES if last else WHOLE).items():
+            for b in range(4):
+                at(AT["x"] + AT["level"] * b * (not last))
+                out = (T.xt[:, 4 * lo + b:4 * hi:4], ["xt%d%s" % (b, k) for k in p])
+                if b in P_FAR[r]:
+                    act(slot("gp", b), by(slot("rb", b), nho), ga(C))
+                    tt((out[0], out[1] + ["p%d" % b]), slot("gp", b), (T["p%d" % b][:, 0:C], []), A.add, el(C))
+                else:
+                    off = (nho[0][:, lo // 16:hi // 16], nho[1])
+                    tt(out, by(slot("rb", b), off), slot("fh", b, C, lo, hi), A.add, ga(hi - lo))
+            quant(T[nq][:, lo:hi], T[ns][:, lo:hi], ["xt%d%s" % (b, k) for b in range(4) for k in p], [nq + p * last],
+                  T.xt[:, 4 * lo:4 * hi], 4 * (hi - lo))
         if not last:
             send_codes(r + 1)
-        else:
-            act(R("nlr"), by(jf, nfo), ga(C))
 
-    phase("out")
-    quant(T.vq[:, :], T.vqs[:, :], ["vb"], ["vq"], T.vb[:, :], 512)
-    mm("p4", T.vq[:, :], T.vqs[:, :], ["vq"], T.xq3[:, :], T.xs3[:, :], ["xq3"])
-    out_of(R("yb"), "p4")
-
-    def store(out, in_, res, tail=2.0):
-        op("y", [res], [], lambda: g.sync.dma_start(out=out, in_=in_), 0.1, "lout", 16, tail)
-
-    store(T.nl[:, :], T.nlr[0:128:16, :], "nlr")
-    store(T.y[:, :], T.yb[:, :], "yb", 3.0)
-    store(T.oc[:, :], T.xq3[:, :].bitcast(dt.uint8), "xq3")
+    at(0.0)
+    act(R("nlr"), by(jc, R("fo3")), ga(C), 1.0, float(H))
+    store("y", T.nl[:, :], T.nlr[0:128:16, :], ["nlr"])
+    for bank, (p, (lo, hi)) in zip(("p0", "p1"), HALVES.items()):
+        mm(bank, T.vq[:, :], T.vqs[:, :], ["vq"], T.xq3[:, lo:hi], T.xs3[:, lo:hi], ["xq3" + p], hi - lo)
+        out_of(R("yb", lo, hi, "yb" + p), bank, n=hi - lo)
+        store("y", T.oc[:, 4 * lo:4 * hi], T.xq3[:, lo:hi].bitcast(dt.uint8), ["xq3" + p], 0.6)
+        store("s", T.y[:, lo:hi], T.yb[:, lo:hi], ["yb" + p], 0.6)
     for k in range(4):
-        store(T.osc[4 * k:4 * k + 4, :], T.xs3[32 * k:32 * k + 4, :], "xq3")
+        store("y", T.osc[4 * k:4 * k + 4, :], T.xs3[32 * k:32 * k + 4, :], ["xq3a", "xq3b"])
     emit()
 
 
@@ -635,7 +651,7 @@ def relay_program(g, core, T, topo):
                 n += send(g, T, topo, core, dst, T["lc%d" % r][:, :].bitcast(dt.uint8),
                           T["lc%d" % r][:, :].bitcast(dt.uint8), "ac%d" % r, NE)
                 n += send(g, T, topo, core, dst, T["ls%d" % r][:, :], T["ls%d" % r][:, :], "ac%d" % r, NE)
-            for k in "ab" if relay_of(src, dst, topo, 1) == core else "":
+            for k in "dab" if relay_of(src, dst, topo, 1) == core else "":
                 g.wait_ge(T.sem["a%s%d" % (k, r)], NL)
                 name = "l%s%d" % (k, r)
                 n += send(g, T, topo, core, dst, T[name][:, :], T[name][:, :], "a%s%d" % (k, r), NL)

@@ -4,6 +4,7 @@ from concourse.mybir import dt, AluOpType, ActivationFunctionType
 A = AluOpType
 COPY = ActivationFunctionType.Copy
 IDENT = ActivationFunctionType.Identity
+RELU = ActivationFunctionType.Relu
 C = 288
 TC = C // 16
 H = C // 2
@@ -14,16 +15,15 @@ MASKS = [4, 1, 2]
 LEVELS = [(2, 1), (2, 2), (2, 4), (2, 8), (2, 16), (3, 32), (3, 96)]
 HALVES = {"a": (0, 160), "b": (160, C)}
 WHOLE = {"ab": (0, C)}
-R_HOME = [(), (), ()]
-P_FAR = [(3,), (3,), ()]
+P_FAR = [(3,), (3,), (0, 1, 2)]
 SMALL_S = ("pef", "tc", "td")
 NE, NL = 8, 8
-NB, NF = 16, 4
+NB, NF = 20, 4
 WAKE, GATHER, SCATTER, EL = 0.15, 1.43e-3, 3.6e-3, 0.955e-3
-LIST_US, CODE_US, HOP_US, FIRST_US = 0.55, 2.9, 2.0, 1.5
+LIST_US, PLANE_US, CODE_US, HOP_US, FIRST_US, STORE_US = 0.55, 0.9, 2.0, 2.1, 1.5, 1.7
 AT = dict(x0=4.0, u=4.2, eq=2.7, mates=5.4, dfm=12.2, h0=16.6, level=1.1, gt=1.7, z=2.5, rb=5.2, x=5.5, fh=13.7, fs=18.7,
           keep=15.6, far=16.4)
-TRIES = 20000
+TRIES = 24000
 SPAN = [0.0]
 FOUND = {}
 
@@ -42,7 +42,7 @@ _b("xq0 xq1 xq2 xq3 lc0 lc1 lc2 zq", C, CODE)
 _b("xs0 xs1 xs2 xs3 ls0 ls1 ls2 zs", C, "uint8")
 _b("fo0 fo1 fo2 fo3 sb0 sb1 sb2 lb0 lb1 lb2 sd0 sd1 sd2 ld0 ld1 ld2 ho0 ho1 mo rep", TC, "uint16")
 _b("sa0 sa1 sa2 la0 la1 la2", 2 * TC, "uint16")
-_b("ft tu", 6 * TC, "uint16")
+_b("ft tu", 7 * TC, "uint16")
 _b("wq eq", 512, CODE)
 _b("wsp eqs", 512, "uint8")
 _b("uq uk vq", 128, CODE)
@@ -52,11 +52,10 @@ _b("ub vb", 512, "bfloat16")
 _b("fli mli", TC, "int32")
 _b("ti", 9 * TC, "int32")
 _b("tf", 20 * TC, "float32")
-_b("key0 key1 keyb step s y0 y1 y2 y3 za0 za1 zb0 twin dn st ord so top ck run lead ms nms yb nlr", C, "float32")
+_b("key0 key1 s y0 y1 y2 y3 za0 za1 zb0 kf kr st ord so top ck run lead ms nms yb nlr", C, "float32")
 _b("fla flb", C + 16, "float32")
 _b("jc", C + 16, "bfloat16")
-_b("cand sw", C, "bfloat16")
-_b("cv pl oer sc2", 2 * C, "bfloat16")
+_b("cand sw orb oer cv", C, "bfloat16")
 _b("both", 2 * C, "float32")
 _b("fr", 8 * C, "bfloat16")
 _b("pr", 3 * C, "bfloat16")
@@ -71,7 +70,7 @@ _b("p16 p17", 2, "float32")
 _b("col", 8, "float32")
 _b("half", 128, "bfloat16")
 _b("p0 p1 p2 p3 p4 p5 p6 p7", 512, "float32", "psum")
-TU = "ro lo wa to eo bo".split()
+TU = "ro lo w wa to eo bo".split()
 TI = "ki dj dd kl q x0i x1i a0i a1i".split()
 TF = "jt ca dfm dh i lnf rl def pef zz t m w0 w0a ta tc th td u0 u1".split()
 
@@ -87,9 +86,10 @@ def relay_of(src, dst, topo, k):
     return cs[k % len(cs)]
 
 
-def send(g, T, topo, src, dst, out_ap, in_ap, sem, count):
+def send(g, T, topo, src, dst, out_ap, in_ap, sem, count, last=False):
     rid, pid = topo.addr(dst, src)
-    e = topo.engines(src, dst)[:count]
+    e = topo.engines(src, dst)
+    e = e[-count:] if last else e[:count]
     m = 0
     for k in e:
         m |= 1 << k
@@ -302,13 +302,13 @@ def rank_program(g, core, T, topo):
     def cp(out, a, c=None):
         op("v", a[1], out[1], lambda: V.tensor_copy(out[0], a[0]), el(TC) if c is None else c)
 
-    def act(out, a, c, scale=1.0, bias=0.0):
+    def act(out, a, c, scale=1.0, bias=0.0, func=IDENT):
         scale, bias = num(scale), num(bias)
         if not scale[1] and not bias[1] and scale[0] == 1.0 and bias[0] == 0.0:
             op("s", a[1], out[1], lambda: S.activation(out[0], a[0], COPY), c)
         else:
             op("s", a[1] + scale[1] + bias[1], out[1],
-               lambda: S.activation(out[0], a[0], IDENT, bias=bias[0], scale=scale[0]), c)
+               lambda: S.activation(out[0], a[0], func, bias=bias[0], scale=scale[0]), c)
 
     def lin(out, a, scale, bias):
         if out[1][0] in SMALL_S:
@@ -333,7 +333,7 @@ def rank_program(g, core, T, topo):
         name = "scf" if wide else "sc"
         k = fresh(name, NF if wide else NB)
         out = slot(name, k)
-        scan(out, slot("cv", 0), row, 0.0, A.mult, A.add, el(C, 1.0 if wide else 0.5))
+        scan(out, R("cv"), row, 0.0, A.mult, A.add, el(C, 1.0 if wide else 0.5))
         return T[name][:, k * C + 15:(k + 1) * C:16], out[1]
 
     def offsets(out, view):
@@ -354,41 +354,38 @@ def rank_program(g, core, T, topo):
     def store(qn, out, in_, res, us=0.1):
         tag = "store%d" % len(ops)
         op(qn, res, [tag], lambda: queues[qn].dma_start(out=out, in_=in_), 0.1, "lout", 16)
-        op("d", [tag], [], None, us, None, 0, HOP_US)
+        op("d", [tag], [], None, us, None, 0, STORE_US)
 
-    def out_of(out, bank, scale=1.0, home=False, n=C):
-        o, a = (out[0], out[1] + [bank]), (T[bank][:, 0:n], [])
-        if home:
-            ts(o, a, scale, A.mult, c=el(n))
-        else:
-            act(o, a, el(n), scale)
+    def out_of(out, bank, scale=1.0, n=C):
+        act((out[0], out[1] + [bank]), (T[bank][:, 0:n], []), el(n), scale)
 
     sends = [0]
 
-    def to_partner(r, bufs, sem, count, land, us, lane):
+    def to_partner(r, bufs, sem, count, land):
         dst = T.cores[rank ^ MASKS[r]]
-        via = relay_of(core, dst, topo, lane)
-        hop = dst if via is None else via
 
-        def go(o, i):
-            sends[0] += send(g, T, topo, core, hop, o, i, sem, count)
+        def go(hop, o, i, lane):
+            sends[0] += send(g, T, topo, core, hop, o, i, sem, count, lane == 0)
 
-        for o, i, res in bufs:
-            op("p", res, ["out" + sem, "lane%d" % lane], lambda o=o, i=i: go(o, i), 0.3)
+        for k, (o, i, res, us, lane) in enumerate(bufs):
+            via = relay_of(core, dst, topo, lane)
+            hop = dst if via is None else via
+            way = "way%s%d" % (sem, k)
+            op("p", res, [way, "lane%d" % lane], lambda hop=hop, o=o, i=i, lane=lane: go(hop, o, i, lane), 0.3)
             ops[-1]["sem"] = None
-        op("d", ["out" + sem], ["way" + sem], None, us, None, 0, HOP_US)
-        if via is not None:
-            us += 0.3 * len(bufs) + FIRST_US * (sem[1] in "cd")
-            op("r%d" % lane, ["way" + sem], ["way" + sem, "hop%d" % lane], None, us, None, 0, HOP_US)
-        op(None, ["way" + sem], [land], None, 0.0, None, 0, 0.0, (sem, count * len(bufs)))
+            op("d" if via is None or lane else "e", [way], [way], None, us, None, 0, HOP_US)
+            if via is not None:
+                op("r%d" % lane, [way], [way], None, us + 0.3 + FIRST_US * (sem[1] == "c"), None, 0, HOP_US)
+        op(None, ["way%s%d" % (sem, k) for k in range(len(bufs))], [land], None, 0.0, None, 0, 0.0, (sem, count * len(bufs)))
 
     def send_list(r, k, res):
         a, b = "l%s%d" % (k, r), "s%s%d" % (k, r)
-        to_partner(r, [(T[a][:, :], T[b][:, :], res)], "a%s%d" % (k, r), NL, a, LIST_US, 1)
+        to_partner(r, [(T[a][:, :], T[b][:, :], res, LIST_US, 1)], "a%s%d" % (k, r), NL, a)
 
     def send_codes(r):
-        to_partner(r, [(T["lc%d" % r][:, :].bitcast(dt.uint8), T["xq%d" % r][:, :].bitcast(dt.uint8), ["xq%d" % r]),
-                       (T["ls%d" % r][:, :], T["xs%d" % r][:, :], ["xq%d" % r])], "ac%d" % r, NE, "lc%d" % r, CODE_US, 0)
+        q = "xq%d" % r
+        to_partner(r, [(T["lc%d" % r][:, :].bitcast(dt.uint8), T[q][:, :].bitcast(dt.uint8), [q], CODE_US, 0),
+                       (T["ls%d" % r][:, :], T["xs%d" % r][:, :], [q], PLANE_US, 1)], "ac%d" % r, NE, "lc%d" % r)
 
     load("y", T.fli[:, :], T.fl[:, :], "fli", "lf")
     load("s", T.x0[:, :], T.x[:, :], "x0", "lx", 3.5)
@@ -419,7 +416,7 @@ def rank_program(g, core, T, topo):
     ts(R("cvb"), R("j32", 0, 16), (T.p17[:, 0:1], ["p17"]), A.is_equal, UP, A.mult)
     tt(R("cv16"), R("cva"), R("cvb"), A.max)
     ts(R("rep"), R("j32", 0, TC), 0.0, A.mult, p16, A.add)
-    act(slot("cv", 0), by(R("cv16"), R("rep")), ga(C))
+    act(R("cv"), by(R("cv16"), R("rep")), ga(C))
     ts(col(DOWN), p16, 15.0, A.is_equal, 1.0 / UP, A.max)
     for k, f in ((DOWN_M, 1.0 / M), (LESS_M, -1.0 / M), (LESS, -1.0), (LESS_2, -2.0)):
         act(col(k), col(DOWN), el(1), f)
@@ -433,13 +430,10 @@ def rank_program(g, core, T, topo):
             T.et[:, 512 * b + b:512 * b + 512:4], T.half[:, :], [[-1, 128]], A.is_equal, 0.0, 0, 1), 0.2 + 256 * EL)
     at(AT["eq"])
     quant(T.eq[:, :], T.eqs[:, :], ["et", "et0", "et1", "et2", "et3"], ["eq"], T.et[:, :], 2048)
-    iota("step", [[0, C]], int(M) + 1, 0, C)
-    iota("keyb", [[-int(M), C]], int(M) * C, 0, C)
     at(AT["x0"])
     quant(T.xq0[:, :], T.xs0[:, :], ["x0"], ["xq0"], T.x0[:, :], 4 * C)
     send_codes(0)
     at(AT["u"])
-    act(slot("cv", 1), slot("cv", 0), el(C))
     quant(T.uq[:, :], T.uqs[:, :], ["ub"], ["uq"], T.ub[:, :], 512)
     quant(T.vq[:, :], T.vqs[:, :], ["vb"], ["vq"], T.vb[:, :], 512)
     ts(R("uo"), R("j32", 0, 8), 16.0, A.mult)
@@ -494,30 +488,34 @@ def rank_program(g, core, T, topo):
         cp(R("sd%d" % r), tab("dj"))
         send_list(r, "d", ["sd%d" % r])
         sa = "sa%d" % r
-        po, ln, eo = R(sa, 0, TC), R(sa, TC, 2 * TC), tab("eo")
-        act(R("twin"), key, el(C))
-        tt(R("dn"), by(key, fo), R("twin"), A.subtract, ga(C))
-        scan(R("st"), R("step"), R("dn"), -1.0 - M - H, A.add, A.add, el(C))
-        tt(slot("pl", 0), by(R("st"), tab("ro")), key, A.subtract, ga(C))
-        act(slot("pl", 1), by(R("dn"), tab("ro")), ga(C), 1.0, 1.0 - H)
-        scan(R("sc2"), (T.cv[:, :], ["cv0", "cv1"]), (T.pl[:, :], ["pl0", "pl1"]), 0.0, A.mult, A.add, el(C))
-        offsets(R(sa), (T.sc2[:, 15:2 * C:16], ["sc2"]))
-        send_list(r, "a", [sa])
+        po, ln, eo = R(sa, 0, TC), R(sa, TC, 2 * TC, sa + "n"), tab("eo")
+        act(R("kf"), by(key, fo), ga(C), 1.0, M + 1.0)
+        scan(R("st"), R("kf"), key, -1.0 - M - H, A.add, A.subtract, el(C))
+        a, drow = spare(), spare()
+        tt(a, by(R("st"), tab("ro")), key, A.subtract, ga(C))
+        offsets(po, table_of(a))
+        act(R("kr"), by(R("kf"), tab("ro")), ga(C))
+        tt(tab("u0"), table_of(R("kr"), True), v, A.subtract)
+        ts(tab("dd"), tab("u0"), col(DOWN), A.mult, -M, A.add)
+        tt(ln, tab("dd"), tab("dj"), A.add)
+        send_list(r, "a", po[1] + ln[1])
         tt(eo, po, tab("dj"), A.add)
-        tt(tab("dd"), tab("dj"), ln, A.subtract)
-        op("v", ["keyb", sa], ["ord"], lambda po=po: V.tensor_copy(T.ord[:, :].indirect(po[0]), T.keyb[:, :]),
+        act(drow, by(jc, R("sd%d" % r)), ga(C))
+        op("v", ["jc", sa], ["orb"], lambda po=po: V.tensor_copy(T.orb[:, :].indirect(po[0]), T.jc[:, 0:C]),
            0.05 + C * SCATTER)
+        act(R("ord"), R("orb"), el(C), -M, M * (C - H))
         oo = R("sb%d" % r)
-        ts(oo, table_of(R("ord"), True), col(LESS_M), A.mult, float(C), A.add)
+        offsets(oo, table_of(R("orb")))
         send_list(r, "b", oo[1])
         if r == 0:
             at(AT["h0"])
-            ts(tab("u0"), tab("dd"), -1.0, A.is_equal)
+            ts(tab("u0"), tab("dd"), 1.0, A.is_equal)
             tt(tab("u1"), tab("u0"), ln, A.mult)
             ts(tab("u0"), po, -1.0, A.add)
             tt(tab("bo"), tab("u0"), tab("u1"), A.add)
-            act(R("nlr"), by(R("ord"), tab("bo")), ga(C))
-            ts(ho, table_of(R("nlr"), True), col(LESS_M), A.mult, float(C), A.add)
+            a = spare()
+            act(a, by(R("orb"), tab("bo")), ga(C))
+            offsets(ho, table_of(a))
             a, b = spare(), spare()
             act(a, by(jc, R("mo")), ga(C))
             act(b, by(a, ho), ga(C))
@@ -525,7 +523,7 @@ def rank_program(g, core, T, topo):
 
         at(0.0)
         mm("p4", T.uk[:, :], T.uks[:, :], ["uk", "uks"], xq[:, :], xs[:, :], xr)
-        out_of(R("s"), "p4")
+        out_of(R("s"), "p4", -1.0)
         at(AT["fh"])
         for b in range(4):
             mm("p%d" % b, T.eq[:, 128 * b:128 * b + 128], T.eqs[:, 128 * b:128 * b + 128], ["eq"], xq[:, :], xs[:, :], xr)
@@ -538,10 +536,10 @@ def rank_program(g, core, T, topo):
 
         at(0.0)
         cp(R("so"), by(R("s"), oo), ga(C))
-        act(R("fla", 1, C + 1), by(R("dn"), oo), ga(C), -BIG, -BIG)
+        act(R("fla", 1, C + 1), by(drow, oo), ga(C), -BIG, BIG * (1 - H), RELU)
         fla = (T.fla[:, 0:C], ["fla", "fla0"])
-        act(R("flb", 0, C), fla, el(C), 1.0, -1.0)
-        scan(R("top"), fla, R("so"), -BIG, A.add, A.max, el(C))
+        act(R("flb", 0, C), fla, el(C), -1.0, -1.0)
+        scan(R("top"), fla, R("so"), BIG, A.add, A.min, el(C))
         tt(R("cand"), by(R("top"), eo), R("s"), A.is_equal, ga(C))
         tt(R("ck"), by(R("cand"), oo), R("ord"), A.mult, ga(C))
         scan(R("run"), R("flb", 0, C), R("ck"), 0.0, A.add, A.max, el(C))
@@ -550,7 +548,7 @@ def rank_program(g, core, T, topo):
         ts(tab("lo"), v, col(LESS_M), A.mult, float(C), A.add)
         ts(tab("kl"), v, col(LESS), A.mult, M * C, A.add)
         tt(tab("x0i"), tab("kl"), tab("dj"), A.subtract)
-        tt(tab("x1i"), tab("kl"), tab("dd"), A.subtract)
+        tt(tab("x1i"), tab("kl"), tab("dd"), A.add)
         ts(tab("a0i", 2), tab("x0i", 2), int(M) - 1, A.bitwise_and)
         tt(tab("i"), tab("a0i"), tab("a1i"), A.min)
 
@@ -558,10 +556,9 @@ def rank_program(g, core, T, topo):
         la, oe = "la%d" % r, R("lb%d" % r)
         for k, off in ((2, R("ld%d" % r)), (1, R(la, TC, 2 * TC)), (0, R(la, 0, TC))):
             act(slot("pr", k), by(jc, off), ga(C))
-        act(slot("both", 0), by(R("s"), oe), ga(C))
-        act(slot("oer", 0), by(jc, oe), ga(C))
-        act(slot("both", 1), slot("both", 0), el(C), -1.0)
-        act(slot("oer", 1), slot("oer", 0), el(C))
+        act(slot("both", 1), by(R("s"), oe), ga(C))
+        act(slot("both", 0), slot("both", 1), el(C), -1.0)
+        act(R("oer"), by(jc, oe), ga(C))
         at(0.0)
         for k, name, home in ((1, "lnf", False), (2, "def", True), (0, "pef", False)):
             a = spare()
@@ -586,8 +583,9 @@ def rank_program(g, core, T, topo):
         tt(R("sw"), by(R("nms"), R("mo")), R("ms"), A.is_gt, ga(C))
         tt(tab("ta"), table_of(R("sw")), tab("dfm"), A.mult)
         tt(nfo, tab("ta"), fo, A.add)
+        tt(tab("w"), tab("w0"), tab("m"), A.add)
         a = spare()
-        act(a, by((T.oer[:, :], ["oer0", "oer1"]), tab("wa")), ga(C))
+        act(a, by(R("oer"), tab("w")), ga(C))
         offsets(tab("to"), table_of(a))
         a = spare()
         act(a, by(R("sw"), ho), ga(C))
@@ -611,17 +609,18 @@ def rank_program(g, core, T, topo):
             bank = "p%d" % (4 + b)
             mm(bank, T.wq[:, 128 * b:128 * b + 128], T.wsp[:, 128 * b:128 * b + 128], ["wq", "wsp"],
                T.zq[:, :], T.zs[:, :], ["zq"])
-            out_of(slot("rb", b), bank, 2.0 ** -6, b in R_HOME[r])
+            out_of(slot("rb", b), bank, 2.0 ** -6)
         nq, ns = "xq%d" % (r + 1), "xs%d" % (r + 1)
         for p, (lo, hi) in (HALVES if last else WHOLE).items():
             for b in range(4):
                 at(AT["x"] + AT["level"] * b * (not last))
                 out = (T.xt[:, 4 * lo + b:4 * hi:4], ["xt%d%s" % (b, k) for k in p])
-                if b in P_FAR[r]:
-                    act(slot("gp", b), by(slot("rb", b), nho), ga(C))
-                    tt((out[0], out[1] + ["p%d" % b]), slot("gp", b), (T["p%d" % b][:, 0:C], []), A.add, el(C))
+                off = (nho[0][:, lo // 16:hi // 16], nho[1])
+                if b in P_FAR[r] and p != "a":
+                    act(slot("gp", b, C, lo, hi), by(slot("rb", b), off), ga(hi - lo))
+                    tt((out[0], out[1] + ["p%d" % b]), slot("gp", b, C, lo, hi), (T["p%d" % b][:, lo:hi], []), A.add,
+                       el(hi - lo))
                 else:
-                    off = (nho[0][:, lo // 16:hi // 16], nho[1])
                     tt(out, by(slot("rb", b), off), slot("fh", b, C, lo, hi), A.add, ga(hi - lo))
             quant(T[nq][:, lo:hi], T[ns][:, lo:hi], ["xt%d%s" % (b, k) for b in range(4) for k in p], [nq + p * last],
                   T.xt[:, 4 * lo:4 * hi], 4 * (hi - lo))
@@ -631,7 +630,7 @@ def rank_program(g, core, T, topo):
     at(0.0)
     act(R("nlr"), by(jc, R("fo3")), ga(C), 1.0, float(H))
     store("y", T.nl[:, :], T.nlr[0:128:16, :], ["nlr"])
-    for bank, (p, (lo, hi)) in zip(("p0", "p1"), HALVES.items()):
+    for bank, (p, (lo, hi)) in zip(("p4", "p5"), HALVES.items()):
         mm(bank, T.vq[:, :], T.vqs[:, :], ["vq"], T.xq3[:, lo:hi], T.xs3[:, lo:hi], ["xq3" + p], hi - lo)
         out_of(R("yb", lo, hi, "yb" + p), bank, n=hi - lo)
         store("y", T.oc[:, 4 * lo:4 * hi], T.xq3[:, lo:hi].bitcast(dt.uint8), ["xq3" + p], 0.6)
@@ -647,13 +646,15 @@ def relay_program(g, core, T, topo):
         for i, src in enumerate(T.cores):
             dst = T.cores[i ^ MASKS[r]]
             if relay_of(src, dst, topo, 0) == core:
-                g.wait_ge(T.sem["ac%d" % r], 2 * NE)
+                g.wait_ge(T.sem["ac%d" % r], NE)
                 n += send(g, T, topo, core, dst, T["lc%d" % r][:, :].bitcast(dt.uint8),
                           T["lc%d" % r][:, :].bitcast(dt.uint8), "ac%d" % r, NE)
+            if relay_of(src, dst, topo, 1) == core:
+                g.wait_ge(T.sem["ac%d" % r], NE)
                 n += send(g, T, topo, core, dst, T["ls%d" % r][:, :], T["ls%d" % r][:, :], "ac%d" % r, NE)
-            for k in "dab" if relay_of(src, dst, topo, 1) == core else "":
-                g.wait_ge(T.sem["a%s%d" % (k, r)], NL)
-                name = "l%s%d" % (k, r)
-                n += send(g, T, topo, core, dst, T[name][:, :], T[name][:, :], "a%s%d" % (k, r), NL)
+                for k in "dab":
+                    g.wait_ge(T.sem["a%s%d" % (k, r)], NL)
+                    name = "l%s%d" % (k, r)
+                    n += send(g, T, topo, core, dst, T[name][:, :], T[name][:, :], "a%s%d" % (k, r), NL)
     if n:
         g.wait_ge(T.sem.sent, n)

@@ -12,19 +12,35 @@ M = 1024.0
 UP = 2.0 ** 40
 BIG = 2.0 ** 72
 MASKS = [4, 1, 2]
-LEVELS = [(2, 1), (2, 2), (2, 4), (2, 8), (2, 16), (3, 32), (3, 96)]
-HALVES = {"a": (0, 160), "b": (160, C)}
+POWERS = [1, 2, 4, 8, 16, 32, 32]
+STEPS = [(1, 1), (2, 2), (4, 4), (8, 8), (16, 16), (32, 32), (32, 32), (96, 96), (96, 96)]
+HALVES = {"a": (0, 128), "b": (128, C)}
 WHOLE = {"ab": (0, C)}
-P_FAR = [(3,), (3,), (0, 1, 2)]
-SMALL_S = ("pef", "tc", "td")
-NE, NL = 8, 8
+Z_RUNS = [WHOLE, WHOLE, HALVES]
+P_FAR = [(3,), (2, 3), (0, 1, 2)]
+PLAIN_A = [False, False, True]
+CUT_F, CUT_ROW, CUT_LEAD, CUT_KF = 10, 10, 8, 12
+ASIDE = ("c1",)
+Z_WORTH = [(0.2, 0.0), (0.2, 0.0), (0.7, 0.0)]
+NEEDED = dict(aa=(0.8, 1.6), ab=(0.8, 3.6), ac=(0.8, 3.6))
+LIFT = 2.0 ** 20
+ROUND = 1.5 * 2.0 ** 23
+NS = 7
+NE, NL, NEAR = 8, 8, 16
 NB, NF = 20, 4
 WAKE, GATHER, SCATTER, EL = 0.15, 1.43e-3, 3.6e-3, 0.955e-3
-LIST_US, PLANE_US, CODE_US, HOP_US, FIRST_US, STORE_US = 0.55, 0.9, 2.0, 2.1, 1.5, 1.7
-AT = dict(x0=4.0, u=4.2, eq=2.7, mates=5.4, dfm=12.2, h0=16.6, level=1.1, gt=1.7, z=2.5, rb=5.2, x=5.5, fh=13.7, fs=18.7,
-          keep=15.6, far=16.4)
-TRIES = 24000
-SPAN = [0.0]
+LIST_US, PLANE_US, CODE_US, HOP_US, FIRST_US, STORE_US = 0.55, 1.1, 2.6, 2.1, 1.5, 1.7
+AT = dict(x0=4.0, u=4.2, mates=5.4, dfm=12.2, h0=16.6, level=1.2, gt=2.2, z=2.9, rb=7.8, x=9.0, fh=13.7, fs=18.7,
+          far=16.4, dz=1.25, dx=1.1)
+SLOW = [dict(gather=1.5, scatter=1.65, el=1.25, issue=1.5, far=1.2, rows=0.3, share=0.35, wake=0.14),
+        dict(gather=1.0, scatter=1.0, el=1.0, issue=2.0, far=1.3, rows=0.6, share=0.15)]
+IN_TURN = ("p", "d", "e", "r0", "r1")
+TRIES, HEAT, TINY = 1000, 0.08, 2e-5
+EFFORT = [2.0, 2.0, 4.0, 2.0, 4.0, 2.0, 2.0]
+SEEDS = [[46], [54], [4], [28], [18], [22], [9]]
+LEFT = (0.1, 0.6)
+LATE = dict(x0=4.5, ub=7.0, wq=12.0, wsp=12.0, vb=14.0)
+SPAN = []
 FOUND = {}
 
 SCRATCH = {}
@@ -40,8 +56,8 @@ _b("x0 xt z fh fs gt", 4 * C, "bfloat16")
 _b("rb gp", 4 * C, "float32")
 _b("xq0 xq1 xq2 xq3 lc0 lc1 lc2 zq", C, CODE)
 _b("xs0 xs1 xs2 xs3 ls0 ls1 ls2 zs", C, "uint8")
-_b("fo0 fo1 fo2 fo3 sb0 sb1 sb2 lb0 lb1 lb2 sd0 sd1 sd2 ld0 ld1 ld2 ho0 ho1 mo rep", TC, "uint16")
-_b("sa0 sa1 sa2 la0 la1 la2", 2 * TC, "uint16")
+_b("fo0 fo1 fo2 fo3 sb0 sb1 sb2 lb0 lb1 lb2 ho0 ho1 mo rep", TC, "uint16")
+_b("sa0 sa1 sa2 la0 la1 la2", 3 * TC, "uint16")
 _b("ft tu", 7 * TC, "uint16")
 _b("wq eq", 512, CODE)
 _b("wsp eqs", 512, "uint8")
@@ -52,18 +68,20 @@ _b("ub vb", 512, "bfloat16")
 _b("fli mli", TC, "int32")
 _b("ti", 9 * TC, "int32")
 _b("tf", 20 * TC, "float32")
-_b("key0 key1 s y0 y1 y2 y3 za0 za1 zb0 kf kr st ord so top ck run lead ms nms yb nlr", C, "float32")
+_b("key0 key1 s y0 y1 y2 y3 za0 za1 za2 kf kr st so top ck run lead ms nms yb nlr", C, "float32")
 _b("fla flb", C + 16, "float32")
 _b("jc", C + 16, "bfloat16")
-_b("cand sw orb oer cv", C, "bfloat16")
+_b("cand sw orb oer cv jcs", C, "bfloat16")
 _b("both", 2 * C, "float32")
 _b("fr", 8 * C, "bfloat16")
-_b("pr", 3 * C, "bfloat16")
+_b("pr", 6 * C, "bfloat16")
 _b("row sc", NB * C, "bfloat16")
 _b("scf", NF * C, "float32")
 _b("uo", 8, "uint16")
 _b("j32", 32, "float32")
-_b("cva cvb", 16, "float32")
+_b("c16", 5 * 16, "float32")
+_b("cw", C, "float32")
+_b("m0 m1 m2", NS * TC, "float32")
 _b("cv16", 16, "bfloat16")
 _b("pi p16i", 2, "int32")
 _b("p16 p17", 2, "float32")
@@ -72,10 +90,10 @@ _b("half", 128, "bfloat16")
 _b("p0 p1 p2 p3 p4 p5 p6 p7", 512, "float32", "psum")
 TU = "ro lo w wa to eo bo".split()
 TI = "ki dj dd kl q x0i x1i a0i a1i".split()
-TF = "jt ca dfm dh i lnf rl def pef zz t m w0 w0a ta tc th td u0 u1".split()
+TF = "jt ca dfm dh i lnf rl def pef zz t m w0 w0a ta th tc td u0 u1".split()
 
 SEMAPHORES = ["cv", "cs", "ct", "cp", "lx", "lu", "lv", "lf", "lm", "lw", "lq", "lout", "sent"]
-SEMAPHORES += [k + str(r) for k in ("ac", "ad", "aa", "ab") for r in range(3)]
+SEMAPHORES += [k + str(r) for k in ("ac", "aa", "ab", "ad") for r in range(3)]
 
 
 def relay_of(src, dst, topo, k):
@@ -84,6 +102,21 @@ def relay_of(src, dst, topo, k):
     cs = [c for c in topo.cores_of(src) if topo.may_write(c, dst)]
     cs = [c for c in cs if topo.die(c) == topo.die(src)] or cs
     return cs[k % len(cs)]
+
+
+def route(T, topo, rank, r, what):
+    src = T.cores[rank]
+    for k in range(r, -1, -1):
+        via = relay_of(src, T.cores[rank ^ MASKS[k]], topo, int(what != "c0"))
+        if via is not None and (k == r or what in ASIDE):
+            return via
+    return None
+
+
+def piece(k, r, straight):
+    if k == "b":
+        return "b%d" % r, 0, TC
+    return ("a%d" % r,) + ((2 * TC, 3 * TC) if k == "d" else (0, (3 if straight else 2) * TC))
 
 
 def send(g, T, topo, src, dst, out_ap, in_ap, sem, count, last=False):
@@ -98,49 +131,50 @@ def send(g, T, topo, src, dst, out_ap, in_ap, sem, count, last=False):
     return len(e)
 
 
-def place(cost, queue, before, after, rank):
-    n = len(cost)
-    left = [len(b) for b in before]
-    ready = [0.0] * n
-    start = [0.0] * n
-    busy = {}
-    free = [(rank[i], i) for i in range(n) if not left[i]]
-    while free:
-        top = min(free)
-        free.remove(top)
-        i = top[1]
-        t, d = ready[i], cost[i]
-        if queue[i] is not None:
-            line = busy.setdefault(queue[i], [])
+def place(some, cost, queue, before, rank, start, held, soon, since=-1.0):
+    for i in some:
+        r = -1e9 if queue[i] in IN_TURN[1:] and before[i] else rank[i]
+        for d, lag in before[i]:
+            if rank[d] > r:
+                r = rank[d]
+        rank[i] = r
+    busy = {q: [x for x in line if x[0] < since or x[2] < 0] for q, line in held.items()}
+    for i in sorted(some, key=lambda i: rank[i]):
+        t, c = soon[i], cost[i]
+        for d, lag in before[i]:
+            if start[d] + lag > t:
+                t = start[d] + lag
+        if queue[i] in IN_TURN:
+            line = busy[queue[i]]
+            if line and line[-1][1] > t:
+                t = line[-1][1]
+            line.append((t, t + c, i))
+        elif queue[i] is not None:
+            line = busy[queue[i]]
             k = len(line)
             while k and line[k - 1][1] > t:
                 k -= 1
-            while k < len(line) and line[k][0] < t + d - 1e-9:
-                t = max(t, line[k][1])
+            while k < len(line) and line[k][0] < t + c - 1e-9:
+                if line[k][1] > t:
+                    t = line[k][1]
                 k += 1
-            line.insert(k, (t, t + d))
+            line.insert(k, (t, t + c, i))
         start[i] = t
-        for u, lag in after[i]:
-            if t + d + lag > ready[u]:
-                ready[u] = t + d + lag
-            left[u] -= 1
-            if not left[u]:
-                free.append((rank[u], u))
-    return start
+    return busy
 
 
-def order(ops):
+def order(ops, stages):
     n = len(ops)
     sign = tuple((o["q"], o["c"], o["tail"], tuple(sorted(o["deps"]))) for o in ops)
     if sign not in FOUND:
-        fore = [[(d, ops[d]["tail"] + WAKE) for d in sorted(o["deps"])] for o in ops]
-        fore.append([(i, ops[i]["tail"]) for i in range(n)])
+        fore = [[(d, ops[d]["c"] + ops[d]["tail"] + WAKE) for d in sorted(o["deps"])] for o in ops]
+        fore.append([(i, ops[i]["c"] + ops[i]["tail"]) for i in range(n)])
         back = [[] for _ in fore]
         for i, b in enumerate(fore):
             for d, lag in b:
                 back[d].append((i, lag))
         cost, queue = [o["c"] for o in ops] + [0.0], [o["q"] for o in ops] + [None]
-        seed = [4]
+        seed = [1]
 
         def draw():
             seed[0] = (seed[0] * 1103515245 + 12345) % 2147483648
@@ -149,43 +183,144 @@ def order(ops):
         def one(of):
             return of[int(draw() * len(of))]
 
-        def worth(start):
-            return start[n] + 2e-6 * sum(start)
+        cost2 = [[o["c"] + u["rows"] * o["k"] if isinstance(o["k"], float) else o["c"] * u[o["k"]] for o in ops] + [0.0]
+                 for u in SLOW]
+        fore2 = [[[(d, c[d] + ops[d]["tail"] * u["far"] + u.get("wake", WAKE)) for d, lag in b] for b in fore] for c, u in zip(cost2, SLOW)]
+        done = [0.0] * (n + 1)
+        slow = [done for u in SLOW]
+        held = {q: [] for q in queue if q is not None}
+        first = 0
+        for keep, end, aim, goals in stages + [(n + 1, n + 1, n, {})]:
+            some = list(range(first, end))
+            free = [i for i in some if i < n and ops[i]["other"]]
+            work = [(i, cost[i]) for i in range(first, min(keep, n)) if queue[i] in ("v", "s")]
+            ahead = [[(d, lag) for d, lag in b if d >= first] for b in fore]
+            behind = [[(u, lag - cost[i] + cost[u]) for u, lag in b if u < end] for i, b in enumerate(back)]
+            soon = [max([0.0] + [done[d] + lag for d, lag in b if d < first]) for b in fore]
+            least = max(0.0, SPAN[-1][0] - 3.5) if first else 0.0
+            tries = int(TRIES * EFFORT[len(SPAN)])
+            near = {q: [x for x in line if x[1] > least] for q, line in held.items()}
+            soon = [max(x, least) for x in soon]
+            rest, none = [0.0] * (n + 1), {q: [] for q in held}
 
-        now = best = place(cost, queue, fore, back, [o["at"] for o in ops] + [1e9])
-        for k in range(TRIES):
-            rank = list(now)
-            how = draw()
-            if how < 0.35:
-                i, s = int(draw() * n), one((-4, -2, -1, -0.5, 0.5, 1, 2, 4))
-                near, w = [i], one((1, 2, 4))
-                for u in near:
-                    for d, lag in (fore if s < 0 else back)[u]:
-                        if d not in near and abs(now[d] - now[i]) < w:
-                            near.append(d)
-                for u in near:
+            again = [i for i in range(first) if done[i] >= least] + some
+            idle = [{q: max([0.0] + [a[i] + c[i] for i in range(first) if queue[i] == q and done[i] < least]) for q in held}
+                    for a, c in zip(slow, cost2)]
+
+            def replay(turn, where, k):
+                out, line, lags, c = list(slow[k]), dict(idle[k]), fore2[k], cost2[k]
+                for i in turn:
+                    q = where[i]
+                    t = line[q] if q else 0.0
+                    for d, lag in lags[i]:
+                        if out[d] + lag > t:
+                            t = out[d] + lag
+                    out[i] = t
+                    if q:
+                        line[q] = t + c[i]
+                return out
+
+            def tried(rank, where, most=1e9, old=None):
+                if old is None:
+                    start = list(done)
+                    busy = place(some, cost, where, ahead, rank, start, near, soon)
+                else:
+                    start = list(old[1])
+                    since = min([min(rank[i], start[i]) for i in some if rank[i] != start[i] or where[i] != old[2][i]] + [1e9])
+                    busy = place([i for i in some if start[i] >= since], cost, where, ahead, rank, start, old[5], soon, since)
+                plain = worth(start, 1.0)
+                if plain > most:
+                    return 1e9, start, where, None, plain, busy
+                turn = sorted(again, key=lambda i: start[i])
+                other = [replay(turn, where, k) for k in range(len(SLOW))]
+                return (plain + sum(u["share"] * (worth(a, u["el"]) - plain) for a, u in zip(other, SLOW))
+                        + TINY * sum(start[first:end]), start, where, other, plain, busy)
+
+            def worth(start, k):
+                t = start[aim]
+                over = [w * max(0.0, start[i] - t - k * slack) for i, (w, slack) in goals.items()] + [0.0]
+                return t + max(over) + 0.03 * sum(over) + LEFT[len(SPAN) % 2] * sum(c for i, c in work if start[i] > t)
+
+            def turned(start, where):
+                late = list(done)
+                place(some[::-1], cost, where, behind, [-(start[i] + cost[i]) for i in range(n + 1)], late, none, rest)
+                return tried([-(late[i] + cost[i]) for i in range(n + 1)], where)
+
+            def blocks(start, where):
+                ends = {(where[i], round(start[i] + cost[i], 6)): i for i in some if where[i]}
+                out, seen = [], set()
+                todo = [aim] + [i for i, (w, slack) in goals.items() if start[i] > start[aim] + slack]
+                while todo:
+                    i = todo.pop()
+                    if i not in seen:
+                        seen.add(i)
+                        tight = [d for d, lag in ahead[i] if start[d] + lag > start[i] - 1e-6]
+                        d = ends.get((where[i], round(start[i], 6)))
+                        if not tight and d is not None:
+                            out.append((d, i))
+                            tight = [d]
+                        todo += tight
+                return out
+
+            def with_kin(i, kin, rank, near_enough, s):
+                group = [i]
+                for u in group:
+                    group += [d for d, lag in kin[u] if d not in group and near_enough(rank[d])]
+                for u in set(group):
                     rank[u] += s
-            elif how < 0.7:
-                for _ in range(one((1, 2, 5))):
-                    rank[int(draw() * n)] += one((-4, -2, -1, -0.5, -0.2, 0.2, 0.5, 1, 2, 4))
-            else:
-                a, w, s = draw() * now[n], one((1, 2, 4)), one((0.2, 0.6, 1.2))
-                for i in range(n):
-                    if a <= rank[i] < a + w:
-                        rank[i] += s * (draw() - 0.5)
-            new = place(cost, queue, fore, back, rank)
-            if draw() < 0.03:
-                late = place(cost, queue, back, fore, [-(new[i] + cost[i]) for i in range(n + 1)])
-                early = place(cost, queue, fore, back, [-(late[i] + cost[i]) for i in range(n + 1)])
-                if early[n] <= new[n]:
-                    new = early
-            heat = 0.15 * (1.0 - k / TRIES) + 0.003
-            if worth(new) <= worth(now) or draw() < math.exp((worth(now) - worth(new)) / heat):
-                now = new
-                if worth(now) < worth(best):
-                    best = now
-        SPAN[0] = best[n]
-        FOUND[sign] = sorted(range(n), key=lambda i: (best[i], i))
+
+            now = tried([o["at"] for o in ops] + [1e9], queue)
+            guess = best = min(now, turned(now[1], queue))
+            seeds = SEEDS[len(SPAN)] + [0]
+            RUNS = len(seeds)
+            for k in range(tries * RUNS):
+                run, k = divmod(k, tries)
+                if k == 0:
+                    now, pairs = (best if run == RUNS - 1 else guess), None
+                    seed[0] = 7919 * seeds[run] + 1
+                rank, where, how = list(now[1]), now[2], draw()
+                if pairs is None:
+                    pairs = blocks(now[1], where)
+                a, b = one(pairs) if pairs else (first, first)
+                if how < 0.2:
+                    i = one((a, b)) if how < 0.12 else one(free)
+                    if i in free:
+                        where = list(where)
+                        where[i] = "s" if where[i] == "v" else "v"
+                    rank[i] += one((-0.5, 0.0, 0.0, 0.5))
+                elif how < 0.4:
+                    rank[a] = rank[b] + one((0.01, 0.3, 0.6, 1.2, 2.5))
+                elif how < 0.55:
+                    with_kin(b, ahead, rank, lambda t, t0=rank[a] - 1.0: t > t0, rank[a] - rank[b] - 0.01)
+                elif how < 0.72:
+                    i, s, w = one(some), one((-4, -2, -1, -0.5, 0.5, 1, 2, 4)), one((1, 2, 4))
+                    with_kin(i, ahead if s < 0 else behind, rank, lambda t, t0=rank[i], w=w: abs(t - t0) < w, s)
+                elif how < 0.86:
+                    for _ in range(one((1, 2, 3))):
+                        rank[one(some)] += one((-4, -2, -1, -0.5, -0.2, 0.2, 0.5, 1, 2, 4))
+                else:
+                    a, w, s = rank[one(some)], one((1, 2, 4)), one((0.2, 0.6, 1.2))
+                    for i in some:
+                        if a <= rank[i] < a + w:
+                            rank[i] += s * (draw() - 0.5)
+                heat = HEAT * (1.0 - k / tries) * (0.3 if run == RUNS - 1 else 1.0) + 0.003
+                room = -heat * math.log(draw() + 1e-9)
+                new = tried(rank, where, now[4] + room + 0.2, now)
+                if draw() < 0.03:
+                    new = min(new, turned(new[1], where), key=lambda x: x[0])
+                if new[0] <= now[0] + room:
+                    now, pairs = new, None
+                    if now[0] < best[0]:
+                        best = now
+            done, queue, slow = best[1:4]
+            for i in range(first, keep):
+                if queue[i] is not None:
+                    held[queue[i]].append((done[i], done[i] + cost[i], -1))
+            for q in held:
+                held[q].sort()
+            SPAN.append((round(done[aim], 2), round(slow[0][aim], 2), round(slow[1][aim], 2)))
+            first = keep
+        FOUND[sign] = [(i, queue[i]) for i in sorted(range(n), key=lambda i: (done[i], i))]
     return FOUND[sign]
 
 
@@ -197,7 +332,7 @@ def rank_program(g, core, T, topo):
     queues = {"v": g.vector, "s": g.scalar, "t": g.tensor, "p": g, "y": g.sync}
     own = {"v": "cv", "s": "cs", "t": "ct", "p": "cp"}
     V, S, P = g.vector, g.scalar, g.tensor
-    ops = []
+    ops, stages = [], []
     clock = [0.0, 0.0]
     acc = {}
 
@@ -206,8 +341,21 @@ def rank_program(g, core, T, topo):
         if base is not None:
             clock[0] = base
 
+    def users(names):
+        out = set()
+        for r in names:
+            a = acc.setdefault(r, [None, []])
+            out.update(a[1])
+            if a[0] is not None:
+                out.add(a[0])
+        return out
+
+    more = set()
+    picks = set()
+
     def op(qn, rd, wr, fn, cost, sem=None, inc=1, tail=0.0, ev=None):
-        deps = set()
+        deps = set(more)
+        more.clear()
         me = len(ops)
         for r in rd:
             a = acc.setdefault(r, [None, []])
@@ -224,12 +372,16 @@ def rank_program(g, core, T, topo):
             acc[r] = [me, []]
         deps.discard(me)
         plan = max([clock[0] + clock[1]] + [ops[d]["at"] + ops[d]["c"] + ops[d]["tail"] + WAKE for d in deps])
-        ops.append(dict(q=qn, c=cost, tail=tail, at=plan, deps=deps, fn=fn, sem=sem or own.get(qn), inc=inc, ev=ev))
+        k = "gather" if cost in picks else "scatter" if cost > 1.0 and qn == "v" else "el" if qn in own else "far"
+        ops.append(dict(q=qn, c=cost, k=k, tail=tail, at=plan, deps=deps, fn=fn, sem=sem or own.get(qn), inc=inc, ev=ev,
+                        other=None))
 
     def emit():
         total, know = {}, {k: {} for k in queues}
-        for i in order(ops):
+        for i, qn in order(ops, stages):
             o = ops[i]
+            if qn != o["q"]:
+                o.update(q=qn, fn=o["other"], sem=own[qn])
             if o["fn"] is None:
                 o["knows"] = {}
                 continue
@@ -265,6 +417,7 @@ def rank_program(g, core, T, topo):
         return max(n * k, 64) * EL
 
     def ga(n):
+        picks.add(0.055 + n * GATHER)
         return 0.055 + n * GATHER
 
     def R(name, lo=None, hi=None, tag=None):
@@ -302,24 +455,39 @@ def rank_program(g, core, T, topo):
     def cp(out, a, c=None):
         op("v", a[1], out[1], lambda: V.tensor_copy(out[0], a[0]), el(TC) if c is None else c)
 
-    def act(out, a, c, scale=1.0, bias=0.0, func=IDENT):
+    def act(out, a, c, scale=1.0, bias=0.0):
         scale, bias = num(scale), num(bias)
         if not scale[1] and not bias[1] and scale[0] == 1.0 and bias[0] == 0.0:
             op("s", a[1], out[1], lambda: S.activation(out[0], a[0], COPY), c)
+            ops[-1]["other"] = lambda: V.tensor_copy(out[0], a[0])
         else:
             op("s", a[1] + scale[1] + bias[1], out[1],
-               lambda: S.activation(out[0], a[0], func, bias=bias[0], scale=scale[0]), c)
+               lambda: S.activation(out[0], a[0], IDENT, bias=bias[0], scale=scale[0]), c)
+            ops[-1]["other"] = lambda: V.tensor_scalar(out[0], a[0], scale[0], bias[0], A.mult, A.add)
 
     def lin(out, a, scale, bias):
-        if out[1][0] in SMALL_S:
-            act(out, a, el(TC), scale, bias)
-        else:
-            ts(out, a, scale, A.mult, bias, A.add)
+        act(out, a, el(TC), scale, bias)
 
     def col(k):
         return T.col[:, k:k + 1], ["col%d" % k]
 
-    DOWN, DOWN_M, LESS_M, LESS, LESS_2 = range(5)
+    def step(buf, k):
+        return T[buf][:, k:NS * TC:NS], ["%s%d" % (buf, k)]
+
+    def two(name, k=0):
+        return T[name][:, k * C:(k + 1) * C], ["%s%da" % (name, k), "%s%db" % (name, k)]
+
+    def shared(out, win, off, cut, scale=1.0, bias=0.0):
+        if cut == TC:
+            act(out, by(win, off), ga(C), scale, bias)
+        else:
+            before = users(out[1])
+            more.update(before)
+            act((out[0][:, 0:16 * cut], out[1][:1]), by(win, (off[0][:, 0:cut], off[1])), ga(16 * cut), scale, bias)
+            more.update(before)
+            act((out[0][:, 16 * cut:C], out[1][1:]), by(win, (off[0][:, cut:TC], off[1])), ga(C - 16 * cut), scale, bias)
+
+    DOWN, LESS_M, LESS, LESS_2, DROP = range(5)
     turn = {"row": 0, "sc": 0, "scf": 0}
 
     def fresh(name, n):
@@ -336,8 +504,14 @@ def rank_program(g, core, T, topo):
         scan(out, R("cv"), row, 0.0, A.mult, A.add, el(C, 1.0 if wide else 0.5))
         return T[name][:, k * C + 15:(k + 1) * C:16], out[1]
 
-    def offsets(out, view):
-        ts(out, view, col(DOWN), A.mult, float(H), A.add)
+    def lifted(row):
+        k = fresh("scf", NF)
+        out = slot("scf", k)
+        scan(out, R("cw"), row, 0.0, A.add, A.max, el(C))
+        return T.scf[:, k * C + 15:(k + 1) * C:16], out[1]
+
+    def offsets(out, view, by_=DOWN):
+        ts(out, view, col(by_), A.mult, float(H), A.add)
 
     def spare():
         return slot("row", fresh("row", NB))
@@ -349,9 +523,10 @@ def rank_program(g, core, T, topo):
         op("v", rd, wr, lambda: V.quantize_mx(q, s, src), 0.015 + 0.26e-3 * n)
 
     def load(qn, out, in_, res, sem, tail=2.2):
-        op(qn, [], [res], lambda: queues[qn].dma_start(out=out, in_=in_), 0.1, sem, 16, tail)
+        queues[qn].dma_start(out=out, in_=in_).then_inc(T.sem[sem], 16)
+        op(None, [], [res], None, 0.0, None, 0, tail, (sem, 16))
 
-    def store(qn, out, in_, res, us=0.1):
+    def store(qn, out, in_, res, us=0.05):
         tag = "store%d" % len(ops)
         op(qn, res, [tag], lambda: queues[qn].dma_start(out=out, in_=in_), 0.1, "lout", 16)
         op("d", [tag], [], None, us, None, 0, STORE_US)
@@ -359,28 +534,36 @@ def rank_program(g, core, T, topo):
     def out_of(out, bank, scale=1.0, n=C):
         act((out[0], out[1] + [bank]), (T[bank][:, 0:n], []), el(n), scale)
 
-    sends = [0]
+    sends, sent = [0], {}
 
     def to_partner(r, bufs, sem, count, land):
         dst = T.cores[rank ^ MASKS[r]]
 
-        def go(hop, o, i, lane):
-            sends[0] += send(g, T, topo, core, hop, o, i, sem, count, lane == 0)
+        straight = topo.may_write(core, dst)
+
+        def go(hop, o, i):
+            sends[0] += send(g, T, topo, core, hop, o, i, sem, count if straight else NEAR, hop != dst)
 
         for k, (o, i, res, us, lane) in enumerate(bufs):
-            via = relay_of(core, dst, topo, lane)
+            via = route(T, topo, rank, r, sem[1] + str(k))
             hop = dst if via is None else via
             way = "way%s%d" % (sem, k)
-            op("p", res, [way, "lane%d" % lane], lambda hop=hop, o=o, i=i, lane=lane: go(hop, o, i, lane), 0.3)
+            op("p", res, [way] + ["lane%d" % lane] * (via is not None), lambda hop=hop, o=o, i=i: go(hop, o, i), 0.3)
             ops[-1]["sem"] = None
-            op("d" if via is None or lane else "e", [way], [way], None, us, None, 0, HOP_US)
+            part = 1.0 if straight else 0.6
+            op("e" if straight and via is not None else "d", [way], [way], None, us * part, None, 0,
+               HOP_US + 2.0 * (sem == "ac0"))
+            ops[-1]["k"], ops[-2]["k"] = part, "issue"
             if via is not None:
-                op("r%d" % lane, [way], [way], None, us + 0.3 + FIRST_US * (sem[1] == "c"), None, 0, HOP_US)
+                op("r%d" % lane, [way], [way], None, us + 0.3 + FIRST_US * (sem == "ac1"), None, 0, HOP_US)
+                ops[-1]["k"] = 1.4
         op(None, ["way%s%d" % (sem, k) for k in range(len(bufs))], [land], None, 0.0, None, 0, 0.0, (sem, count * len(bufs)))
+        sent[sem] = len(ops) - 1
 
     def send_list(r, k, res):
-        a, b = "l%s%d" % (k, r), "s%s%d" % (k, r)
-        to_partner(r, [(T[a][:, :], T[b][:, :], res, LIST_US, 1)], "a%s%d" % (k, r), NL, a)
+        name, lo, hi = piece(k, r, topo.may_write(core, T.cores[rank ^ MASKS[r]]))
+        to_partner(r, [(T["l" + name][:, lo:hi], T["s" + name][:, lo:hi], res, LIST_US, 1)], "a%s%d" % (k, r), NL,
+                   "l%s%d" % (k, r))
 
     def send_codes(r):
         q = "xq%d" % r
@@ -388,12 +571,12 @@ def rank_program(g, core, T, topo):
                        (T["ls%d" % r][:, :], T["xs%d" % r][:, :], [q], PLANE_US, 1)], "ac%d" % r, NE, "lc%d" % r)
 
     load("y", T.fli[:, :], T.fl[:, :], "fli", "lf")
-    load("s", T.x0[:, :], T.x[:, :], "x0", "lx", 3.5)
     load("y", T.mli[:, :], T.ml[:, :], "mli", "lm")
-    load("y", T.ub[:, :], T.u[:, :], "ub", "lu", 2.9)
-    load("y", T.wq[:, :].bitcast(dt.uint8), T.wc[:, :], "wq", "lw", 3.5)
-    load("y", T.wsp[:, :], T.ws[:, :], "wsp", "lq")
-    load("y", T.vb[:, :], T.v[:, :], "vb", "lv", 2.9)
+    load("y", T.x0[:, :], T.x[:, :], "x0", "lx", LATE["x0"])
+    load("y", T.ub[:, :], T.u[:, :], "ub", "lu", LATE["ub"])
+    load("y", T.wq[:, :].bitcast(dt.uint8), T.wc[:, :], "wq", "lw", LATE["wq"])
+    load("y", T.wsp[:, :], T.ws[:, :], "wsp", "lq", LATE["wsp"])
+    load("y", T.vb[:, :], T.v[:, :], "vb", "lv", LATE["vb"])
 
     def iota(name, pattern, base, mult, n, flag=True):
         if flag:
@@ -408,18 +591,28 @@ def rank_program(g, core, T, topo):
     jc = R("jc")
     act(R("key0"), R("jc", 0, C), el(C), M, M * H + C - 1.0)
     act(R("key1"), R("jc", 0, C), el(C), M, M * H + C - 2.0)
+    act(R("jcs"), R("jc", 0, C), el(C), -1.0 / M)
     p16 = (T.p16[:, 0:1], ["p16"])
     ts(R("p16i"), R("pi"), 15, A.bitwise_and)
     cp(R("p16"), R("p16i"))
     ts(R("p17"), R("p16i"), 1.0, A.add)
-    ts(R("cva"), R("j32", 0, 16), p16, A.not_equal)
-    ts(R("cvb"), R("j32", 0, 16), (T.p17[:, 0:1], ["p17"]), A.is_equal, UP, A.mult)
-    tt(R("cv16"), R("cva"), R("cvb"), A.max)
+    c16 = [slot("c16", k, 16) for k in range(5)]
+    ts(c16[0], R("j32", 0, 16), p16, A.not_equal)
+    ts(c16[1], R("j32", 0, 16), (T.p17[:, 0:1], ["p17"]), A.is_equal, UP, A.mult)
+    tt(R("cv16"), c16[0], c16[1], A.max)
     ts(R("rep"), R("j32", 0, TC), 0.0, A.mult, p16, A.add)
     act(R("cv"), by(R("cv16"), R("rep")), ga(C))
     ts(col(DOWN), p16, 15.0, A.is_equal, 1.0 / UP, A.max)
-    for k, f in ((DOWN_M, 1.0 / M), (LESS_M, -1.0 / M), (LESS, -1.0), (LESS_2, -2.0)):
+    for k, f in ((LESS_M, -M), (LESS, -M * M), (LESS_2, -2.0)):
         act(col(k), col(DOWN), el(1), f)
+    ts(c16[2], R("j32", 0, 16), p16, A.is_equal, -BIG, A.mult)
+    ts(c16[3], R("j32", 0, 16), (T.p17[:, 0:1], ["p17"]), A.is_equal, LIFT, A.mult)
+    tt(c16[4], c16[2], c16[3], A.add)
+    act(R("cw"), by(c16[4], R("rep")), ga(C))
+    ts(col(DROP), p16, 15.0, A.is_lt, -LIFT, A.mult)
+    for buf, k, f in (("m0", 0, 0.0), ("m0", 2, 1.0), ("m0", 3, 1.0), ("m0", 5, 1.0), ("m0", 6, 1.0),
+                      ("m1", 1, -0.499), ("m1", 2, ROUND), ("m1", 3, -ROUND)):
+        act(step(buf, k), R("j32", 0, TC), el(TC), 0.0, f)
     act(R("fla", 0, 1, "fla0"), R("j32", 0, 1), el(1))
     cp(R("fo0"), R("fli"))
     op("v", [], ["et"], lambda: V.memset(T.et[:, :], 0.0), el(2048, 0.5))
@@ -428,8 +621,8 @@ def rank_program(g, core, T, topo):
     for b in range(4):
         op("p", ["half", "et"], ["et%d" % b], lambda b=b: g.affine_select(
             T.et[:, 512 * b + b:512 * b + 512:4], T.half[:, :], [[-1, 128]], A.is_equal, 0.0, 0, 1), 0.2 + 256 * EL)
-    at(AT["eq"])
-    quant(T.eq[:, :], T.eqs[:, :], ["et", "et0", "et1", "et2", "et3"], ["eq"], T.et[:, :], 2048)
+        quant(T.eq[:, 128 * b:128 * b + 128], T.eqs[:, 128 * b:128 * b + 128], ["et", "et%d" % b], ["eq%d" % b],
+              T.et[:, 512 * b:512 * b + 512], 512)
     at(AT["x0"])
     quant(T.xq0[:, :], T.xs0[:, :], ["x0"], ["xq0"], T.x0[:, :], 4 * C)
     send_codes(0)
@@ -443,7 +636,7 @@ def rank_program(g, core, T, topo):
     cp(R("mo"), R("mli"))
     ts(tab("jt"), R("j32", 0, TC), 16.0, A.mult, p16, A.add)
     tt(tab("u0"), R("mli"), tab("jt"), A.is_lt)
-    ts(tab("ca"), tab("u0"), float(C), A.mult)
+    ts(step("m1", 6), tab("u0"), float(C), A.mult)
 
     def difference(out, view, minus):
         offsets(tab("u0"), view)
@@ -455,173 +648,194 @@ def rank_program(g, core, T, topo):
         xq, xs, xr = T["xq%d" % r], T["xs%d" % r], ["xq%d" % r]
         fo, nfo = R("fo%d" % r), R("fo%d" % (r + 1))
         ho, nho = R("ho%d" % (r % 2)), R("ho%d" % ((r + 1) % 2))
-        tabs = [fo] + [slot("ft", k, TC) for k in range(6)]
+        powers, steps = POWERS, STEPS
+        tabs, have = {1: fo}, 1
         at(2.1)
-        act(slot("fr", 0), by(jc, fo), ga(C))
-        for k in range(1, 8):
+        shared(two("fr", 0), jc, fo, TC if r else CUT_F)
+        for k, n in enumerate(powers, 1):
             at(1.6 + AT["level"] * min(k, 6))
-            act(slot("fr", k), by(slot("fr", k - 1), tabs[min(k - 1, 5)]), ga(C))
-            if k != 6:
-                offsets(tabs[min(k, 6)], table_of(slot("fr", k)))
+            act(two("fr", k), by(two("fr", k - 1), tabs[n]), ga(C))
+            have += n
+            if have in powers or have in [a for a, b in steps]:
+                tabs[have] = slot("ft", len(tabs) - 1, TC)
+                offsets(tabs[have], table_of(two("fr", k)))
         if r == 0:
             at(AT["dfm"])
             a = spare()
-            act(a, by(slot("fr", 0), R("mo")), ga(C))
+            act(a, by(two("fr", 0), R("mo")), ga(C))
             difference(tab("dfm"), table_of(a), R("fli"))
         at(0.0)
-        cur, k = "key0", 0
-        for level, (rad, n) in enumerate(LEVELS):
-            base = cur
-            for i in range(rad - 1):
-                zz = "key1" if level == 0 else "za%d" % (level % 2) if i == 0 else "zb0"
-                if level:
-                    act(R(zz), R(base), el(C), 1.0, float(-n * (i + 1)))
-                d = "y%d" % (k % 4)
-                k += 1
-                tt(R(d), by(R(cur), tabs[level]), R(zz), A.min, ga(C))
-                cur = d
-        key = R(cur)
-        v = table_of(key, True)
-        ts(tab("ro"), v, col(DOWN_M), A.mult)
-        ts(tab("ki"), v, col(DOWN), A.mult)
-        ts(tab("dj"), tab("ki"), int(M) - 1, A.bitwise_and)
-        cp(R("sd%d" % r), tab("dj"))
-        send_list(r, "d", ["sd%d" % r])
+        keys, have = {1: R("key0")}, 1
+        for k, (n, old) in enumerate(steps):
+            zz = R("za%d" % (k % 3)) if k else R("key1")
+            if k:
+                act(zz, keys[old], el(C), 1.0, float(old - have - n))
+            keys[have + n] = R("y%d" % (k % 4))
+            tt(keys[have + n], by(keys[have], tabs[n]), zz, A.min, ga(C))
+            have += n
+        key = keys[C]
+        v = lifted(key)
+        ts(tab("ro"), v, col(DROP), A.add, 1.0 / M, A.mult)
+        ts(tab("t"), v, M * ROUND, A.add, M * ROUND, A.subtract)
         sa = "sa%d" % r
+        dj = R(sa, 2 * TC, 3 * TC, sa + "d")
+        tt(dj, v, tab("t"), A.subtract)
+        handed = not topo.may_write(core, T.cores[rank ^ MASKS[r]])
+        if handed:
+            send_list(r, "d", dj[1])
         po, ln, eo = R(sa, 0, TC), R(sa, TC, 2 * TC, sa + "n"), tab("eo")
-        act(R("kf"), by(key, fo), ga(C), 1.0, M + 1.0)
-        scan(R("st"), R("kf"), key, -1.0 - M - H, A.add, A.subtract, el(C))
+        shared(two("kf"), key, fo, CUT_KF, 1.0, M + 1.0)
+        scan(R("st"), two("kf"), key, -1.0 - M - H * (not PLAIN_A[r]), A.add, A.subtract, el(C))
         a, drow = spare(), spare()
-        tt(a, by(R("st"), tab("ro")), key, A.subtract, ga(C))
-        offsets(po, table_of(a))
-        act(R("kr"), by(R("kf"), tab("ro")), ga(C))
-        tt(tab("u0"), table_of(R("kr"), True), v, A.subtract)
-        ts(tab("dd"), tab("u0"), col(DOWN), A.mult, -M, A.add)
-        tt(ln, tab("dd"), tab("dj"), A.add)
-        send_list(r, "a", po[1] + ln[1])
-        tt(eo, po, tab("dj"), A.add)
-        act(drow, by(jc, R("sd%d" % r)), ga(C))
-        op("v", ["jc", sa], ["orb"], lambda po=po: V.tensor_copy(T.orb[:, :].indirect(po[0]), T.jc[:, 0:C]),
+        if PLAIN_A[r]:
+            act(two("ck"), by(R("st"), tab("ro")), ga(C))
+            tt(po, lifted(two("ck")), v, A.subtract)
+        else:
+            tt(a, by(R("st"), tab("ro")), key, A.subtract, ga(C))
+            offsets(po, table_of(a))
+        act(R("kr"), by(two("kf"), tab("ro")), ga(C), 1.0, -M)
+        tt(ln, lifted(R("kr")), tab("t"), A.subtract)
+        send_list(r, "a", po[1] + ln[1] + dj[1] * (not handed))
+        tt(eo, po, dj, A.add)
+        act(drow, by(jc, dj), ga(C))
+        op("v", ["jcs", sa], ["orb"], lambda po=po: V.tensor_copy(T.orb[:, :].indirect(po[0]), T.jcs[:, :]),
            0.05 + C * SCATTER)
-        act(R("ord"), R("orb"), el(C), -M, M * (C - H))
         oo = R("sb%d" % r)
-        offsets(oo, table_of(R("orb")))
+        offsets(oo, table_of(R("orb")), LESS_M)
         send_list(r, "b", oo[1])
+        at(0.0)
+        mm("p4", T.uk[:, :], T.uks[:, :], ["uk", "uks"], xq[:, :], xs[:, :], xr)
+        out_of(R("s"), "p4", -1.0)
+        act(R("so"), by(R("s"), oo), ga(C))
+        ends = by(drow, oo)
+        op("s", ends[1], ["fla"], lambda ends=ends: S.activation(T.fla[:, 1:C + 1], ends[0], RELU, bias=BIG * (1 - H),
+                                                                 scale=-BIG), ga(C))
+        ops[-1]["other"] = lambda ends=ends: V.tensor_scalar(T.fla[:, 1:C + 1], ends[0], float(-H), BIG, A.is_equal, A.mult)
+        fla = (T.fla[:, 0:C], ["fla", "fla0"])
+
+        def unpack(name, first, q, s, rd):
+            at(AT[name] - 6.0 * (r == 0))
+            for b in range(4):
+                mm("p%d" % (first + b), T.eq[:, 128 * b:128 * b + 128], T.eqs[:, 128 * b:128 * b + 128], ["eq%d" % b], q, s, rd)
+                out_of(slot(name, b), "p%d" % (first + b))
+
+        goals = {sent[k + str(r)]: w for k, w in NEEDED.items()}
+        if r == 0:
+            unpack("fh", 0, xq[:, :], xs[:, :], xr)
+            goals.update({i: (0.3, -0.5) for i in range(len(ops) - 7, len(ops), 2)})
+            goals[sent["ac0"]] = (0.1, -1.5)
+        keep = len(ops)
+        at(0.0)
+        scan(R("top"), fla, R("so"), BIG, A.add, A.min, el(C))
+        stages.append((keep, len(ops), len(ops) - 1, goals))
         if r == 0:
             at(AT["h0"])
+            tt(tab("dd"), ln, dj, A.subtract)
             ts(tab("u0"), tab("dd"), 1.0, A.is_equal)
             tt(tab("u1"), tab("u0"), ln, A.mult)
             ts(tab("u0"), po, -1.0, A.add)
             tt(tab("bo"), tab("u0"), tab("u1"), A.add)
             a = spare()
             act(a, by(R("orb"), tab("bo")), ga(C))
-            offsets(ho, table_of(a))
+            offsets(ho, table_of(a), LESS_M)
             a, b = spare(), spare()
             act(a, by(jc, R("mo")), ga(C))
             act(b, by(a, ho), ga(C))
             difference(tab("dh"), table_of(b), ho)
 
-        at(0.0)
-        mm("p4", T.uk[:, :], T.uks[:, :], ["uk", "uks"], xq[:, :], xs[:, :], xr)
-        out_of(R("s"), "p4", -1.0)
-        at(AT["fh"])
-        for b in range(4):
-            mm("p%d" % b, T.eq[:, 128 * b:128 * b + 128], T.eqs[:, 128 * b:128 * b + 128], ["eq"], xq[:, :], xs[:, :], xr)
-            out_of(slot("fh", b), "p%d" % b)
-        at(AT["fs"])
-        for b in range(4):
-            mm("p%d" % (4 + b), T.eq[:, 128 * b:128 * b + 128], T.eqs[:, 128 * b:128 * b + 128], ["eq"],
-               T["lc%d" % r][:, :], T["ls%d" % r][:, :], ["lc%d" % r])
-            out_of(slot("fs", b), "p%d" % (4 + b))
+        else:
+            unpack("fh", 0, xq[:, :], xs[:, :], xr)
+            lin(tab("tc", 2), tab("ta", 2), col(LESS_2), 0.0)
+            tt(tab("dfm", 2), tab("tc", 2), tab("dfm", 2), A.add)
 
+        unpack("fs", 4, T["lc%d" % r][:, :], T["ls%d" % r][:, :], ["lc%d" % r])
         at(0.0)
-        cp(R("so"), by(R("s"), oo), ga(C))
-        act(R("fla", 1, C + 1), by(drow, oo), ga(C), -BIG, BIG * (1 - H), RELU)
-        fla = (T.fla[:, 0:C], ["fla", "fla0"])
-        act(R("flb", 0, C), fla, el(C), -1.0, -1.0)
-        scan(R("top"), fla, R("so"), BIG, A.add, A.min, el(C))
+        act(R("flb", 0, C), fla, el(C), -1.0, -1.0 / M / M)
         tt(R("cand"), by(R("top"), eo), R("s"), A.is_equal, ga(C))
-        tt(R("ck"), by(R("cand"), oo), R("ord"), A.mult, ga(C))
-        scan(R("run"), R("flb", 0, C), R("ck"), 0.0, A.add, A.max, el(C))
-        cp(R("lead"), by(R("run"), eo), ga(C))
-        v = table_of(R("lead"), True)
-        ts(tab("lo"), v, col(LESS_M), A.mult, float(C), A.add)
-        ts(tab("kl"), v, col(LESS), A.mult, M * C, A.add)
-        tt(tab("x0i"), tab("kl"), tab("dj"), A.subtract)
-        tt(tab("x1i"), tab("kl"), tab("dd"), A.add)
+        tt(two("ck"), by(R("cand"), oo), R("orb"), A.add, ga(C))
+        scan(R("run"), R("flb", 0, C), two("ck"), 0.0, A.add, A.max, el(C))
+        shared(two("lead"), R("run"), eo, CUT_LEAD)
+        v = table_of(two("lead"), True)
+        ts(tab("lo"), v, col(LESS_M), A.mult, M + H, A.add)
+        ts(tab("kl"), v, col(LESS), A.mult, M * (M + H), A.add)
+        tt(tab("x0i"), tab("kl"), dj, A.subtract)
+        tt(tab("x1i"), tab("x0i"), ln, A.add)
         ts(tab("a0i", 2), tab("x0i", 2), int(M) - 1, A.bitwise_and)
-        tt(tab("i"), tab("a0i"), tab("a1i"), A.min)
+        tt(step("m1", 5), tab("a0i"), tab("a1i"), A.min)
 
         at(AT["far"])
         la, oe = "la%d" % r, R("lb%d" % r)
-        for k, off in ((2, R("ld%d" % r)), (1, R(la, TC, 2 * TC)), (0, R(la, 0, TC))):
-            act(slot("pr", k), by(jc, off), ga(C))
+        far_d = R(la, 2 * TC, 3 * TC, "ld%d" % r if handed else la)
+        for k, off in ((1, R(la, TC, 2 * TC)), (2, far_d), (0, R(la, 0, TC))):
+            shared(two("pr", k), jc, off, CUT_ROW if handed and k < 2 else TC)
         act(slot("both", 1), by(R("s"), oe), ga(C))
         act(slot("both", 0), slot("both", 1), el(C), -1.0)
         act(R("oer"), by(jc, oe), ga(C))
         at(0.0)
-        for k, name, home in ((1, "lnf", False), (2, "def", True), (0, "pef", False)):
-            a = spare()
-            if home:
-                cp(a, by(slot("pr", k), tab("lo")), ga(C))
-            else:
-                act(a, by(slot("pr", k), tab("lo")), ga(C))
-            lin(tab(name), table_of(a), col(DOWN), float(H))
-        op("v", ["lnf"], ["rl"], lambda: V.reciprocal(tab("rl")[0], tab("lnf")[0]), 0.32)
-        tt(tab("zz"), tab("def"), tab("i"), A.subtract)
-        tt(tab("t"), tab("zz"), tab("rl"), A.mult)
-        ts(tab("q"), tab("t"), -0.499, A.add)
-        tt(tab("m"), tab("q"), tab("lnf"), A.mult)
-        tt(tab("w0"), tab("pef"), tab("i"), A.add)
-        tt(tab("w0a"), tab("w0"), tab("ca"), A.add)
-        tt(tab("wa"), tab("w0a"), tab("m"), A.add)
+        for k, name in ((1, step("m0", 4)), (2, tab("def")), (0, step("m1", 4))):
+            a = two("pr", 3 + k)
+            act(a, by(two("pr", k), tab("lo")), ga(C))
+            lin(name, table_of(a), col(DOWN), float(H))
+        op("v", ["m04"], ["m01"], lambda: V.reciprocal(step("m0", 1)[0], step("m0", 4)[0]), 0.32)
+        tt(step("m1", 0), tab("def"), step("m1", 5), A.subtract)
+        scan((T.m2[:, :], ["m2"]), (T.m0[:, :], ["m0%d" % k for k in range(NS)]),
+             (T.m1[:, :], ["m1%d" % k for k in range(NS)]), 0.0, A.mult, A.add, el(NS * TC))
+        cp(tab("wa"), (step("m2", 6)[0], ["m2"]))
 
         at(0.0, ops[-1]["at"])
         both = (T.both[:, :], ["both0", "both1"])
         act(R("nms"), by(both, tab("wa")), ga(C), -1.0)
-        cp(R("ms"), by(both, tab("wa")), ga(C))
+        act(R("ms"), by(both, tab("wa")), ga(C))
         tt(R("sw"), by(R("nms"), R("mo")), R("ms"), A.is_gt, ga(C))
         tt(tab("ta"), table_of(R("sw")), tab("dfm"), A.mult)
         tt(nfo, tab("ta"), fo, A.add)
-        tt(tab("w"), tab("w0"), tab("m"), A.add)
+        goal = len(ops) - 1
+        cp(tab("w"), (step("m2", 5)[0], ["m2"]))
         a = spare()
         act(a, by(R("oer"), tab("w")), ga(C))
         offsets(tab("to"), table_of(a))
+        keep = len(ops)
         a = spare()
         act(a, by(R("sw"), ho), ga(C))
         tt(tab("th"), table_of(a), tab("dh"), A.mult)
         tt(nho, tab("th"), ho, A.add)
-        if not last:
-            at(AT["keep"])
-            lin(tab("tc"), tab("ta"), col(LESS_2), 0.0)
-            tt(tab("dfm"), tab("tc"), tab("dfm"), A.add)
-            lin(tab("td"), tab("th"), col(LESS_2), 0.0)
-            tt(tab("dh"), tab("td"), tab("dh"), A.add)
 
-        for b in range(4):
-            at(AT["gt"] + 0.5 * b)
-            act(slot("gt", b), by(slot("fs", b), tab("to")), ga(C))
-            at(AT["z"] + 0.5 * b)
-            tt((T.z[:, b:4 * C:4], ["z%d" % b]), by(slot("fh", b), nfo), slot("gt", b), A.add, ga(C))
-        quant(T.zq[:, :], T.zs[:, :], ["z0", "z1", "z2", "z3"], ["zq"], T.z[:, :], 4 * C)
-        for b in range(4):
-            at(AT["rb"] + 0.5 * b)
-            bank = "p%d" % (4 + b)
-            mm(bank, T.wq[:, 128 * b:128 * b + 128], T.wsp[:, 128 * b:128 * b + 128], ["wq", "wsp"],
-               T.zq[:, :], T.zs[:, :], ["zq"])
-            out_of(slot("rb", b), bank, 2.0 ** -6)
+        def part(name, b, p, lo, hi):
+            return T[name][:, b * C + lo:b * C + hi], ["%s%d%s" % (name, b, k) for k in p]
+
+        def cols(off, lo, hi):
+            return off[0][:, lo // 16:hi // 16], off[1]
+
+        for n, (p, (lo, hi)) in enumerate(Z_RUNS[r].items()):
+            for b in range(4):
+                apart = (0.5 if last else AT["dz"]) * (b + 4 * n) / len(Z_RUNS[r])
+                at(AT["gt"] + apart)
+                act(part("gt", b, p, lo, hi), by(slot("fs", b), cols(tab("to"), lo, hi)), ga(hi - lo))
+                at(AT["z"] + apart)
+                tt((T.z[:, 4 * lo + b:4 * hi:4], ["z%d%s" % (b, k) for k in p]), by(slot("fh", b), cols(nfo, lo, hi)),
+                   part("gt", b, p, lo, hi), A.add, ga(hi - lo))
+            quant(T.zq[:, lo:hi], T.zs[:, lo:hi], ["z%d%s" % (b, k) for b in range(4) for k in p], ["zq" + k for k in p],
+                  T.z[:, 4 * lo:4 * hi], 4 * (hi - lo))
+            if hi == C:
+                stages.append((keep, len(ops), goal, {len(ops) - 1: Z_WORTH[r]}))
+            for b in range(4):
+                at(0.0 if last else AT["rb"] + 0.5 * b)
+                bank = "p%d" % (4 + b)
+                mm(bank, T.wq[:, 128 * b:128 * b + 128], T.wsp[:, 128 * b:128 * b + 128], ["wq", "wsp"],
+                   T.zq[:, lo:hi], T.zs[:, lo:hi], ["zq" + k for k in p], hi - lo)
+                out_of(part("rb", b, p, lo, hi), bank, 2.0 ** -6, hi - lo)
         nq, ns = "xq%d" % (r + 1), "xs%d" % (r + 1)
         for p, (lo, hi) in (HALVES if last else WHOLE).items():
             for b in range(4):
-                at(AT["x"] + AT["level"] * b * (not last))
+                at(0.0 if last else AT["x"] + AT["dx"] * b)
                 out = (T.xt[:, 4 * lo + b:4 * hi:4], ["xt%d%s" % (b, k) for k in p])
                 off = (nho[0][:, lo // 16:hi // 16], nho[1])
                 if b in P_FAR[r] and p != "a":
-                    act(slot("gp", b, C, lo, hi), by(slot("rb", b), off), ga(hi - lo))
+                    act(slot("gp", b, C, lo, hi), by(two("rb", b), off), ga(hi - lo))
                     tt((out[0], out[1] + ["p%d" % b]), slot("gp", b, C, lo, hi), (T["p%d" % b][:, lo:hi], []), A.add,
                        el(hi - lo))
                 else:
-                    tt(out, by(slot("rb", b), off), slot("fh", b, C, lo, hi), A.add, ga(hi - lo))
+                    tt(out, by(two("rb", b), off), slot("fh", b, C, lo, hi), A.add, ga(hi - lo))
             quant(T[nq][:, lo:hi], T[ns][:, lo:hi], ["xt%d%s" % (b, k) for b in range(4) for k in p], [nq + p * last],
                   T.xt[:, 4 * lo:4 * hi], 4 * (hi - lo))
         if not last:
@@ -633,8 +847,8 @@ def rank_program(g, core, T, topo):
     for bank, (p, (lo, hi)) in zip(("p4", "p5"), HALVES.items()):
         mm(bank, T.vq[:, :], T.vqs[:, :], ["vq"], T.xq3[:, lo:hi], T.xs3[:, lo:hi], ["xq3" + p], hi - lo)
         out_of(R("yb", lo, hi, "yb" + p), bank, n=hi - lo)
-        store("y", T.oc[:, 4 * lo:4 * hi], T.xq3[:, lo:hi].bitcast(dt.uint8), ["xq3" + p], 0.6)
-        store("s", T.y[:, lo:hi], T.yb[:, lo:hi], ["yb" + p], 0.6)
+        store("y", T.oc[:, 4 * lo:4 * hi], T.xq3[:, lo:hi].bitcast(dt.uint8), ["xq3" + p], 0.35)
+        store("s", T.y[:, lo:hi], T.yb[:, lo:hi], ["yb" + p], 0.4)
     for k in range(4):
         store("y", T.osc[4 * k:4 * k + 4, :], T.xs3[32 * k:32 * k + 4, :], ["xq3a", "xq3b"])
     emit()
@@ -645,16 +859,18 @@ def relay_program(g, core, T, topo):
     for r in range(3):
         for i, src in enumerate(T.cores):
             dst = T.cores[i ^ MASKS[r]]
-            if relay_of(src, dst, topo, 0) == core:
-                g.wait_ge(T.sem["ac%d" % r], NE)
+            came = NE if topo.may_write(src, dst) else NEAR
+            if route(T, topo, i, r, "c0") == core:
+                g.wait_ge(T.sem["ac%d" % r], came)
                 n += send(g, T, topo, core, dst, T["lc%d" % r][:, :].bitcast(dt.uint8),
                           T["lc%d" % r][:, :].bitcast(dt.uint8), "ac%d" % r, NE)
-            if relay_of(src, dst, topo, 1) == core:
-                g.wait_ge(T.sem["ac%d" % r], NE)
+            if route(T, topo, i, r, "c1") == core:
+                g.wait_ge(T.sem["ac%d" % r], came)
                 n += send(g, T, topo, core, dst, T["ls%d" % r][:, :], T["ls%d" % r][:, :], "ac%d" % r, NE)
-                for k in "dab":
-                    g.wait_ge(T.sem["a%s%d" % (k, r)], NL)
-                    name = "l%s%d" % (k, r)
-                    n += send(g, T, topo, core, dst, T[name][:, :], T[name][:, :], "a%s%d" % (k, r), NL)
+            for k in "dab":
+                if route(T, topo, i, r, k + "0") == core:
+                    name, lo, hi = piece(k, r, False)
+                    g.wait_ge(T.sem["a%s%d" % (k, r)], NEAR)
+                    n += send(g, T, topo, core, dst, T["l" + name][:, lo:hi], T["l" + name][:, lo:hi], "a%s%d" % (k, r), NL)
     if n:
         g.wait_ge(T.sem.sent, n)

import math
from concourse.mybir import dt, AluOpType, ActivationFunctionType

A = AluOpType
COPY = ActivationFunctionType.Copy
IDENT = ActivationFunctionType.Identity
RELU = ActivationFunctionType.Relu
C = 288
TC = C // 16
H = C // 2
M = 1024.0
UP = 2.0 ** 40
BIG = 2.0 ** 72
MASKS = [4, 1, 2]
POWERS = [1, 2, 4, 8, 16, 32, 32]
STEPS = [(1, 1), (2, 2), (4, 4), (8, 8), (16, 16), (32, 32), (32, 32), (96, 96), (96, 96)]
HALVES = {"a": (0, 128), "b": (128, C)}
WHOLE = {"ab": (0, C)}
Z_RUNS = [WHOLE, WHOLE, HALVES]
P_FAR = [(3,), (2, 3), (0, 1, 2)]
PLAIN_A = [False, False, True]
CUT_F, CUT_ROW, CUT_LEAD, CUT_KF = 10, 10, 8, 12
ASIDE = ("c1",)
Z_WORTH = [(0.2, 0.0), (0.2, 0.0), (0.7, 0.0)]
NEEDED = dict(aa=(0.8, 1.6), ab=(0.8, 3.6), ac=(0.8, 3.6))
LIFT = 2.0 ** 20
ROUND = 1.5 * 2.0 ** 23
NS = 7
NE, NL, NEAR = 8, 8, 16
NB, NF = 20, 4
WAKE, GATHER, SCATTER, EL = 0.15, 1.43e-3, 3.6e-3, 0.955e-3
LIST_US, PLANE_US, CODE_US, HOP_US, FIRST_US, STORE_US = 0.55, 1.1, 2.6, 2.1, 1.5, 1.7
AT = dict(x0=4.0, u=4.2, mates=5.4, dfm=12.2, h0=16.6, level=1.2, gt=2.2, z=2.9, rb=7.8, x=9.0, fh=13.7, fs=18.7,
          far=16.4, dz=1.25, dx=1.1)
SLOW = [dict(gather=1.5, scatter=1.65, el=1.25, issue=1.5, far=1.2, rows=0.3, share=0.35, wake=0.14),
        dict(gather=1.0, scatter=1.0, el=1.0, issue=2.0, far=1.3, rows=0.6, share=0.15)]
IN_TURN = ("p", "d", "e", "r0", "r1")
TRIES, HEAT, TINY = 1000, 0.08, 2e-5
EFFORT = [2.0, 2.0, 4.0, 2.0, 4.0, 2.0, 2.0]
SEEDS = [[46], [54], [4], [28], [18], [22], [9]]
LEFT = (0.1, 0.6)
LATE = dict(x0=4.5, ub=7.0, wq=12.0, wsp=12.0, vb=14.0)
SPAN = []
FOUND = {}

SCRATCH = {}


def _b(names, n, dtype, where="sbuf"):
    for name in names.split():
        SCRATCH[name] = (where, [128, n], dtype)


CODE = "float8_e4m3fn_x4"
_b("x0 xt z fh fs gt", 4 * C, "bfloat16")
_b("rb gp", 4 * C, "float32")
_b("xq0 xq1 xq2 xq3 lc0 lc1 lc2 zq", C, CODE)
_b("xs0 xs1 xs2 xs3 ls0 ls1 ls2 zs", C, "uint8")
_b("fo0 fo1 fo2 fo3 sb0 sb1 sb2 lb0 lb1 lb2 ho0 ho1 mo rep", TC, "uint16")
_b("sa0 sa1 sa2 la0 la1 la2", 3 * TC, "uint16")
_b("ft tu", 7 * TC, "uint16")
_b("wq eq", 512, CODE)
_b("wsp eqs", 512, "uint8")
_b("uq uk vq", 128, CODE)
_b("uqs uks vqs", 128, "uint8")
_b("et", 2048, "bfloat16")
_b("ub vb", 512, "bfloat16")
_b("fli mli", TC, "int32")
_b("ti", 9 * TC, "int32")
_b("tf", 20 * TC, "float32")
_b("key0 key1 s y0 y1 y2 y3 za0 za1 za2 kf kr st so top ck run lead ms nms yb nlr", C, "float32")
_b("fla flb", C + 16, "float32")
_b("jc", C + 16, "bfloat16")
_b("cand sw orb oer cv jcs", C, "bfloat16")
_b("both", 2 * C, "float32")
_b("fr", 8 * C, "bfloat16")
_b("pr", 6 * C, "bfloat16")
_b("row sc", NB * C, "bfloat16")
_b("scf", NF * C, "float32")
_b("uo", 8, "uint16")
_b("j32", 32, "float32")
_b("c16", 5 * 16, "float32")
_b("cw", C, "float32")
_b("m0 m1 m2", NS * TC, "float32")
_b("cv16", 16, "bfloat16")
_b("pi p16i", 2, "int32")
_b("p16 p17", 2, "float32")
_b("col", 8, "float32")
_b("half", 128, "bfloat16")
_b("p0 p1 p2 p3 p4 p5 p6 p7", 512, "float32", "psum")
TU = "ro lo w wa to eo bo".split()
TI = "ki dj dd kl q x0i x1i a0i a1i".split()
TF = "jt ca dfm dh i lnf rl def pef zz t m w0 w0a ta th tc td u0 u1".split()

SEMAPHORES = ["cv", "cs", "ct", "cp", "lx", "lu", "lv", "lf", "lm", "lw", "lq", "lout", "sent"]
SEMAPHORES += [k + str(r) for k in ("ac", "aa", "ab", "ad") for r in range(3)]


def relay_of(src, dst, topo, k):
    if topo.may_write(src, dst):
        return None
    cs = [c for c in topo.cores_of(src) if topo.may_write(c, dst)]
    cs = [c for c in cs if topo.die(c) == topo.die(src)] or cs
    return cs[k % len(cs)]


def route(T, topo, rank, r, what):
    src = T.cores[rank]
    for k in range(r, -1, -1):
        via = relay_of(src, T.cores[rank ^ MASKS[k]], topo, int(what != "c0"))
        if via is not None and (k == r or what in ASIDE):
            return via
    return None


def piece(k, r, straight):
    if k == "b":
        return "b%d" % r, 0, TC
    return ("a%d" % r,) + ((2 * TC, 3 * TC) if k == "d" else (0, (3 if straight else 2) * TC))


def send(g, T, topo, src, dst, out_ap, in_ap, sem, count, last=False):
    rid, pid = topo.addr(dst, src)
    e = topo.engines(src, dst)
    e = e[-count:] if last else e[:count]
    m = 0
    for k in e:
        m |= 1 << k
    g.remote_dma(out_ap=out_ap, in_ap=in_ap, remote_sem=T.sem[sem], local_sem=T.sem.sent, pid=pid, routing_id=rid,
                 dma_engine_mask=m)
    return len(e)


def place(some, cost, queue, before, rank, start, held, soon, since=-1.0):
    for i in some:
        r = -1e9 if queue[i] in IN_TURN[1:] and before[i] else rank[i]
        for d, lag in before[i]:
            if rank[d] > r:
                r = rank[d]
        rank[i] = r
    busy = {q: [x for x in line if x[0] < since or x[2] < 0] for q, line in held.items()}
    for i in sorted(some, key=lambda i: rank[i]):
        t, c = soon[i], cost[i]
        for d, lag in before[i]:
            if start[d] + lag > t:
                t = start[d] + lag
        if queue[i] in IN_TURN:
            line = busy[queue[i]]
            if line and line[-1][1] > t:
                t = line[-1][1]
            line.append((t, t + c, i))
        elif queue[i] is not None:
            line = busy[queue[i]]
            k = len(line)
            while k and line[k - 1][1] > t:
                k -= 1
            while k < len(line) and line[k][0] < t + c - 1e-9:
                if line[k][1] > t:
                    t = line[k][1]
                k += 1
            line.insert(k, (t, t + c, i))
        start[i] = t
    return busy


def order(ops, stages):
    n = len(ops)
    sign = tuple((o["q"], o["c"], o["tail"], tuple(sorted(o["deps"]))) for o in ops)
    if sign not in FOUND:
        fore = [[(d, ops[d]["c"] + ops[d]["tail"] + WAKE) for d in sorted(o["deps"])] for o in ops]
        fore.append([(i, ops[i]["c"] + ops[i]["tail"]) for i in range(n)])
        back = [[] for _ in fore]
        for i, b in enumerate(fore):
            for d, lag in b:
                back[d].append((i, lag))
        cost, queue = [o["c"] for o in ops] + [0.0], [o["q"] for o in ops] + [None]
        seed = [1]

        def draw():
            seed[0] = (seed[0] * 1103515245 + 12345) % 2147483648
            return (seed[0] >> 8) / 8388608.0

        def one(of):
            return of[int(draw() * len(of))]

        cost2 = [[o["c"] + u["rows"] * o["k"] if isinstance(o["k"], float) else o["c"] * u[o["k"]] for o in ops] + [0.0]
                 for u in SLOW]
        fore2 = [[[(d, c[d] + ops[d]["tail"] * u["far"] + u.get("wake", WAKE)) for d, lag in b] for b in fore] for c, u in zip(cost2, SLOW)]
        done = [0.0] * (n + 1)
        slow = [done for u in SLOW]
        held = {q: [] for q in queue if q is not None}
        first = 0
        for keep, end, aim, goals in stages + [(n + 1, n + 1, n, {})]:
            some = list(range(first, end))
            free = [i for i in some if i < n and ops[i]["other"]]
            work = [(i, cost[i]) for i in range(first, min(keep, n)) if queue[i] in ("v", "s")]
            ahead = [[(d, lag) for d, lag in b if d >= first] for b in fore]
            behind = [[(u, lag - cost[i] + cost[u]) for u, lag in b if u < end] for i, b in enumerate(back)]
            soon = [max([0.0] + [done[d] + lag for d, lag in b if d < first]) for b in fore]
            least = max(0.0, SPAN[-1][0] - 3.5) if first else 0.0
            tries = int(TRIES * EFFORT[len(SPAN)])
            near = {q: [x for x in line if x[1] > least] for q, line in held.items()}
            soon = [max(x, least) for x in soon]
            rest, none = [0.0] * (n + 1), {q: [] for q in held}

            again = [i for i in range(first) if done[i] >= least] + some
            idle = [{q: max([0.0] + [a[i] + c[i] for i in range(first) if queue[i] == q and done[i] < least]) for q in held}
                    for a, c in zip(slow, cost2)]

            def replay(turn, where, k):
                out, line, lags, c = list(slow[k]), dict(idle[k]), fore2[k], cost2[k]
                for i in turn:
                    q = where[i]
                    t = line[q] if q else 0.0
                    for d, lag in lags[i]:
                        if out[d] + lag > t:
                            t = out[d] + lag
                    out[i] = t
                    if q:
                        line[q] = t + c[i]
                return out

            def tried(rank, where, most=1e9, old=None):
                if old is None:
                    start = list(done)
                    busy = place(some, cost, where, ahead, rank, start, near, soon)
                else:
                    start = list(old[1])
                    since = min([min(rank[i], start[i]) for i in some if rank[i] != start[i] or where[i] != old[2][i]] + [1e9])
                    busy = place([i for i in some if start[i] >= since], cost, where, ahead, rank, start, old[5], soon, since)
                plain = worth(start, 1.0)
                if plain > most:
                    return 1e9, start, where, None, plain, busy
                turn = sorted(again, key=lambda i: start[i])
                other = [replay(turn, where, k) for k in range(len(SLOW))]
                return (plain + sum(u["share"] * (worth(a, u["el"]) - plain) for a, u in zip(other, SLOW))
                        + TINY * sum(start[first:end]), start, where, other, plain, busy)

            def worth(start, k):
                t = start[aim]
                over = [w * max(0.0, start[i] - t - k * slack) for i, (w, slack) in goals.items()] + [0.0]
                return t + max(over) + 0.03 * sum(over) + LEFT[len(SPAN) % 2] * sum(c for i, c in work if start[i] > t)

            def turned(start, where):
                late = list(done)
                place(some[::-1], cost, where, behind, [-(start[i] + cost[i]) for i in range(n + 1)], late, none, rest)
                return tried([-(late[i] + cost[i]) for i in range(n + 1)], where)

            def blocks(start, where):
                ends = {(where[i], round(start[i] + cost[i], 6)): i for i in some if where[i]}
                out, seen = [], set()
                todo = [aim] + [i for i, (w, slack) in goals.items() if start[i] > start[aim] + slack]
                while todo:
                    i = todo.pop()
                    if i not in seen:
                        seen.add(i)
                        tight = [d for d, lag in ahead[i] if start[d] + lag > start[i] - 1e-6]
                        d = ends.get((where[i], round(start[i], 6)))
                        if not tight and d is not None:
                            out.append((d, i))
                            tight = [d]
                        todo += tight
                return out

            def with_kin(i, kin, rank, near_enough, s):
                group = [i]
                for u in group:
                    group += [d for d, lag in kin[u] if d not in group and near_enough(rank[d])]
                for u in set(group):
                    rank[u] += s

            now = tried([o["at"] for o in ops] + [1e9], queue)
            guess = best = min(now, turned(now[1], queue))
            seeds = SEEDS[len(SPAN)] + [0]
            RUNS = len(seeds)
            for k in range(tries * RUNS):
                run, k = divmod(k, tries)
                if k == 0:
                    now, pairs = (best if run == RUNS - 1 else guess), None
                    seed[0] = 7919 * seeds[run] + 1
                rank, where, how = list(now[1]), now[2], draw()
                if pairs is None:
                    pairs = blocks(now[1], where)
                a, b = one(pairs) if pairs else (first, first)
                if how < 0.2:
                    i = one((a, b)) if how < 0.12 else one(free)
                    if i in free:
                        where = list(where)
                        where[i] = "s" if where[i] == "v" else "v"
                    rank[i] += one((-0.5, 0.0, 0.0, 0.5))
                elif how < 0.4:
                    rank[a] = rank[b] + one((0.01, 0.3, 0.6, 1.2, 2.5))
                elif how < 0.55:
                    with_kin(b, ahead, rank, lambda t, t0=rank[a] - 1.0: t > t0, rank[a] - rank[b] - 0.01)
                elif how < 0.72:
                    i, s, w = one(some), one((-4, -2, -1, -0.5, 0.5, 1, 2, 4)), one((1, 2, 4))
                    with_kin(i, ahead if s < 0 else behind, rank, lambda t, t0=rank[i], w=w: abs(t - t0) < w, s)
                elif how < 0.86:
                    for _ in range(one((1, 2, 3))):
                        rank[one(some)] += one((-4, -2, -1, -0.5, -0.2, 0.2, 0.5, 1, 2, 4))
                else:
                    a, w, s = rank[one(some)], one((1, 2, 4)), one((0.2, 0.6, 1.2))
                    for i in some:
                        if a <= rank[i] < a + w:
                            rank[i] += s * (draw() - 0.5)
                heat = HEAT * (1.0 - k / tries) * (0.3 if run == RUNS - 1 else 1.0) + 0.003
                room = -heat * math.log(draw() + 1e-9)
                new = tried(rank, where, now[4] + room + 0.2, now)
                if draw() < 0.03:
                    new = min(new, turned(new[1], where), key=lambda x: x[0])
                if new[0] <= now[0] + room:
                    now, pairs = new, None
                    if now[0] < best[0]:
                        best = now
            done, queue, slow = best[1:4]
            for i in range(first, keep):
                if queue[i] is not None:
                    held[queue[i]].append((done[i], done[i] + cost[i], -1))
            for q in held:
                held[q].sort()
            SPAN.append((round(done[aim], 2), round(slow[0][aim], 2), round(slow[1][aim], 2)))
            first = keep
        FOUND[sign] = [(i, queue[i]) for i in sorted(range(n), key=lambda i: (done[i], i))]
    return FOUND[sign]


def rank_program(g, core, T, topo):
    rank = T.rank_of(core)
    if rank is None:
        relay_program(g, core, T, topo)
        return
    queues = {"v": g.vector, "s": g.scalar, "t": g.tensor, "p": g, "y": g.sync}
    own = {"v": "cv", "s": "cs", "t": "ct", "p": "cp"}
    V, S, P = g.vector, g.scalar, g.tensor
    ops, stages = [], []
    clock = [0.0, 0.0]
    acc = {}

    def at(t, base=None):
        clock[1] = t
        if base is not None:
            clock[0] = base

    def users(names):
        out = set()
        for r in names:
            a = acc.setdefault(r, [None, []])
            out.update(a[1])
            if a[0] is not None:
                out.add(a[0])
        return out

    more = set()
    picks = set()

    def op(qn, rd, wr, fn, cost, sem=None, inc=1, tail=0.0, ev=None):
        deps = set(more)
        more.clear()
        me = len(ops)
        for r in rd:
            a = acc.setdefault(r, [None, []])
            if a[0] is not None:
                deps.add(a[0])
        for r in wr:
            a = acc.setdefault(r, [None, []])
            deps.update(a[1])
            if a[0] is not None:
                deps.add(a[0])
        for r in rd:
            acc[r][1].append(me)
        for r in wr:
            acc[r] = [me, []]
        deps.discard(me)
        plan = max([clock[0] + clock[1]] + [ops[d]["at"] + ops[d]["c"] + ops[d]["tail"] + WAKE for d in deps])
        k = "gather" if cost in picks else "scatter" if cost > 1.0 and qn == "v" else "el" if qn in own else "far"
        ops.append(dict(q=qn, c=cost, k=k, tail=tail, at=plan, deps=deps, fn=fn, sem=sem or own.get(qn), inc=inc, ev=ev,
                        other=None))

    def emit():
        total, know = {}, {k: {} for k in queues}
        for i, qn in order(ops, stages):
            o = ops[i]
            if qn != o["q"]:
                o.update(q=qn, fn=o["other"], sem=own[qn])
            if o["fn"] is None:
                o["knows"] = {}
                continue
            k = know[o["q"]]
            waits = sorted((ops[d]["ev"] + (d,) for d in o["deps"] if ops[d]["ev"]), key=lambda e: -len(ops[e[2]]["knows"]))
            top = {}
            for s, n, d in waits:
                if n > top.get(s, (0,))[0]:
                    top[s] = (n, d)
            for s, n, d in waits:
                if top[s] != (n, d) or k.get(s, 0) >= n:
                    continue
                queues[o["q"]].wait_ge(T.sem[s], n)
                for a, b in ops[d]["knows"].items():
                    if k.get(a, 0) < b:
                        k[a] = b
                k[s] = n
            if o["sem"] is None:
                o["fn"]()
                o["knows"] = {}
                continue
            total[o["sem"]] = total.get(o["sem"], 0) + o["inc"]
            o["fn"]().then_inc(T.sem[o["sem"]], o["inc"])
            o["ev"] = (o["sem"], total[o["sem"]])
            o["knows"] = dict(k)
            o["knows"][o["sem"]] = total[o["sem"]]
        for s in sorted(total):
            if know["p"].get(s, 0) < total[s]:
                g.wait_ge(T.sem[s], total[s])
        g.wait_ge(T.sem.sent, sends[0])

    def el(n, k=1.0):
        return max(n * k, 64) * EL

    def ga(n):
        picks.add(0.055 + n * GATHER)
        return 0.055 + n * GATHER

    def R(name, lo=None, hi=None, tag=None):
        if lo is None:
            return T[name][:, :], [name]
        return T[name][:, lo:hi], [tag or name]

    def slot(name, k, n=C, lo=0, hi=None):
        return T[name][:, k * n + lo:k * n + (hi or n)], ["%s%d" % (name, k)]

    def tab(name, n=1):
        for buf, names in (("tu", TU), ("ti", TI), ("tf", TF)):
            if name in names:
                k = names.index(name)
                return T[buf][:, k * TC:(k + n) * TC], names[k:k + n]

    def by(win, off):
        return win[0].indirect(off[0]), win[1] + off[1]

    def num(x):
        return (x, []) if isinstance(x, (int, float)) else x

    def ts(out, a, s1, o1, s2=None, o2=None, c=None):
        s1 = num(s1)
        c = el(TC) if c is None else c
        if o2 is None:
            op("v", a[1] + s1[1], out[1], lambda: V.tensor_scalar(out[0], a[0], s1[0], None, o1), c)
        else:
            s2 = num(s2)
            op("v", a[1] + s1[1] + s2[1], out[1], lambda: V.tensor_scalar(out[0], a[0], s1[0], s2[0], o1, o2), c)

    def tt(out, a, b, o, c=None):
        op("v", a[1] + b[1], out[1], lambda: V.tensor_tensor(out[0], a[0], b[0], o), el(TC) if c is None else c)

    def cp(out, a, c=None):
        op("v", a[1], out[1], lambda: V.tensor_copy(out[0], a[0]), el(TC) if c is None else c)

    def act(out, a, c, scale=1.0, bias=0.0):
        scale, bias = num(scale), num(bias)
        if not scale[1] and not bias[1] and scale[0] == 1.0 and bias[0] == 0.0:
            op("s", a[1], out[1], lambda: S.activation(out[0], a[0], COPY), c)
            ops[-1]["other"] = lambda: V.tensor_copy(out[0], a[0])
        else:
            op("s", a[1] + scale[1] + bias[1], out[1],
               lambda: S.activation(out[0], a[0], IDENT, bias=bias[0], scale=scale[0]), c)
            ops[-1]["other"] = lambda: V.tensor_scalar(out[0], a[0], scale[0], bias[0], A.mult, A.add)

    def lin(out, a, scale, bias):
        act(out, a, el(TC), scale, bias)

    def col(k):
        return T.col[:, k:k + 1], ["col%d" % k]

    def step(buf, k):
        return T[buf][:, k:NS * TC:NS], ["%s%d" % (buf, k)]

    def two(name, k=0):
        return T[name][:, k * C:(k + 1) * C], ["%s%da" % (name, k), "%s%db" % (name, k)]

    def shared(out, win, off, cut, scale=1.0, bias=0.0):
        if cut == TC:
            act(out, by(win, off), ga(C), scale, bias)
        else:
            before = users(out[1])
            more.update(before)
            act((out[0][:, 0:16 * cut], out[1][:1]), by(win, (off[0][:, 0:cut], off[1])), ga(16 * cut), scale, bias)
            more.update(before)
            act((out[0][:, 16 * cut:C], out[1][1:]), by(win, (off[0][:, cut:TC], off[1])), ga(C - 16 * cut), scale, bias)

    DOWN, LESS_M, LESS, LESS_2, DROP = range(5)
    turn = {"row": 0, "sc": 0, "scf": 0}

    def fresh(name, n):
        turn[name] += 1
        return turn[name] % n

    def scan(out, d0, d1, first, o0, o1, c):
        op("v", d0[1] + d1[1], out[1], lambda: V.tensor_tensor_scan(out[0], d0[0], d1[0], first, o0, o1), c)

    def table_of(row, wide=False):
        name = "scf" if wide else "sc"
        k = fresh(name, NF if wide else NB)
        out = slot(name, k)
        scan(out, R("cv"), row, 0.0, A.mult, A.add, el(C, 1.0 if wide else 0.5))
        return T[name][:, k * C + 15:(k + 1) * C:16], out[1]

    def lifted(row):
        k = fresh("scf", NF)
        out = slot("scf", k)
        scan(out, R("cw"), row, 0.0, A.add, A.max, el(C))
        return T.scf[:, k * C + 15:(k + 1) * C:16], out[1]

    def offsets(out, view, by_=DOWN):
        ts(out, view, col(by_), A.mult, float(H), A.add)

    def spare():
        return slot("row", fresh("row", NB))

    def mm(bank, st, sts, sr, mv, mvs, mr, n=C):
        op("t", sr + mr, [bank], lambda: P.matmul_mx(T[bank][:, 0:n], st, sts, mv, mvs, True, True), (n + 16) * 1.25e-3)

    def quant(q, s, rd, wr, src, n):
        op("v", rd, wr, lambda: V.quantize_mx(q, s, src), 0.015 + 0.26e-3 * n)

    def load(qn, out, in_, res, sem, tail=2.2):
        queues[qn].dma_start(out=out, in_=in_).then_inc(T.sem[sem], 16)
        op(None, [], [res], None, 0.0, None, 0, tail, (sem, 16))

    def store(qn, out, in_, res, us=0.05):
        tag = "store%d" % len(ops)
        op(qn, res, [tag], lambda: queues[qn].dma_start(out=out, in_=in_), 0.1, "lout", 16)
        op("d", [tag], [], None, us, None, 0, STORE_US)

    def out_of(out, bank, scale=1.0, n=C):
        act((out[0], out[1] + [bank]), (T[bank][:, 0:n], []), el(n), scale)

    sends, sent = [0], {}

    def to_partner(r, bufs, sem, count, land):
        dst = T.cores[rank ^ MASKS[r]]

        straight = topo.may_write(core, dst)

        def go(hop, o, i):
            sends[0] += send(g, T, topo, core, hop, o, i, sem, count if straight else NEAR, hop != dst)

        for k, (o, i, res, us, lane) in enumerate(bufs):
            via = route(T, topo, rank, r, sem[1] + str(k))
            hop = dst if via is None else via
            way = "way%s%d" % (sem, k)
            op("p", res, [way] + ["lane%d" % lane] * (via is not None), lambda hop=hop, o=o, i=i: go(hop, o, i), 0.3)
            ops[-1]["sem"] = None
            part = 1.0 if straight else 0.6
            op("e" if straight and via is not None else "d", [way], [way], None, us * part, None, 0,
               HOP_US + 2.0 * (sem == "ac0"))
            ops[-1]["k"], ops[-2]["k"] = part, "issue"
            if via is not None:
                op("r%d" % lane, [way], [way], None, us + 0.3 + FIRST_US * (sem == "ac1"), None, 0, HOP_US)
                ops[-1]["k"] = 1.4
        op(None, ["way%s%d" % (sem, k) for k in range(len(bufs))], [land], None, 0.0, None, 0, 0.0, (sem, count * len(bufs)))
        sent[sem] = len(ops) - 1

    def send_list(r, k, res):
        name, lo, hi = piece(k, r, topo.may_write(core, T.cores[rank ^ MASKS[r]]))
        to_partner(r, [(T["l" + name][:, lo:hi], T["s" + name][:, lo:hi], res, LIST_US, 1)], "a%s%d" % (k, r), NL,
                   "l%s%d" % (k, r))

    def send_codes(r):
        q = "xq%d" % r
        to_partner(r, [(T["lc%d" % r][:, :].bitcast(dt.uint8), T[q][:, :].bitcast(dt.uint8), [q], CODE_US, 0),
                       (T["ls%d" % r][:, :], T["xs%d" % r][:, :], [q], PLANE_US, 1)], "ac%d" % r, NE, "lc%d" % r)

    load("y", T.fli[:, :], T.fl[:, :], "fli", "lf")
    load("y", T.mli[:, :], T.ml[:, :], "mli", "lm")
    load("y", T.x0[:, :], T.x[:, :], "x0", "lx", LATE["x0"])
    load("y", T.ub[:, :], T.u[:, :], "ub", "lu", LATE["ub"])
    load("y", T.wq[:, :].bitcast(dt.uint8), T.wc[:, :], "wq", "lw", LATE["wq"])
    load("y", T.wsp[:, :], T.ws[:, :], "wsp", "lq", LATE["wsp"])
    load("y", T.vb[:, :], T.v[:, :], "vb", "lv", LATE["vb"])

    def iota(name, pattern, base, mult, n, flag=True):
        if flag:
            op("p", [], [name], lambda: g.iota(T[name][:, :], pattern, base, mult, allow_small_or_imprecise_dtypes=True),
               0.15 + 2 * n * EL)
        else:
            op("p", [], [name], lambda: g.iota(T[name][:, :], pattern, base, mult), 0.15 + 2 * n * EL)

    iota("pi", [[0, 2]], 0, 1, 2, False)
    iota("j32", [[1, 32]], 0, 0, 32)
    iota("jc", [[1, C + 16]], -H, 0, C + 16)
    jc = R("jc")
    act(R("key0"), R("jc", 0, C), el(C), M, M * H + C - 1.0)
    act(R("key1"), R("jc", 0, C), el(C), M, M * H + C - 2.0)
    act(R("jcs"), R("jc", 0, C), el(C), -1.0 / M)
    p16 = (T.p16[:, 0:1], ["p16"])
    ts(R("p16i"), R("pi"), 15, A.bitwise_and)
    cp(R("p16"), R("p16i"))
    ts(R("p17"), R("p16i"), 1.0, A.add)
    c16 = [slot("c16", k, 16) for k in range(5)]
    ts(c16[0], R("j32", 0, 16), p16, A.not_equal)
    ts(c16[1], R("j32", 0, 16), (T.p17[:, 0:1], ["p17"]), A.is_equal, UP, A.mult)
    tt(R("cv16"), c16[0], c16[1], A.max)
    ts(R("rep"), R("j32", 0, TC), 0.0, A.mult, p16, A.add)
    act(R("cv"), by(R("cv16"), R("rep")), ga(C))
    ts(col(DOWN), p16, 15.0, A.is_equal, 1.0 / UP, A.max)
    for k, f in ((LESS_M, -M), (LESS, -M * M), (LESS_2, -2.0)):
        act(col(k), col(DOWN), el(1), f)
    ts(c16[2], R("j32", 0, 16), p16, A.is_equal, -BIG, A.mult)
    ts(c16[3], R("j32", 0, 16), (T.p17[:, 0:1], ["p17"]), A.is_equal, LIFT, A.mult)
    tt(c16[4], c16[2], c16[3], A.add)
    act(R("cw"), by(c16[4], R("rep")), ga(C))
    ts(col(DROP), p16, 15.0, A.is_lt, -LIFT, A.mult)
    for buf, k, f in (("m0", 0, 0.0), ("m0", 2, 1.0), ("m0", 3, 1.0), ("m0", 5, 1.0), ("m0", 6, 1.0),
                      ("m1", 1, -0.499), ("m1", 2, ROUND), ("m1", 3, -ROUND)):
        act(step(buf, k), R("j32", 0, TC), el(TC), 0.0, f)
    act(R("fla", 0, 1, "fla0"), R("j32", 0, 1), el(1))
    cp(R("fo0"), R("fli"))
    op("v", [], ["et"], lambda: V.memset(T.et[:, :], 0.0), el(2048, 0.5))
    op("v", [], ["half"], lambda: V.memset(T.half[:, :], 0.5), el(64))
    at(1.0)
    for b in range(4):
        op("p", ["half", "et"], ["et%d" % b], lambda b=b: g.affine_select(
            T.et[:, 512 * b + b:512 * b + 512:4], T.half[:, :], [[-1, 128]], A.is_equal, 0.0, 0, 1), 0.2 + 256 * EL)
        quant(T.eq[:, 128 * b:128 * b + 128], T.eqs[:, 128 * b:128 * b + 128], ["et", "et%d" % b], ["eq%d" % b],
              T.et[:, 512 * b:512 * b + 512], 512)
    at(AT["x0"])
    quant(T.xq0[:, :], T.xs0[:, :], ["x0"], ["xq0"], T.x0[:, :], 4 * C)
    send_codes(0)
    at(AT["u"])
    quant(T.uq[:, :], T.uqs[:, :], ["ub"], ["uq"], T.ub[:, :], 512)
    quant(T.vq[:, :], T.vqs[:, :], ["vb"], ["vq"], T.vb[:, :], 512)
    ts(R("uo"), R("j32", 0, 8), 16.0, A.mult)
    cp((T.uk[:, :].bitcast(dt.uint32), ["uk"]), (T.uq[:, :].bitcast(dt.uint32).indirect(T.uo[:, :]), ["uq", "uo"]), ga(128))
    act(R("uks"), (T.uqs[:, :].indirect(T.uo[:, :]), ["uq", "uo"]), ga(128))
    at(AT["mates"])
    cp(R("mo"), R("mli"))
    ts(tab("jt"), R("j32", 0, TC), 16.0, A.mult, p16, A.add)
    tt(tab("u0"), R("mli"), tab("jt"), A.is_lt)
    ts(step("m1", 6), tab("u0"), float(C), A.mult)

    def difference(out, view, minus):
        offsets(tab("u0"), view)
        tt(tab("u1"), tab("u0"), minus, A.subtract)
        ts(out, tab("u1"), col(DOWN), A.mult)

    for r in range(3):
        last = r == 2
        xq, xs, xr = T["xq%d" % r], T["xs%d" % r], ["xq%d" % r]
        fo, nfo = R("fo%d" % r), R("fo%d" % (r + 1))
        ho, nho = R("ho%d" % (r % 2)), R("ho%d" % ((r + 1) % 2))
        powers, steps = POWERS, STEPS
        tabs, have = {1: fo}, 1
        at(2.1)
        shared(two("fr", 0), jc, fo, TC if r else CUT_F)
        for k, n in enumerate(powers, 1):
            at(1.6 + AT["level"] * min(k, 6))
            act(two("fr", k), by(two("fr", k - 1), tabs[n]), ga(C))
            have += n
            if have in powers or have in [a for a, b in steps]:
                tabs[have] = slot("ft", len(tabs) - 1, TC)
                offsets(tabs[have], table_of(two("fr", k)))
        if r == 0:
            at(AT["dfm"])
            a = spare()
            act(a, by(two("fr", 0), R("mo")), ga(C))
            difference(tab("dfm"), table_of(a), R("fli"))
        at(0.0)
        keys, have = {1: R("key0")}, 1
        for k, (n, old) in enumerate(steps):
            zz = R("za%d" % (k % 3)) if k else R("key1")
            if k:
                act(zz, keys[old], el(C), 1.0, float(old - have - n))
            keys[have + n] = R("y%d" % (k % 4))
            tt(keys[have + n], by(keys[have], tabs[n]), zz, A.min, ga(C))
            have += n
        key = keys[C]
        v = lifted(key)
        ts(tab("ro"), v, col(DROP), A.add, 1.0 / M, A.mult)
        ts(tab("t"), v, M * ROUND, A.add, M * ROUND, A.subtract)
        sa = "sa%d" % r
        dj = R(sa, 2 * TC, 3 * TC, sa + "d")
        tt(dj, v, tab("t"), A.subtract)
        handed = not topo.may_write(core, T.cores[rank ^ MASKS[r]])
        if handed:
            send_list(r, "d", dj[1])
        po, ln, eo = R(sa, 0, TC), R(sa, TC, 2 * TC, sa + "n"), tab("eo")
        shared(two("kf"), key, fo, CUT_KF, 1.0, M + 1.0)
        scan(R("st"), two("kf"), key, -1.0 - M - H * (not PLAIN_A[r]), A.add, A.subtract, el(C))
        a, drow = spare(), spare()
        if PLAIN_A[r]:
            act(two("ck"), by(R("st"), tab("ro")), ga(C))
            tt(po, lifted(two("ck")), v, A.subtract)
        else:
            tt(a, by(R("st"), tab("ro")), key, A.subtract, ga(C))
            offsets(po, table_of(a))
        act(R("kr"), by(two("kf"), tab("ro")), ga(C), 1.0, -M)
        tt(ln, lifted(R("kr")), tab("t"), A.subtract)
        send_list(r, "a", po[1] + ln[1] + dj[1] * (not handed))
        tt(eo, po, dj, A.add)
        act(drow, by(jc, dj), ga(C))
        op("v", ["jcs", sa], ["orb"], lambda po=po: V.tensor_copy(T.orb[:, :].indirect(po[0]), T.jcs[:, :]),
           0.05 + C * SCATTER)
        oo = R("sb%d" % r)
        offsets(oo, table_of(R("orb")), LESS_M)
        send_list(r, "b", oo[1])
        at(0.0)
        mm("p4", T.uk[:, :], T.uks[:, :], ["uk", "uks"], xq[:, :], xs[:, :], xr)
        out_of(R("s"), "p4", -1.0)
        act(R("so"), by(R("s"), oo), ga(C))
        ends = by(drow, oo)
        op("s", ends[1], ["fla"], lambda ends=ends: S.activation(T.fla[:, 1:C + 1], ends[0], RELU, bias=BIG * (1 - H),
                                                                 scale=-BIG), ga(C))
        ops[-1]["other"] = lambda ends=ends: V.tensor_scalar(T.fla[:, 1:C + 1], ends[0], float(-H), BIG, A.is_equal, A.mult)
        fla = (T.fla[:, 0:C], ["fla", "fla0"])

        def unpack(name, first, q, s, rd):
            at(AT[name] - 6.0 * (r == 0))
            for b in range(4):
                mm("p%d" % (first + b), T.eq[:, 128 * b:128 * b + 128], T.eqs[:, 128 * b:128 * b + 128], ["eq%d" % b], q, s, rd)
                out_of(slot(name, b), "p%d" % (first + b))

        goals = {sent[k + str(r)]: w for k, w in NEEDED.items()}
        if r == 0:
            unpack("fh", 0, xq[:, :], xs[:, :], xr)
            goals.update({i: (0.3, -0.5) for i in range(len(ops) - 7, len(ops), 2)})
            goals[sent["ac0"]] = (0.1, -1.5)
        keep = len(ops)
        at(0.0)
        scan(R("top"), fla, R("so"), BIG, A.add, A.min, el(C))
        stages.append((keep, len(ops), len(ops) - 1, goals))
        if r == 0:
            at(AT["h0"])
            tt(tab("dd"), ln, dj, A.subtract)
            ts(tab("u0"), tab("dd"), 1.0, A.is_equal)
            tt(tab("u1"), tab("u0"), ln, A.mult)
            ts(tab("u0"), po, -1.0, A.add)
            tt(tab("bo"), tab("u0"), tab("u1"), A.add)
            a = spare()
            act(a, by(R("orb"), tab("bo")), ga(C))
            offsets(ho, table_of(a), LESS_M)
            a, b = spare(), spare()
            act(a, by(jc, R("mo")), ga(C))
            act(b, by(a, ho), ga(C))
            difference(tab("dh"), table_of(b), ho)

        else:
            unpack("fh", 0, xq[:, :], xs[:, :], xr)
            lin(tab("tc", 2), tab("ta", 2), col(LESS_2), 0.0)
            tt(tab("dfm", 2), tab("tc", 2), tab("dfm", 2), A.add)

        unpack("fs", 4, T["lc%d" % r][:, :], T["ls%d" % r][:, :], ["lc%d" % r])
        at(0.0)
        act(R("flb", 0, C), fla, el(C), -1.0, -1.0 / M / M)
        tt(R("cand"), by(R("top"), eo), R("s"), A.is_equal, ga(C))
        tt(two("ck"), by(R("cand"), oo), R("orb"), A.add, ga(C))
        scan(R("run"), R("flb", 0, C), two("ck"), 0.0, A.add, A.max, el(C))
        shared(two("lead"), R("run"), eo, CUT_LEAD)
        v = table_of(two("lead"), True)
        ts(tab("lo"), v, col(LESS_M), A.mult, M + H, A.add)
        ts(tab("kl"), v, col(LESS), A.mult, M * (M + H), A.add)
        tt(tab("x0i"), tab("kl"), dj, A.subtract)
        tt(tab("x1i"), tab("x0i"), ln, A.add)
        ts(tab("a0i", 2), tab("x0i", 2), int(M) - 1, A.bitwise_and)
        tt(step("m1", 5), tab("a0i"), tab("a1i"), A.min)

        at(AT["far"])
        la, oe = "la%d" % r, R("lb%d" % r)
        far_d = R(la, 2 * TC, 3 * TC, "ld%d" % r if handed else la)
        for k, off in ((1, R(la, TC, 2 * TC)), (2, far_d), (0, R(la, 0, TC))):
            shared(two("pr", k), jc, off, CUT_ROW if handed and k < 2 else TC)
        act(slot("both", 1), by(R("s"), oe), ga(C))
        act(slot("both", 0), slot("both", 1), el(C), -1.0)
        act(R("oer"), by(jc, oe), ga(C))
        at(0.0)
        for k, name in ((1, step("m0", 4)), (2, tab("def")), (0, step("m1", 4))):
            a = two("pr", 3 + k)
            act(a, by(two("pr", k), tab("lo")), ga(C))
            lin(name, table_of(a), col(DOWN), float(H))
        op("v", ["m04"], ["m01"], lambda: V.reciprocal(step("m0", 1)[0], step("m0", 4)[0]), 0.32)
        tt(step("m1", 0), tab("def"), step("m1", 5), A.subtract)
        scan((T.m2[:, :], ["m2"]), (T.m0[:, :], ["m0%d" % k for k in range(NS)]),
             (T.m1[:, :], ["m1%d" % k for k in range(NS)]), 0.0, A.mult, A.add, el(NS * TC))
        cp(tab("wa"), (step("m2", 6)[0], ["m2"]))

        at(0.0, ops[-1]["at"])
        both = (T.both[:, :], ["both0", "both1"])
        act(R("nms"), by(both, tab("wa")), ga(C), -1.0)
        act(R("ms"), by(both, tab("wa")), ga(C))
        tt(R("sw"), by(R("nms"), R("mo")), R("ms"), A.is_gt, ga(C))
        tt(tab("ta"), table_of(R("sw")), tab("dfm"), A.mult)
        tt(nfo, tab("ta"), fo, A.add)
        goal = len(ops) - 1
        cp(tab("w"), (step("m2", 5)[0], ["m2"]))
        a = spare()
        act(a, by(R("oer"), tab("w")), ga(C))
        offsets(tab("to"), table_of(a))
        keep = len(ops)
        a = spare()
        act(a, by(R("sw"), ho), ga(C))
        tt(tab("th"), table_of(a), tab("dh"), A.mult)
        tt(nho, tab("th"), ho, A.add)

        def part(name, b, p, lo, hi):
            return T[name][:, b * C + lo:b * C + hi], ["%s%d%s" % (name, b, k) for k in p]

        def cols(off, lo, hi):
            return off[0][:, lo // 16:hi // 16], off[1]

        for n, (p, (lo, hi)) in enumerate(Z_RUNS[r].items()):
            for b in range(4):
                apart = (0.5 if last else AT["dz"]) * (b + 4 * n) / len(Z_RUNS[r])
                at(AT["gt"] + apart)
                act(part("gt", b, p, lo, hi), by(slot("fs", b), cols(tab("to"), lo, hi)), ga(hi - lo))
                at(AT["z"] + apart)
                tt((T.z[:, 4 * lo + b:4 * hi:4], ["z%d%s" % (b, k) for k in p]), by(slot("fh", b), cols(nfo, lo, hi)),
                   part("gt", b, p, lo, hi), A.add, ga(hi - lo))
            quant(T.zq[:, lo:hi], T.zs[:, lo:hi], ["z%d%s" % (b, k) for b in range(4) for k in p], ["zq" + k for k in p],
                  T.z[:, 4 * lo:4 * hi], 4 * (hi - lo))
            if hi == C:
                stages.append((keep, len(ops), goal, {len(ops) - 1: Z_WORTH[r]}))
            for b in range(4):
                at(0.0 if last else AT["rb"] + 0.5 * b)
                bank = "p%d" % (4 + b)
                mm(bank, T.wq[:, 128 * b:128 * b + 128], T.wsp[:, 128 * b:128 * b + 128], ["wq", "wsp"],
                   T.zq[:, lo:hi], T.zs[:, lo:hi], ["zq" + k for k in p], hi - lo)
                out_of(part("rb", b, p, lo, hi), bank, 2.0 ** -6, hi - lo)
        nq, ns = "xq%d" % (r + 1), "xs%d" % (r + 1)
        for p, (lo, hi) in (HALVES if last else WHOLE).items():
            for b in range(4):
                at(0.0 if last else AT["x"] + AT["dx"] * b)
                out = (T.xt[:, 4 * lo + b:4 * hi:4], ["xt%d%s" % (b, k) for k in p])
                off = (nho[0][:, lo // 16:hi // 16], nho[1])
                if b in P_FAR[r] and p != "a":
                    act(slot("gp", b, C, lo, hi), by(two("rb", b), off), ga(hi - lo))
                    tt((out[0], out[1] + ["p%d" % b]), slot("gp", b, C, lo, hi), (T["p%d" % b][:, lo:hi], []), A.add,
                       el(hi - lo))
                else:
                    tt(out, by(two("rb", b), off), slot("fh", b, C, lo, hi), A.add, ga(hi - lo))
            quant(T[nq][:, lo:hi], T[ns][:, lo:hi], ["xt%d%s" % (b, k) for b in range(4) for k in p], [nq + p * last],
                  T.xt[:, 4 * lo:4 * hi], 4 * (hi - lo))
        if not last:
            send_codes(r + 1)

    at(0.0)
    act(R("nlr"), by(jc, R("fo3")), ga(C), 1.0, float(H))
    store("y", T.nl[:, :], T.nlr[0:128:16, :], ["nlr"])
    for bank, (p, (lo, hi)) in zip(("p4", "p5"), HALVES.items()):
        mm(bank, T.vq[:, :], T.vqs[:, :], ["vq"], T.xq3[:, lo:hi], T.xs3[:, lo:hi], ["xq3" + p], hi - lo)
        out_of(R("yb", lo, hi, "yb" + p), bank, n=hi - lo)
        store("y", T.oc[:, 4 * lo:4 * hi], T.xq3[:, lo:hi].bitcast(dt.uint8), ["xq3" + p], 0.35)
        store("s", T.y[:, lo:hi], T.yb[:, lo:hi], ["yb" + p], 0.4)
    for k in range(4):
        store("y", T.osc[4 * k:4 * k + 4, :], T.xs3[32 * k:32 * k + 4, :], ["xq3a", "xq3b"])
    emit()


def relay_program(g, core, T, topo):
    n = 0
    for r in range(3):
        for i, src in enumerate(T.cores):
            dst = T.cores[i ^ MASKS[r]]
            came = NE if topo.may_write(src, dst) else NEAR
            if route(T, topo, i, r, "c0") == core:
                g.wait_ge(T.sem["ac%d" % r], came)
                n += send(g, T, topo, core, dst, T["lc%d" % r][:, :].bitcast(dt.uint8),
                          T["lc%d" % r][:, :].bitcast(dt.uint8), "ac%d" % r, NE)
            if route(T, topo, i, r, "c1") == core:
                g.wait_ge(T.sem["ac%d" % r], came)
                n += send(g, T, topo, core, dst, T["ls%d" % r][:, :], T["ls%d" % r][:, :], "ac%d" % r, NE)
            for k in "dab":
                if route(T, topo, i, r, k + "0") == core:
                    name, lo, hi = piece(k, r, False)
                    g.wait_ge(T.sem["a%s%d" % (k, r)], NEAR)
                    n += send(g, T, topo, core, dst, T["l" + name][:, lo:hi], T["l" + name][:, lo:hi], "a%s%d" % (k, r), NL)
    if n:
        g.wait_ge(T.sem.sent, n)
